import numpy as np
import ml_dtypes


def mxq(x, axis, fmt="e4m3"):
    dtype, down = {"e4m3": (ml_dtypes.float8_e4m3fn, 7), "e5m2": (ml_dtypes.float8_e5m2, 14)}[fmt]
    v = np.moveaxis(np.asarray(x, np.float32).astype(ml_dtypes.bfloat16).astype(np.float64), axis, -1)
    blocks = v.reshape(v.shape[:-1] + (-1, 32))
    amax = np.abs(blocks).max(-1, keepdims=True)
    byte = np.maximum(np.where(amax > 0, np.frexp(amax)[1] - 1 + 127, 0) - down, 1)
    scale = np.exp2(byte - 127.0)
    codes = (blocks / scale).astype(np.float32).astype(dtype).astype(np.float64)
    return np.moveaxis((codes * scale).reshape(v.shape), -1, axis)


WIDE = False


def mx_kscale(k):
    if not WIDE:
        return np.ones(k)
    levels = np.array([24, -24, 12, -12, 0])
    if k % 512:
        return np.exp2(np.random.permutation(np.resize(levels, k // 32))).repeat(32)
    a = np.empty((k // 512, 16))
    for p in range(k // 512):
        a[p, :8] = np.random.permutation(np.resize(levels, 8))
        for g in range(8):
            far = levels[np.abs(levels - a[p, g]) >= 10]
            a[p, g + 8] = far[np.random.randint(len(far))]
    return np.exp2(a.ravel()).repeat(32)


def f64(x):
    return np.asarray(x).astype(np.float64)


def striped8(idx):
    return np.concatenate([v.reshape(-1, 16).T for v in idx]).astype(np.uint16)


def unstriped8(offs):
    return np.stack([offs[16 * g:16 * g + 16].T.reshape(-1) for g in range(8)]).astype(np.int64)


E2M1 = np.array([0.0, 0.5, 1.0, 1.5, 2.0, 3.0, 4.0, 6.0, -0.0, -0.5, -1.0, -1.5, -2.0, -3.0, -4.0, -6.0])


def pack_weight(w, fmt):
    k, n = w.shape
    w = f64(np.asarray(w, np.float32).astype(ml_dtypes.bfloat16)).reshape(k // 32, 32, n)
    amax = np.abs(w).max(1)
    if fmt == "e4m3":
        byte = np.frexp(amax)[1] - 1 + 127 - 7
    else:
        mant, ex = np.frexp(amax / 6.0)
        byte = np.where(mant > 0.5, ex, ex - 1) + 127
    byte = np.clip(np.where(amax > 0, byte, 1), 1, 254)
    scaled = (w * np.exp2(127.0 - byte)[:, None, :]).reshape(k, n).astype(np.float32)
    by_word = np.ascontiguousarray(scaled.reshape(k // 512, 128, 4, n).transpose(0, 1, 3, 2))
    if fmt == "e4m3":
        words = by_word.astype(ml_dtypes.float8_e4m3fn).view(np.uint8)
    else:
        c = by_word.astype(ml_dtypes.float4_e2m1fn).view(np.uint8) & 0xF
        words = (c[..., 0::2] | (c[..., 1::2] << 4)).reshape(k // 512, 128, 2 * n)
    return np.ascontiguousarray(words), np.ascontiguousarray(byte.astype(np.uint8).reshape(k // 512, 16, n))


def unpack_weight(words, scales, fmt):
    g, _, n = scales.shape
    words = np.ascontiguousarray(words).reshape(g, 128, n, -1)
    if fmt == "e4m3":
        vals = words.view(ml_dtypes.float8_e4m3fn).astype(np.float64)
    else:
        nib = np.empty((g, 128, n, 4), np.uint8)
        nib[..., 0::2] = words & 0xF
        nib[..., 1::2] = words >> 4
        vals = E2M1[nib]
    vals = vals * np.repeat(np.exp2(scales.astype(np.float64) - 127.0), 8, axis=1)[..., None]
    return vals.transpose(0, 1, 3, 2).reshape(g * 512, n)


K, N, T, J = 512, 512, 2048, 512


def setup_inputs():
    n = np.random.standard_normal
    s = mx_kscale(K)[:, None]
    p_w4 = pack_weight(n((K, N)) / np.sqrt(K) / s, "e2m1")
    return {
        "xT": (n((K, T)) * s).astype(np.float32),
        "wgt": np.repeat(np.random.uniform(0.5, 2.0, (8, 3 * J)), 16, axis=0).astype(np.float32),
        "w4_words": p_w4[0],
        "w4_scales": p_w4[1],
        "wd": (0.4 * (n((K, N)) / np.sqrt(K) / s)).astype(np.float32),
        "res": (n((N, J))).astype(np.float32),
        "offs": striped8(np.stack([np.concatenate([np.random.permutation(T)[:J] for _ in range(3)]) for _ in range(8)])),
    }


def reference(xT, wgt, w4_words, w4_scales, wd, res, offs):
    idx = unstriped8(offs)
    rows = np.arange(K)
    xg = f64(wgt)[rows // 4 % 128] * f64(xT)[rows[:, None], idx[rows % 512 // 64]]
    xT_ = mxq(xg, 0, "e4m3").reshape(K, 3, J)
    w4_ = unpack_weight(w4_words, w4_scales, "e2m1")
    wd_ = mxq(f64(wd), 0, "e4m3")
    a0 = w4_.T @ xT_[:, 0] + wd_.T @ xT_[:, 0]
    a1 = w4_.T @ xT_[:, 1] + wd_.T @ xT_[:, 1]
    a2 = w4_.T @ xT_[:, 2] + wd_.T @ xT_[:, 2]
    return f64(res) + a0 * a1 * a2

@@ -1,0 +1,181 @@
+from contextlib import ExitStack
+
+import concourse.mybir as mybir
+
+K, N, T, J, PICKS = 512, 512, 2048, 512, 3
+FLOPS = 2 * 2 * K * N * J * PICKS
+
+F32 = mybir.dt.float32
+BF16 = mybir.dt.bfloat16
+I32 = mybir.dt.int32
+U32 = mybir.dt.uint32
+U16 = mybir.dt.uint16
+U8 = mybir.dt.uint8
+FP8X4 = mybir.dt.float8_e4m3fn_x4
+FP4X4 = mybir.dt.float4_e2m1fn_x4
+MULT = mybir.AluOpType.mult
+ADD = mybir.AluOpType.add
+
+P = 128
+PACK = 4
+GROUP = 16
+HALF = 256
+CHUNK = 128
+N_TILES = N // P
+RUN = 4
+
+
+def tile_list_dl_prod_res_kernel(tc, xT, wgt, w4_words, w4_scales, wd, res, offs, out):
+    nc = tc.nc
+    with ExitStack() as ctx:
+        keep = ctx.enter_context(tc.tile_pool(name="keep", bufs=1))
+        psum = ctx.enter_context(tc.psum_pool(name="psum", bufs=8))
+
+        offsets = keep.tile([P, PICKS * J // GROUP], U16, name="offsets")
+        planes = [keep.tile([P, T], F32, name="plane%d" % t) for t in range(PACK)]
+        weights = [keep.tile([P, PICKS, HALF], F32, name="weights%d" % h) for h in range(2)]
+        w4_codes = keep.tile([P, 2 * N], U8, name="w4_codes", align_bytes=64)
+        w4_plane = keep.tile([P, N], U8, name="w4_plane", align_bytes=64)
+        wd_raw = [keep.tile([P, PACK, HALF], F32, name="wd_raw%d" % h) for h in range(2)]
+        wd_codes = keep.tile([P, N], U32, name="wd_codes", align_bytes=64)
+        wd_plane = keep.tile([P, N], U8, name="wd_plane", align_bytes=64)
+        residual = keep.tile([P, N_TILES, J], F32, name="residual")
+
+        x_rows = xT.rearrange("(p t) w -> t p w", t=PACK)
+        wd_rows = wd.rearrange("(p t) n -> p t n", t=PACK)
+        wgt_rows = wgt.rearrange("p (c h m) -> h p c m", c=PICKS, h=2)
+        out_rows = out.rearrange("(a p) j -> p a j", p=P)
+
+        nc.vector.memset(w4_plane[:].bitcast(U32), 0)
+        nc.sync.dma_start(offsets[:], offs)
+        nc.sync.dma_start(out=weights[0][:, 0, :], in_=wgt_rows[0][:, 0, :])
+        nc.sync.dma_start(out=planes[0][:], in_=x_rows[0])
+        nc.sync.dma_start(out=weights[0][:, 1:PICKS, :], in_=wgt_rows[0][:, 1:PICKS, :])
+        nc.sync.dma_start(out=weights[1][:], in_=wgt_rows[1])
+        nc.sync.dma_start(out=planes[1][:], in_=x_rows[1])
+        nc.sync.dma_start(out=wd_raw[0][:], in_=wd_rows[:, :, 0:HALF])
+        nc.sync.dma_start(out=planes[2][:], in_=x_rows[2])
+        nc.sync.dma_start(out=wd_raw[1][:], in_=wd_rows[:, :, HALF:N])
+        nc.sync.dma_start(out=planes[3][:], in_=x_rows[3])
+        for q in range(4):
+            nc.sync.dma_start(
+                out=w4_plane[32 * q : 32 * q + 4, :].bitcast(I32),
+                in_=w4_scales[0, 4 * q : 4 * q + 4, :].bitcast(I32),
+            )
+        nc.sync.dma_start(out=w4_codes[:].bitcast(I32), in_=w4_words[0].bitcast(I32))
+        nc.sync.dma_start(out=residual[:], in_=res.rearrange("(a p) j -> p a j", p=P))
+
+        units = [(h, c) for h in range(2) for c in range(PICKS)]
+        picked = {u: keep.tile([P, PACK, HALF], F32, name="picked%d%d" % u) for u in units}
+        rounded = {u: keep.tile([P, HALF * PACK], BF16, name="rounded%d%d" % u, align_bytes=64) for u in units}
+        x_codes = {u: keep.tile([P, HALF], U32, name="x_codes%d%d" % u, align_bytes=64) for u in units}
+        x_plane = {u: keep.tile([P, HALF], U8, name="x_plane%d%d" % u, align_bytes=64) for u in units}
+        wd_rounded = [keep.tile([P, HALF * PACK], BF16, name="wd_rounded%d" % h, align_bytes=64) for h in range(2)]
+        chunks = range(J // CHUNK)
+        first = [keep.tile([P, N_TILES, CHUNK], F32, name="first%d" % k) for k in chunks]
+        pair = [keep.tile([P, N_TILES, CHUNK], F32, name="pair%d" % k) for k in chunks]
+        triple = [keep.tile([P, N_TILES, CHUNK], F32, name="triple%d" % k) for k in chunks]
+        result = [keep.tile([P, N_TILES, CHUNK], F32, name="result%d" % k) for k in chunks]
+        sums = {}
+
+        def gather(t, u):
+            m0 = u[1] * J + u[0] * HALF
+            window = planes[t][:].indirect(offsets[:, m0 // GROUP : (m0 + HALF) // GROUP])
+            nc.vector.tensor_tensor(picked[u][:, t, :], window, weights[u[0]][:, u[1], :], MULT)
+
+        def interleave(dst, src):
+            nc.scalar.copy(
+                out=dst.rearrange("p (c i t) -> p c t i", i=RUN, t=PACK),
+                in_=src.rearrange("p t (c i) -> p c t i", i=RUN),
+            )
+
+        def quantize_x(u):
+            nc.vector.quantize_mx(out=x_codes[u][:].bitcast(FP8X4), scales=x_plane[u][:], in_=rounded[u][:])
+
+        def quantize_wd(h):
+            cols = slice(h * HALF, (h + 1) * HALF)
+            nc.vector.quantize_mx(out=wd_codes[:, cols].bitcast(FP8X4), scales=wd_plane[:, cols], in_=wd_rounded[h][:])
+
+        def project(k, c):
+            u = (k // 2, c)
+            cols = slice((k % 2) * CHUNK, (k % 2 + 1) * CHUNK)
+            acc = psum.tile([P, N_TILES, CHUNK], F32, name="acc")
+            sums[k, c] = acc
+            for a in range(N_TILES):
+                nc.tensor.matmul_mx(
+                    out=acc[:, a, :],
+                    lhsT=w4_codes[:, 2 * P * a : 2 * P * (a + 1)].bitcast(FP4X4),
+                    lhsT_scale=w4_plane[:, P * a : P * (a + 1)],
+                    rhs=x_codes[u][:, cols].bitcast(FP8X4),
+                    rhs_scale=x_plane[u][:, cols],
+                    start=True,
+                    stop=False,
+                )
+                nc.tensor.matmul_mx(
+                    out=acc[:, a, :],
+                    lhsT=wd_codes[:, P * a : P * (a + 1)].bitcast(FP8X4),
+                    lhsT_scale=wd_plane[:, P * a : P * (a + 1)],
+                    rhs=x_codes[u][:, cols].bitcast(FP8X4),
+                    rhs_scale=x_plane[u][:, cols],
+                    start=False,
+                    stop=True,
+                )
+
+        def project_unit(u):
+            for k in (2 * u[0], 2 * u[0] + 1):
+                project(k, u[1])
+
+        def copy_first(k):
+            nc.scalar.copy(out=first[k][:], in_=sums[k, 0][:])
+
+        def times_second(k):
+            nc.vector.tensor_tensor(pair[k][:], sums[k, 1][:], first[k][:], MULT)
+
+        def times_third(k):
+            nc.vector.tensor_tensor(triple[k][:], sums[k, 2][:], pair[k][:], MULT)
+
+        def finish(k):
+            cols = slice(k * CHUNK, (k + 1) * CHUNK)
+            nc.vector.tensor_tensor(result[k][:], triple[k][:], residual[:, :, cols], ADD)
+            nc.sync.dma_start(out=out_rows[:, :, cols], in_=result[k][:])
+
+        def prepare(u):
+            for t in range(PACK):
+                gather(t, u)
+            interleave(rounded[u][:], picked[u][:])
+
+        def multiply(u):
+            quantize_x(u)
+            project_unit(u)
+
+        for h in range(2):
+            interleave(wd_rounded[h][:], wd_raw[h][:])
+            quantize_wd(h)
+        prepare(units[0])
+        prepare(units[1])
+        multiply(units[0])
+        prepare(units[2])
+        multiply(units[1])
+        prepare(units[3])
+        multiply(units[2])
+        copy_first(0)
+        copy_first(1)
+        prepare(units[4])
+        multiply(units[3])
+        prepare(units[5])
+        multiply(units[4])
+        copy_first(2)
+        copy_first(3)
+        times_second(0)
+        times_second(1)
+        multiply(units[5])
+        times_third(0)
+        times_third(1)
+        finish(0)
+        finish(1)
+        times_second(2)
+        times_second(3)
+        times_third(2)
+        times_third(3)
+        finish(2)
+        finish(3)

@@ -47,9 +47,9 @@ def tile_list_dl_prod_res_kernel(tc, xT, wgt, w4_words, w4_scales, wd, res, offs
         out_rows = out.rearrange("(a p) j -> p a j", p=P)
 
         nc.vector.memset(w4_plane[:].bitcast(U32), 0)
-        nc.sync.dma_start(offsets[:], offs)
-        nc.sync.dma_start(out=weights[0][:, 0, :], in_=wgt_rows[0][:, 0, :])
         nc.sync.dma_start(out=planes[0][:], in_=x_rows[0])
+        nc.sync.dma_start(offsets[:], offs)
+        nc.scalar.dma_start(out=weights[0][:, 0, :], in_=wgt_rows[0][:, 0, :])
         nc.sync.dma_start(out=weights[0][:, 1:PICKS, :], in_=wgt_rows[0][:, 1:PICKS, :])
         nc.sync.dma_start(out=weights[1][:], in_=wgt_rows[1])
         nc.sync.dma_start(out=planes[1][:], in_=x_rows[1])
@@ -66,7 +66,8 @@ def tile_list_dl_prod_res_kernel(tc, xT, wgt, w4_words, w4_scales, wd, res, offs
         nc.sync.dma_start(out=residual[:], in_=res.rearrange("(a p) j -> p a j", p=P))
 
         units = [(h, c) for h in range(2) for c in range(PICKS)]
-        picked = {u: keep.tile([P, PACK, HALF], F32, name="picked%d%d" % u) for u in units}
+        slots = [keep.tile([P, 7, HALF], F32, name="slots%d" % c) for c in range(PICKS)]
+        picked = {(h, c): slots[c][:, 0:7:2, :] if h else slots[c][:, 3:7, :] for h, c in units}
         rounded = {u: keep.tile([P, HALF * PACK], BF16, name="rounded%d%d" % u, align_bytes=64) for u in units}
         x_codes = {u: keep.tile([P, HALF], U32, name="x_codes%d%d" % u, align_bytes=64) for u in units}
         x_plane = {u: keep.tile([P, HALF], U8, name="x_plane%d%d" % u, align_bytes=64) for u in units}
@@ -134,15 +135,15 @@ def tile_list_dl_prod_res_kernel(tc, xT, wgt, w4_words, w4_scales, wd, res, offs
         def times_third(k):
             nc.vector.tensor_tensor(triple[k][:], sums[k, 2][:], pair[k][:], MULT)
 
-        def finish(k):
+        def finish(k, rows=slice(0, N_TILES)):
             cols = slice(k * CHUNK, (k + 1) * CHUNK)
-            nc.vector.tensor_tensor(result[k][:], triple[k][:], residual[:, :, cols], ADD)
-            nc.sync.dma_start(out=out_rows[:, :, cols], in_=result[k][:])
+            nc.vector.tensor_tensor(result[k][:, rows, :], triple[k][:, rows, :], residual[:, rows, cols], ADD)
+            nc.sync.dma_start(out=out_rows[:, rows, cols], in_=result[k][:, rows, :])
 
         def prepare(u):
-            for t in range(PACK):
-                gather(t, u)
-            interleave(rounded[u][:], picked[u][:])
+            gather(2, u)
+            gather(3, u)
+            interleave(rounded[u][:], picked[u])
 
         def multiply(u):
             quantize_x(u)
@@ -151,24 +152,27 @@ def tile_list_dl_prod_res_kernel(tc, xT, wgt, w4_words, w4_scales, wd, res, offs
         for h in range(2):
             interleave(wd_rounded[h][:], wd_raw[h][:])
             quantize_wd(h)
+        for t in range(2):
+            for u in units:
+                gather(t, u)
         prepare(units[0])
         prepare(units[1])
-        multiply(units[0])
         prepare(units[2])
-        multiply(units[1])
+        multiply(units[0])
         prepare(units[3])
-        multiply(units[2])
+        multiply(units[1])
+        prepare(units[4])
         copy_first(0)
         copy_first(1)
-        prepare(units[4])
-        multiply(units[3])
+        multiply(units[2])
         prepare(units[5])
+        multiply(units[3])
         multiply(units[4])
+        multiply(units[5])
         copy_first(2)
         copy_first(3)
         times_second(0)
         times_second(1)
-        multiply(units[5])
         times_third(0)
         times_third(1)
         finish(0)
@@ -178,4 +182,5 @@ def tile_list_dl_prod_res_kernel(tc, xT, wgt, w4_words, w4_scales, wd, res, offs
         times_third(2)
         times_third(3)
         finish(2)
-        finish(3)
+        finish(3, slice(0, 2))
+        finish(3, slice(2, 4))

@@ -33,7 +33,7 @@ def tile_list_dl_prod_res_kernel(tc, xT, wgt, w4_words, w4_scales, wd, res, offs
 
         offsets = keep.tile([P, PICKS * J // GROUP], U16, name="offsets")
         planes = [keep.tile([P, T], F32, name="plane%d" % t) for t in range(PACK)]
-        weights = [keep.tile([P, PICKS, HALF], F32, name="weights%d" % h) for h in range(2)]
+        weights = keep.tile([P, PICKS * J], F32, name="weights")
         w4_codes = keep.tile([P, 2 * N], U8, name="w4_codes", align_bytes=64)
         w4_plane = keep.tile([P, N], U8, name="w4_plane", align_bytes=64)
         wd_raw = [keep.tile([P, PACK, HALF], F32, name="wd_raw%d" % h) for h in range(2)]
@@ -43,20 +43,19 @@ def tile_list_dl_prod_res_kernel(tc, xT, wgt, w4_words, w4_scales, wd, res, offs
 
         x_rows = xT.rearrange("(p t) w -> t p w", t=PACK)
         wd_rows = wd.rearrange("(p t) n -> p t n", t=PACK)
-        wgt_rows = wgt.rearrange("p (c h m) -> h p c m", c=PICKS, h=2)
         out_rows = out.rearrange("(a p) j -> p a j", p=P)
 
         nc.vector.memset(w4_plane[:].bitcast(U32), 0)
         nc.sync.dma_start(out=planes[0][:], in_=x_rows[0])
         nc.sync.dma_start(offsets[:], offs)
-        nc.scalar.dma_start(out=weights[0][:, 0, :], in_=wgt_rows[0][:, 0, :])
-        nc.sync.dma_start(out=weights[0][:, 1:PICKS, :], in_=wgt_rows[0][:, 1:PICKS, :])
-        nc.sync.dma_start(out=weights[1][:], in_=wgt_rows[1])
+        nc.scalar.dma_start(out=weights[:, 0:256], in_=wgt[:, 0:256])
+        nc.sync.dma_start(out=weights[:, 256:768], in_=wgt[:, 256:768])
+        nc.sync.dma_start(out=weights[:, 768:1536], in_=wgt[:, 768:1536])
         nc.sync.dma_start(out=planes[1][:], in_=x_rows[1])
         nc.sync.dma_start(out=wd_raw[0][:], in_=wd_rows[:, :, 0:HALF])
         nc.sync.dma_start(out=planes[2][:], in_=x_rows[2])
-        nc.sync.dma_start(out=wd_raw[1][:], in_=wd_rows[:, :, HALF:N])
         nc.sync.dma_start(out=planes[3][:], in_=x_rows[3])
+        nc.sync.dma_start(out=wd_raw[1][:], in_=wd_rows[:, :, HALF:N])
         for q in range(4):
             nc.sync.dma_start(
                 out=w4_plane[32 * q : 32 * q + 4, :].bitcast(I32),
@@ -68,7 +67,8 @@ def tile_list_dl_prod_res_kernel(tc, xT, wgt, w4_words, w4_scales, wd, res, offs
         units = [(h, c) for h in range(2) for c in range(PICKS)]
         slots = [keep.tile([P, 7, HALF], F32, name="slots%d" % c) for c in range(PICKS)]
         picked = {(h, c): slots[c][:, 0:7:2, :] if h else slots[c][:, 3:7, :] for h, c in units}
-        rounded = {u: keep.tile([P, HALF * PACK], BF16, name="rounded%d%d" % u, align_bytes=64) for u in units}
+        rounded = {u: keep.tile([P, HALF * PACK], BF16, name="rounded%d%d" % u, align_bytes=64) for u in units[:-1]}
+        rounded[units[-1]] = keep.tile([P, HALF * PACK], BF16, name="rounded_last", tag="reused", align_bytes=64)
         x_codes = {u: keep.tile([P, HALF], U32, name="x_codes%d%d" % u, align_bytes=64) for u in units}
         x_plane = {u: keep.tile([P, HALF], U8, name="x_plane%d%d" % u, align_bytes=64) for u in units}
         wd_rounded = [keep.tile([P, HALF * PACK], BF16, name="wd_rounded%d" % h, align_bytes=64) for h in range(2)]
@@ -76,13 +76,13 @@ def tile_list_dl_prod_res_kernel(tc, xT, wgt, w4_words, w4_scales, wd, res, offs
         first = [keep.tile([P, N_TILES, CHUNK], F32, name="first%d" % k) for k in chunks]
         pair = [keep.tile([P, N_TILES, CHUNK], F32, name="pair%d" % k) for k in chunks]
         triple = [keep.tile([P, N_TILES, CHUNK], F32, name="triple%d" % k) for k in chunks]
-        result = [keep.tile([P, N_TILES, CHUNK], F32, name="result%d" % k) for k in chunks]
+        result = {k: keep.tile([P, N_TILES, CHUNK], F32, name="result%d" % k) for k in (2, 3)}
         sums = {}
 
         def gather(t, u):
             m0 = u[1] * J + u[0] * HALF
             window = planes[t][:].indirect(offsets[:, m0 // GROUP : (m0 + HALF) // GROUP])
-            nc.vector.tensor_tensor(picked[u][:, t, :], window, weights[u[0]][:, u[1], :], MULT)
+            nc.vector.tensor_tensor(picked[u][:, t, :], window, weights[:, m0 : m0 + HALF], MULT)
 
         def interleave(dst, src):
             nc.scalar.copy(
@@ -90,8 +90,9 @@ def tile_list_dl_prod_res_kernel(tc, xT, wgt, w4_words, w4_scales, wd, res, offs
                 in_=src.rearrange("p t (c i) -> p c t i", i=RUN),
             )
 
-        def quantize_x(u):
-            nc.vector.quantize_mx(out=x_codes[u][:].bitcast(FP8X4), scales=x_plane[u][:], in_=rounded[u][:])
+        def quantize_x(u, cols=slice(0, HALF)):
+            values = rounded[u][:, PACK * cols.start : PACK * cols.stop]
+            nc.vector.quantize_mx(out=x_codes[u][:, cols].bitcast(FP8X4), scales=x_plane[u][:, cols], in_=values)
 
         def quantize_wd(h):
             cols = slice(h * HALF, (h + 1) * HALF)
@@ -135,9 +136,9 @@ def tile_list_dl_prod_res_kernel(tc, xT, wgt, w4_words, w4_scales, wd, res, offs
         def times_third(k):
             nc.vector.tensor_tensor(triple[k][:], sums[k, 2][:], pair[k][:], MULT)
 
-        def finish(k, rows=slice(0, N_TILES)):
+        def finish(engine, k, rows=slice(0, N_TILES)):
             cols = slice(k * CHUNK, (k + 1) * CHUNK)
-            nc.vector.tensor_tensor(result[k][:, rows, :], triple[k][:, rows, :], residual[:, rows, cols], ADD)
+            engine.tensor_tensor(result[k][:, rows, :], triple[k][:, rows, :], residual[:, rows, cols], ADD)
             nc.sync.dma_start(out=out_rows[:, rows, cols], in_=result[k][:, rows, :])
 
         def prepare(u):
@@ -149,38 +150,51 @@ def tile_list_dl_prod_res_kernel(tc, xT, wgt, w4_words, w4_scales, wd, res, offs
             quantize_x(u)
             project_unit(u)
 
-        for h in range(2):
-            interleave(wd_rounded[h][:], wd_raw[h][:])
-            quantize_wd(h)
-        for t in range(2):
-            for u in units:
-                gather(t, u)
+        interleave(wd_rounded[0][:], wd_raw[0][:])
+        quantize_wd(0)
+        for c in range(PICKS):
+            for h in range(2):
+                gather(0, (h, c))
+        for u in units:
+            gather(1, u)
         prepare(units[0])
+        interleave(wd_rounded[1][:], wd_raw[1][:])
         prepare(units[1])
         prepare(units[2])
-        multiply(units[0])
+        quantize_x(units[0])
+        quantize_wd(1)
+        project_unit(units[0])
         prepare(units[3])
         multiply(units[1])
         prepare(units[4])
         copy_first(0)
         copy_first(1)
         multiply(units[2])
-        prepare(units[5])
+        last = units[5]
+        last_cols = [slice(0, CHUNK), slice(CHUNK, HALF)]
+        gather(2, last)
+        gather(3, last)
+        for cols in last_cols:
+            interleave(rounded[last][:, PACK * cols.start : PACK * cols.stop], picked[last][:, :, cols])
         multiply(units[3])
         multiply(units[4])
-        multiply(units[5])
+        for i, cols in enumerate(last_cols):
+            quantize_x(last, cols)
+            project(2 + i, last[1])
         copy_first(2)
         copy_first(3)
         times_second(0)
         times_second(1)
         times_third(0)
         times_third(1)
-        finish(0)
-        finish(1)
+        early = keep.tile([P, 2, N_TILES, CHUNK], F32, name="early", tag="reused", align_bytes=64)
+        result[0], result[1] = early[:, 0], early[:, 1]
+        finish(nc.gpsimd, 0)
+        finish(nc.gpsimd, 1)
         times_second(2)
         times_second(3)
         times_third(2)
         times_third(3)
-        finish(2)
-        finish(3, slice(0, 2))
-        finish(3, slice(2, 4))
+        finish(nc.vector, 2)
+        finish(nc.vector, 3, slice(0, 2))
+        finish(nc.vector, 3, slice(2, 4))

@@ -54,8 +54,8 @@ def tile_list_dl_prod_res_kernel(tc, xT, wgt, w4_words, w4_scales, wd, res, offs
         nc.sync.dma_start(out=planes[1][:], in_=x_rows[1])
         nc.sync.dma_start(out=wd_raw[0][:], in_=wd_rows[:, :, 0:HALF])
         nc.sync.dma_start(out=planes[2][:], in_=x_rows[2])
-        nc.sync.dma_start(out=planes[3][:], in_=x_rows[3])
         nc.sync.dma_start(out=wd_raw[1][:], in_=wd_rows[:, :, HALF:N])
+        nc.sync.dma_start(out=planes[3][:], in_=x_rows[3])
         for q in range(4):
             nc.sync.dma_start(
                 out=w4_plane[32 * q : 32 * q + 4, :].bitcast(I32),
@@ -65,29 +65,50 @@ def tile_list_dl_prod_res_kernel(tc, xT, wgt, w4_words, w4_scales, wd, res, offs
         nc.sync.dma_start(out=residual[:], in_=res.rearrange("(a p) j -> p a j", p=P))
 
         units = [(h, c) for h in range(2) for c in range(PICKS)]
-        slots = [keep.tile([P, 7, HALF], F32, name="slots%d" % c) for c in range(PICKS)]
-        picked = {(h, c): slots[c][:, 0:7:2, :] if h else slots[c][:, 3:7, :] for h, c in units}
+        low0 = keep.tile([P, 2, J], F32, name="low0")
+        slots1 = keep.tile([P, PACK, HALF], F32, name="slots1")
+        slots2 = keep.tile([P, PACK, HALF], F32, name="slots2")
+        high0 = keep.tile([P, 3, HALF], F32, name="high0")
+        whole = {(0, 1): slots1[:], (0, 2): slots2[:]}
+        low = {(0, 0): low0[:, :, 0:HALF], (1, 0): low0[:, :, HALF:J]}
+        high = {(0, 0): high0[:, 1:3, :], (1, 0): high0[:, 0:3:2, :]}
+        for c in (1, 2):
+            low[0, c] = whole[0, c][:, 0:2, :]
+            low[1, c] = keep.tile([P, 2, HALF], F32, name="low%d" % c)[:]
+            high[0, c] = high[1, c] = whole[0, c][:, 2:4, :]
         rounded = {u: keep.tile([P, HALF * PACK], BF16, name="rounded%d%d" % u, align_bytes=64) for u in units[:-1]}
         rounded[units[-1]] = keep.tile([P, HALF * PACK], BF16, name="rounded_last", tag="reused", align_bytes=64)
         x_codes = {u: keep.tile([P, HALF], U32, name="x_codes%d%d" % u, align_bytes=64) for u in units}
         x_plane = {u: keep.tile([P, HALF], U8, name="x_plane%d%d" % u, align_bytes=64) for u in units}
         wd_rounded = [keep.tile([P, HALF * PACK], BF16, name="wd_rounded%d" % h, align_bytes=64) for h in range(2)]
-        chunks = range(J // CHUNK)
-        first = [keep.tile([P, N_TILES, CHUNK], F32, name="first%d" % k) for k in chunks]
-        pair = [keep.tile([P, N_TILES, CHUNK], F32, name="pair%d" % k) for k in chunks]
-        triple = [keep.tile([P, N_TILES, CHUNK], F32, name="triple%d" % k) for k in chunks]
-        result = {k: keep.tile([P, N_TILES, CHUNK], F32, name="result%d" % k) for k in (2, 3)}
+        blocks = [(h, r) for h in range(2) for r in range(2)]
+        first = {b: keep.tile([P, 2, HALF], F32, name="first%d%d" % b) for b in blocks}
+        pair = {b: keep.tile([P, 2, HALF], F32, name="pair%d%d" % b) for b in blocks}
+        triple = {b: keep.tile([P, 2, HALF], F32, name="triple%d%d" % b) for b in blocks}
+        result = {b: keep.tile([P, 2, HALF], F32, name="result%d%d" % b) for b in blocks[2:]}
         sums = {}
 
-        def gather(t, u):
-            m0 = u[1] * J + u[0] * HALF
-            window = planes[t][:].indirect(offsets[:, m0 // GROUP : (m0 + HALF) // GROUP])
-            nc.vector.tensor_tensor(picked[u][:, t, :], window, weights[:, m0 : m0 + HALF], MULT)
+        def gather(dst, t, c, places):
+            m0, m1 = c * J + places.start, c * J + places.stop
+            window = planes[t][:].indirect(offsets[:, m0 // GROUP : m1 // GROUP])
+            nc.vector.tensor_tensor(dst, window, weights[:, m0:m1], MULT)
+
+        def half(h):
+            return slice(h * HALF, (h + 1) * HALF)
+
+        def gather_unit(t, u):
+            gather((low, high)[t // 2][u][:, t % 2, :], t, u[1], half(u[0]))
 
         def interleave(dst, src):
             nc.scalar.copy(
                 out=dst.rearrange("p (c i t) -> p c t i", i=RUN, t=PACK),
                 in_=src.rearrange("p t (c i) -> p c t i", i=RUN),
+            )
+
+        def interleave_pair(u, e, cols=slice(0, HALF)):
+            nc.scalar.copy(
+                out=rounded[u][:].rearrange("p (j t) -> p j t", t=PACK)[:, cols, 2 * e : 2 * e + 2],
+                in_=(low, high)[e][u][:, :, cols].rearrange("p t j -> p j t"),
             )
 
         def quantize_x(u, cols=slice(0, HALF)):
@@ -98,103 +119,102 @@ def tile_list_dl_prod_res_kernel(tc, xT, wgt, w4_words, w4_scales, wd, res, offs
             cols = slice(h * HALF, (h + 1) * HALF)
             nc.vector.quantize_mx(out=wd_codes[:, cols].bitcast(FP8X4), scales=wd_plane[:, cols], in_=wd_rounded[h][:])
 
-        def project(k, c):
-            u = (k // 2, c)
-            cols = slice((k % 2) * CHUNK, (k % 2 + 1) * CHUNK)
-            acc = psum.tile([P, N_TILES, CHUNK], F32, name="acc")
-            sums[k, c] = acc
-            for a in range(N_TILES):
+        def project(u, r):
+            acc = psum.tile([P, 2, HALF], F32, name="acc")
+            sums[u, r] = acc
+            for i in range(2):
+                a = 2 * r + i
                 nc.tensor.matmul_mx(
-                    out=acc[:, a, :],
-                    lhsT=w4_codes[:, 2 * P * a : 2 * P * (a + 1)].bitcast(FP4X4),
-                    lhsT_scale=w4_plane[:, P * a : P * (a + 1)],
-                    rhs=x_codes[u][:, cols].bitcast(FP8X4),
-                    rhs_scale=x_plane[u][:, cols],
+                    out=acc[:, i, :],
+                    lhsT=wd_codes[:, P * a : P * (a + 1)].bitcast(FP8X4),
+                    lhsT_scale=wd_plane[:, P * a : P * (a + 1)],
+                    rhs=x_codes[u][:].bitcast(FP8X4),
+                    rhs_scale=x_plane[u][:],
                     start=True,
                     stop=False,
                 )
-                nc.tensor.matmul_mx(
-                    out=acc[:, a, :],
-                    lhsT=wd_codes[:, P * a : P * (a + 1)].bitcast(FP8X4),
-                    lhsT_scale=wd_plane[:, P * a : P * (a + 1)],
-                    rhs=x_codes[u][:, cols].bitcast(FP8X4),
-                    rhs_scale=x_plane[u][:, cols],
-                    start=False,
-                    stop=True,
-                )
+                for k in range(2):
+                    cols = slice(k * CHUNK, (k + 1) * CHUNK)
+                    nc.tensor.matmul_mx(
+                        out=acc[:, i, cols],
+                        lhsT=w4_codes[:, 2 * P * a : 2 * P * (a + 1)].bitcast(FP4X4),
+                        lhsT_scale=w4_plane[:, P * a : P * (a + 1)],
+                        rhs=x_codes[u][:, cols].bitcast(FP8X4),
+                        rhs_scale=x_plane[u][:, cols],
+                        start=False,
+                        stop=(k == 1),
+                    )
 
-        def project_unit(u):
-            for k in (2 * u[0], 2 * u[0] + 1):
-                project(k, u[1])
+        def copy_first(b):
+            nc.scalar.copy(out=first[b][:], in_=sums[(b[0], 0), b[1]][:])
 
-        def copy_first(k):
-            nc.scalar.copy(out=first[k][:], in_=sums[k, 0][:])
+        def times_second(b):
+            nc.vector.tensor_tensor(pair[b][:], sums[(b[0], 1), b[1]][:], first[b][:], MULT)
 
-        def times_second(k):
-            nc.vector.tensor_tensor(pair[k][:], sums[k, 1][:], first[k][:], MULT)
+        def times_third(b):
+            nc.vector.tensor_tensor(triple[b][:], sums[(b[0], 2), b[1]][:], pair[b][:], MULT)
 
-        def times_third(k):
-            nc.vector.tensor_tensor(triple[k][:], sums[k, 2][:], pair[k][:], MULT)
-
-        def finish(engine, k, rows=slice(0, N_TILES)):
-            cols = slice(k * CHUNK, (k + 1) * CHUNK)
-            engine.tensor_tensor(result[k][:, rows, :], triple[k][:, rows, :], residual[:, rows, cols], ADD)
-            nc.sync.dma_start(out=out_rows[:, rows, cols], in_=result[k][:, rows, :])
+        def finish(engine, b, tiles=slice(0, 2)):
+            h, r = b
+            rows = slice(2 * r + tiles.start, 2 * r + tiles.stop)
+            engine.tensor_tensor(result[b][:, tiles, :], triple[b][:, tiles, :], residual[:, rows, half(h)], ADD)
+            nc.sync.dma_start(out=out_rows[:, rows, half(h)], in_=result[b][:, tiles, :])
 
         def prepare(u):
-            gather(2, u)
-            gather(3, u)
-            interleave(rounded[u][:], picked[u])
+            gather_unit(2, u)
+            gather_unit(3, u)
+            if u in whole:
+                interleave(rounded[u][:], whole[u])
+            else:
+                interleave_pair(u, 1)
 
         def multiply(u):
             quantize_x(u)
-            project_unit(u)
+            project(u, 0)
+            project(u, 1)
 
-        interleave(wd_rounded[0][:], wd_raw[0][:])
-        quantize_wd(0)
+        for h in range(2):
+            interleave(wd_rounded[h][:], wd_raw[h][:])
+            quantize_wd(h)
         for c in range(PICKS):
             for h in range(2):
-                gather(0, (h, c))
+                gather_unit(0, (h, c))
+        gather_unit(1, (0, 1))
+        gather_unit(1, (0, 2))
+        gather(low0[:, 1, :], 1, 0, slice(0, J))
+        gather_unit(1, (1, 1))
+        gather_unit(1, (1, 2))
         for u in units:
-            gather(1, u)
+            if u not in whole:
+                interleave_pair(u, 0)
         prepare(units[0])
-        interleave(wd_rounded[1][:], wd_raw[1][:])
         prepare(units[1])
         prepare(units[2])
-        quantize_x(units[0])
-        quantize_wd(1)
-        project_unit(units[0])
+        multiply(units[0])
         prepare(units[3])
         multiply(units[1])
         prepare(units[4])
-        copy_first(0)
-        copy_first(1)
+        copy_first(blocks[0])
+        copy_first(blocks[1])
         multiply(units[2])
-        last = units[5]
-        last_cols = [slice(0, CHUNK), slice(CHUNK, HALF)]
-        gather(2, last)
-        gather(3, last)
-        for cols in last_cols:
-            interleave(rounded[last][:, PACK * cols.start : PACK * cols.stop], picked[last][:, :, cols])
+        prepare(units[5])
         multiply(units[3])
         multiply(units[4])
-        for i, cols in enumerate(last_cols):
-            quantize_x(last, cols)
-            project(2 + i, last[1])
-        copy_first(2)
-        copy_first(3)
-        times_second(0)
-        times_second(1)
-        times_third(0)
-        times_third(1)
-        early = keep.tile([P, 2, N_TILES, CHUNK], F32, name="early", tag="reused", align_bytes=64)
-        result[0], result[1] = early[:, 0], early[:, 1]
-        finish(nc.gpsimd, 0)
-        finish(nc.gpsimd, 1)
-        times_second(2)
-        times_second(3)
-        times_third(2)
-        times_third(3)
-        finish(nc.vector, 2)
-        finish(nc.vector, 3, slice(0, 2))
-        finish(nc.vector, 3, slice(2, 4))
+        multiply(units[5])
+        copy_first(blocks[2])
+        copy_first(blocks[3])
+        times_second(blocks[0])
+        times_second(blocks[1])
+        times_third(blocks[0])
+        times_third(blocks[1])
+        early = keep.tile([P, 2, 2, HALF], F32, name="early", tag="reused", align_bytes=64)
+        result[blocks[0]], result[blocks[1]] = early[:, 0], early[:, 1]
+        finish(nc.gpsimd, blocks[0])
+        finish(nc.gpsimd, blocks[1])
+        times_second(blocks[2])
+        times_second(blocks[3])
+        times_third(blocks[2])
+        times_third(blocks[3])
+        finish(nc.vector, blocks[2])
+        finish(nc.vector, blocks[3], slice(0, 1))
+        finish(nc.vector, blocks[3], slice(1, 2))

@@ -20,56 +20,60 @@ P = 128
 PACK = 4
 GROUP = 16
 HALF = 256
-CHUNK = 128
+W4_COLS = 128
 N_TILES = N // P
 RUN = 4
+BANKS = 8
+QUADRANT = 32
+WGT_CUTS = (0, 256, 768, 1536)
 
 
 def tile_list_dl_prod_res_kernel(tc, xT, wgt, w4_words, w4_scales, wd, res, offs, out):
     nc = tc.nc
     with ExitStack() as ctx:
         keep = ctx.enter_context(tc.tile_pool(name="keep", bufs=1))
-        psum = ctx.enter_context(tc.psum_pool(name="psum", bufs=8))
+        psum = ctx.enter_context(tc.psum_pool(name="psum", bufs=BANKS))
 
         offsets = keep.tile([P, PICKS * J // GROUP], U16, name="offsets")
         planes = [keep.tile([P, T], F32, name="plane%d" % t) for t in range(PACK)]
         weights = keep.tile([P, PICKS * J], F32, name="weights")
         w4_codes = keep.tile([P, 2 * N], U8, name="w4_codes", align_bytes=64)
-        w4_plane = keep.tile([P, N], U8, name="w4_plane", align_bytes=64)
+        w4_scale = keep.tile([P, N], U8, name="w4_scale", align_bytes=64)
         wd_raw = [keep.tile([P, PACK, HALF], F32, name="wd_raw%d" % h) for h in range(2)]
         wd_codes = keep.tile([P, N], U32, name="wd_codes", align_bytes=64)
-        wd_plane = keep.tile([P, N], U8, name="wd_plane", align_bytes=64)
+        wd_scale = keep.tile([P, N], U8, name="wd_scale", align_bytes=64)
         residual = keep.tile([P, N_TILES, J], F32, name="residual")
 
         x_rows = xT.rearrange("(p t) w -> t p w", t=PACK)
         wd_rows = wd.rearrange("(p t) n -> p t n", t=PACK)
         out_rows = out.rearrange("(a p) j -> p a j", p=P)
+        wgt_pieces = [slice(WGT_CUTS[i], WGT_CUTS[i + 1]) for i in range(3)]
 
-        nc.vector.memset(w4_plane[:].bitcast(U32), 0)
+        nc.vector.memset(w4_scale[:].bitcast(U32), 0)
         nc.sync.dma_start(out=planes[0][:], in_=x_rows[0])
         nc.sync.dma_start(offsets[:], offs)
-        nc.scalar.dma_start(out=weights[:, 0:256], in_=wgt[:, 0:256])
-        nc.sync.dma_start(out=weights[:, 256:768], in_=wgt[:, 256:768])
-        nc.sync.dma_start(out=weights[:, 768:1536], in_=wgt[:, 768:1536])
-        nc.sync.dma_start(out=planes[1][:], in_=x_rows[1])
-        nc.sync.dma_start(out=wd_raw[0][:], in_=wd_rows[:, :, 0:HALF])
-        nc.sync.dma_start(out=planes[2][:], in_=x_rows[2])
-        nc.sync.dma_start(out=wd_raw[1][:], in_=wd_rows[:, :, HALF:N])
+        nc.scalar.dma_start(out=weights[:, wgt_pieces[0]], in_=wgt[:, wgt_pieces[0]])
+        for piece in wgt_pieces[1:]:
+            nc.sync.dma_start(out=weights[:, piece], in_=wgt[:, piece])
+        for h in range(2):
+            nc.sync.dma_start(out=planes[h + 1][:], in_=x_rows[h + 1])
+            nc.sync.dma_start(out=wd_raw[h][:], in_=wd_rows[:, :, h * HALF : (h + 1) * HALF])
         nc.sync.dma_start(out=planes[3][:], in_=x_rows[3])
-        for q in range(4):
+        for q in range(P // QUADRANT):
             nc.sync.dma_start(
-                out=w4_plane[32 * q : 32 * q + 4, :].bitcast(I32),
+                out=w4_scale[QUADRANT * q : QUADRANT * q + 4, :].bitcast(I32),
                 in_=w4_scales[0, 4 * q : 4 * q + 4, :].bitcast(I32),
             )
         nc.sync.dma_start(out=w4_codes[:].bitcast(I32), in_=w4_words[0].bitcast(I32))
         nc.sync.dma_start(out=residual[:], in_=res.rearrange("(a p) j -> p a j", p=P))
 
         units = [(h, c) for h in range(2) for c in range(PICKS)]
+        last = units[-1]
         low0 = keep.tile([P, 2, J], F32, name="low0")
-        slots1 = keep.tile([P, PACK, HALF], F32, name="slots1")
-        slots2 = keep.tile([P, PACK, HALF], F32, name="slots2")
+        whole1 = keep.tile([P, PACK, HALF], F32, name="whole1")
+        whole2 = keep.tile([P, PACK, HALF], F32, name="whole2")
         high0 = keep.tile([P, 3, HALF], F32, name="high0")
-        whole = {(0, 1): slots1[:], (0, 2): slots2[:]}
+        whole = {(0, 1): whole1[:], (0, 2): whole2[:]}
         low = {(0, 0): low0[:, :, 0:HALF], (1, 0): low0[:, :, HALF:J]}
         high = {(0, 0): high0[:, 1:3, :], (1, 0): high0[:, 0:3:2, :]}
         for c in (1, 2):
@@ -77,9 +81,9 @@ def tile_list_dl_prod_res_kernel(tc, xT, wgt, w4_words, w4_scales, wd, res, offs
             low[1, c] = keep.tile([P, 2, HALF], F32, name="low%d" % c)[:]
             high[0, c] = high[1, c] = whole[0, c][:, 2:4, :]
         rounded = {u: keep.tile([P, HALF * PACK], BF16, name="rounded%d%d" % u, align_bytes=64) for u in units[:-1]}
-        rounded[units[-1]] = keep.tile([P, HALF * PACK], BF16, name="rounded_last", tag="reused", align_bytes=64)
+        rounded[last] = keep.tile([P, HALF * PACK], BF16, name="rounded_last", tag="reused", align_bytes=64)
         x_codes = {u: keep.tile([P, HALF], U32, name="x_codes%d%d" % u, align_bytes=64) for u in units}
-        x_plane = {u: keep.tile([P, HALF], U8, name="x_plane%d%d" % u, align_bytes=64) for u in units}
+        x_scale = {u: keep.tile([P, HALF], U8, name="x_scale%d%d" % u, align_bytes=64) for u in units}
         wd_rounded = [keep.tile([P, HALF * PACK], BF16, name="wd_rounded%d" % h, align_bytes=64) for h in range(2)]
         blocks = [(h, r) for h in range(2) for r in range(2)]
         first = {b: keep.tile([P, 2, HALF], F32, name="first%d%d" % b) for b in blocks}
@@ -88,77 +92,59 @@ def tile_list_dl_prod_res_kernel(tc, xT, wgt, w4_words, w4_scales, wd, res, offs
         result = {b: keep.tile([P, 2, HALF], F32, name="result%d%d" % b) for b in blocks[2:]}
         sums = {}
 
+        def half(h):
+            return slice(h * HALF, (h + 1) * HALF)
+
         def gather(dst, t, c, places):
             m0, m1 = c * J + places.start, c * J + places.stop
             window = planes[t][:].indirect(offsets[:, m0 // GROUP : m1 // GROUP])
             nc.vector.tensor_tensor(dst, window, weights[:, m0:m1], MULT)
-
-        def half(h):
-            return slice(h * HALF, (h + 1) * HALF)
 
         def gather_unit(t, u):
             gather((low, high)[t // 2][u][:, t % 2, :], t, u[1], half(u[0]))
 
         def interleave(dst, src):
             nc.scalar.copy(
-                out=dst.rearrange("p (c i t) -> p c t i", i=RUN, t=PACK),
-                in_=src.rearrange("p t (c i) -> p c t i", i=RUN),
+                out=dst.rearrange("p (g i t) -> p g t i", i=RUN, t=PACK),
+                in_=src.rearrange("p t (g i) -> p g t i", i=RUN),
             )
 
-        def interleave_pair(u, e, cols=slice(0, HALF)):
+        def interleave_pair(u, e):
             nc.scalar.copy(
-                out=rounded[u][:].rearrange("p (j t) -> p j t", t=PACK)[:, cols, 2 * e : 2 * e + 2],
-                in_=(low, high)[e][u][:, :, cols].rearrange("p t j -> p j t"),
+                out=rounded[u][:].rearrange("p (j t) -> p j t", t=PACK)[:, :, 2 * e : 2 * e + 2],
+                in_=(low, high)[e][u].rearrange("p t j -> p j t"),
             )
-
-        def quantize_x(u, cols=slice(0, HALF)):
-            values = rounded[u][:, PACK * cols.start : PACK * cols.stop]
-            nc.vector.quantize_mx(out=x_codes[u][:, cols].bitcast(FP8X4), scales=x_plane[u][:, cols], in_=values)
-
-        def quantize_wd(h):
-            cols = slice(h * HALF, (h + 1) * HALF)
-            nc.vector.quantize_mx(out=wd_codes[:, cols].bitcast(FP8X4), scales=wd_plane[:, cols], in_=wd_rounded[h][:])
 
         def project(u, r):
-            acc = psum.tile([P, 2, HALF], F32, name="acc")
-            sums[u, r] = acc
+            if u == last:
+                acc = [psum.tile([P, HALF], F32, name="acc")[:] for i in range(2)]
+                sums[u, r] = acc
+            else:
+                bank = psum.tile([P, 2, HALF], F32, name="acc")
+                sums[u, r] = bank
+                acc = [bank[:, i, :] for i in range(2)]
             for i in range(2):
                 a = 2 * r + i
                 nc.tensor.matmul_mx(
-                    out=acc[:, i, :],
+                    out=acc[i],
                     lhsT=wd_codes[:, P * a : P * (a + 1)].bitcast(FP8X4),
-                    lhsT_scale=wd_plane[:, P * a : P * (a + 1)],
+                    lhsT_scale=wd_scale[:, P * a : P * (a + 1)],
                     rhs=x_codes[u][:].bitcast(FP8X4),
-                    rhs_scale=x_plane[u][:],
+                    rhs_scale=x_scale[u][:],
                     start=True,
                     stop=False,
                 )
-                for k in range(2):
-                    cols = slice(k * CHUNK, (k + 1) * CHUNK)
+                for j0 in range(0, HALF, W4_COLS):
+                    cols = slice(j0, j0 + W4_COLS)
                     nc.tensor.matmul_mx(
-                        out=acc[:, i, cols],
+                        out=acc[i][:, cols],
                         lhsT=w4_codes[:, 2 * P * a : 2 * P * (a + 1)].bitcast(FP4X4),
-                        lhsT_scale=w4_plane[:, P * a : P * (a + 1)],
+                        lhsT_scale=w4_scale[:, P * a : P * (a + 1)],
                         rhs=x_codes[u][:, cols].bitcast(FP8X4),
-                        rhs_scale=x_plane[u][:, cols],
+                        rhs_scale=x_scale[u][:, cols],
                         start=False,
-                        stop=(k == 1),
+                        stop=(j0 + W4_COLS == HALF),
                     )
-
-        def copy_first(b):
-            nc.scalar.copy(out=first[b][:], in_=sums[(b[0], 0), b[1]][:])
-
-        def times_second(b):
-            nc.vector.tensor_tensor(pair[b][:], sums[(b[0], 1), b[1]][:], first[b][:], MULT)
-
-        def times_third(b):
-            nc.vector.tensor_tensor(triple[b][:], sums[(b[0], 2), b[1]][:], pair[b][:], MULT)
-
-        def finish(engine, b, tiles=slice(0, 2)):
-            h, r = b
-            rows = slice(2 * r + tiles.start, 2 * r + tiles.stop)
-            engine.tensor_tensor(result[b][:, tiles, :], triple[b][:, tiles, :], residual[:, rows, half(h)], ADD)
-            nc.sync.dma_start(out=out_rows[:, rows, half(h)], in_=result[b][:, tiles, :])
 
         def prepare(u):
             gather_unit(2, u)
@@ -169,52 +155,74 @@ def tile_list_dl_prod_res_kernel(tc, xT, wgt, w4_words, w4_scales, wd, res, offs
                 interleave_pair(u, 1)
 
         def multiply(u):
-            quantize_x(u)
+            nc.vector.quantize_mx(out=x_codes[u][:].bitcast(FP8X4), scales=x_scale[u][:], in_=rounded[u][:])
             project(u, 0)
             project(u, 1)
 
+        def copy_first(b):
+            nc.scalar.copy(out=first[b][:], in_=sums[(b[0], 0), b[1]][:])
+
+        def times_second(b):
+            nc.vector.tensor_tensor(pair[b][:], sums[(b[0], 1), b[1]][:], first[b][:], MULT)
+
+        def times_third(b):
+            nc.vector.tensor_tensor(triple[b][:], sums[(b[0], 2), b[1]][:], pair[b][:], MULT)
+
+        def times_third_last(b, i):
+            nc.vector.tensor_tensor(triple[b][:, i, :], sums[last, b[1]][i], pair[b][:, i, :], MULT)
+
+        def finish(engine, queue, b, tiles):
+            h, r = b
+            rows = slice(2 * r + tiles.start, 2 * r + tiles.stop)
+            engine.tensor_tensor(result[b][:, tiles, :], triple[b][:, tiles, :], residual[:, rows, half(h)], ADD)
+            queue.dma_start(out=out_rows[:, rows, half(h)], in_=result[b][:, tiles, :])
+
         for h in range(2):
             interleave(wd_rounded[h][:], wd_raw[h][:])
-            quantize_wd(h)
+            nc.vector.quantize_mx(
+                out=wd_codes[:, half(h)].bitcast(FP8X4), scales=wd_scale[:, half(h)], in_=wd_rounded[h][:]
+            )
+
         for c in range(PICKS):
             for h in range(2):
                 gather_unit(0, (h, c))
-        gather_unit(1, (0, 1))
-        gather_unit(1, (0, 2))
+        for u in whole:
+            gather_unit(1, u)
         gather(low0[:, 1, :], 1, 0, slice(0, J))
-        gather_unit(1, (1, 1))
-        gather_unit(1, (1, 2))
+        for u in units[4:]:
+            gather_unit(1, u)
         for u in units:
             if u not in whole:
                 interleave_pair(u, 0)
-        prepare(units[0])
-        prepare(units[1])
-        prepare(units[2])
-        multiply(units[0])
-        prepare(units[3])
-        multiply(units[1])
-        prepare(units[4])
-        copy_first(blocks[0])
-        copy_first(blocks[1])
-        multiply(units[2])
-        prepare(units[5])
-        multiply(units[3])
-        multiply(units[4])
-        multiply(units[5])
+
+        for u in units[:PICKS]:
+            prepare(u)
+        for i in range(PICKS):
+            if i == PICKS - 1:
+                copy_first(blocks[0])
+                copy_first(blocks[1])
+            multiply(units[i])
+            prepare(units[i + PICKS])
+        for u in units[PICKS:]:
+            multiply(u)
         copy_first(blocks[2])
         copy_first(blocks[3])
-        times_second(blocks[0])
-        times_second(blocks[1])
-        times_third(blocks[0])
-        times_third(blocks[1])
+
+        for b in blocks[:2]:
+            times_second(b)
+        for b in blocks[:2]:
+            times_third(b)
         early = keep.tile([P, 2, 2, HALF], F32, name="early", tag="reused", align_bytes=64)
-        result[blocks[0]], result[blocks[1]] = early[:, 0], early[:, 1]
-        finish(nc.gpsimd, blocks[0])
-        finish(nc.gpsimd, blocks[1])
-        times_second(blocks[2])
-        times_second(blocks[3])
-        times_third(blocks[2])
-        times_third(blocks[3])
-        finish(nc.vector, blocks[2])
-        finish(nc.vector, blocks[3], slice(0, 1))
-        finish(nc.vector, blocks[3], slice(1, 2))
+        for b in blocks[:2]:
+            result[b] = early[:, b[1]]
+            finish(nc.gpsimd, nc.sync, b, slice(0, 2))
+
+        for b in blocks[2:]:
+            times_second(b)
+        for b in blocks[2:]:
+            for i in range(2):
+                times_third_last(b, i)
+        finish(nc.gpsimd, nc.sync, blocks[2], slice(0, 1))
+        finish(nc.vector, nc.sync, blocks[2], slice(1, 2))
+        finish(nc.vector, nc.scalar, blocks[3], slice(0, 1))
+        finish(nc.vector, nc.sync, blocks[3], slice(1, 2))

@@ -36,12 +36,13 @@ def tile_list_dl_prod_res_kernel(tc, xT, wgt, w4_words, w4_scales, wd, res, offs
 
         offsets = keep.tile([P, PICKS * J // GROUP], U16, name="offsets")
         planes = [keep.tile([P, T], F32, name="plane%d" % t) for t in range(PACK)]
-        weights = keep.tile([P, PICKS * J], F32, name="weights")
+        weights0 = keep.tile([P, HALF], F32, name="weights0", tag="head", align_bytes=64)
+        weights = keep.tile([P, PICKS * J], F32, name="weights", tag="late")
         w4_codes = keep.tile([P, 2 * N], U8, name="w4_codes", align_bytes=64)
         w4_scale = keep.tile([P, N], U8, name="w4_scale", align_bytes=64)
         wd_raw = [keep.tile([P, PACK, HALF], F32, name="wd_raw%d" % h) for h in range(2)]
-        wd_codes = keep.tile([P, N], U32, name="wd_codes", align_bytes=64)
-        wd_scale = keep.tile([P, N], U8, name="wd_scale", align_bytes=64)
+        wd_codes = [keep.tile([P, HALF], U32, name="wd_codes0", align_bytes=64)]
+        wd_scale = [keep.tile([P, HALF], U8, name="wd_scale%d" % h, align_bytes=64) for h in range(2)]
         residual = keep.tile([P, N_TILES, J], F32, name="residual")
 
         x_rows = xT.rearrange("(p t) w -> t p w", t=PACK)
@@ -52,34 +53,38 @@ def tile_list_dl_prod_res_kernel(tc, xT, wgt, w4_words, w4_scales, wd, res, offs
         nc.vector.memset(w4_scale[:].bitcast(U32), 0)
         nc.sync.dma_start(out=planes[0][:], in_=x_rows[0])
         nc.sync.dma_start(offsets[:], offs)
-        nc.scalar.dma_start(out=weights[:, wgt_pieces[0]], in_=wgt[:, wgt_pieces[0]])
+        nc.scalar.dma_start(out=weights0[:], in_=wgt[:, wgt_pieces[0]])
         for piece in wgt_pieces[1:]:
             nc.sync.dma_start(out=weights[:, piece], in_=wgt[:, piece])
-        for h in range(2):
-            nc.sync.dma_start(out=planes[h + 1][:], in_=x_rows[h + 1])
-            nc.sync.dma_start(out=wd_raw[h][:], in_=wd_rows[:, :, h * HALF : (h + 1) * HALF])
-        nc.sync.dma_start(out=planes[3][:], in_=x_rows[3])
+        nc.sync.dma_start(out=planes[1][:], in_=x_rows[1])
+        nc.sync.dma_start(out=wd_raw[0][:], in_=wd_rows[:, :, 0:HALF])
+        nc.sync.dma_start(out=planes[2][:], in_=x_rows[2])
         for q in range(P // QUADRANT):
             nc.sync.dma_start(
                 out=w4_scale[QUADRANT * q : QUADRANT * q + 4, :].bitcast(I32),
                 in_=w4_scales[0, 4 * q : 4 * q + 4, :].bitcast(I32),
             )
+        nc.sync.dma_start(out=wd_raw[1][:], in_=wd_rows[:, :, HALF:N])
+        nc.sync.dma_start(out=planes[3][:], in_=x_rows[3])
         nc.sync.dma_start(out=w4_codes[:].bitcast(I32), in_=w4_words[0].bitcast(I32))
         nc.sync.dma_start(out=residual[:], in_=res.rearrange("(a p) j -> p a j", p=P))
 
         units = [(h, c) for h in range(2) for c in range(PICKS)]
         last = units[-1]
-        low0 = keep.tile([P, 2, J], F32, name="low0")
-        whole1 = keep.tile([P, PACK, HALF], F32, name="whole1")
-        whole2 = keep.tile([P, PACK, HALF], F32, name="whole2")
-        high0 = keep.tile([P, 3, HALF], F32, name="high0")
-        whole = {(0, 1): whole1[:], (0, 2): whole2[:]}
-        low = {(0, 0): low0[:, :, 0:HALF], (1, 0): low0[:, :, HALF:J]}
-        high = {(0, 0): high0[:, 1:3, :], (1, 0): high0[:, 0:3:2, :]}
-        for c in (1, 2):
-            low[0, c] = whole[0, c][:, 0:2, :]
-            low[1, c] = keep.tile([P, 2, HALF], F32, name="low%d" % c)[:]
-            high[0, c] = high[1, c] = whole[0, c][:, 2:4, :]
+        lows = keep.tile([P, 2, 5 * HALF], F32, name="lows")
+        even = keep.tile([P, PACK, HALF], F32, name="even")
+        odd = keep.tile([P, PACK, HALF], F32, name="odd")
+        low = {(h, c): lows[:, :, (2 * c + h) * HALF : (2 * c + h + 1) * HALF] for (h, c) in units[:-1]}
+        low[last] = odd[:, 0:2, :]
+        high = {
+            (0, 0): even[:, 0:4:3, :],
+            (0, 1): odd[:, 2:4, :],
+            (0, 2): even[:, 2:4, :],
+            (1, 0): odd[:, 1:4:2, :],
+            (1, 1): even[:, 1:4:2, :],
+            (1, 2): odd[:, 2:4, :],
+        }
+        whole = {last: odd[:]}
         rounded = {u: keep.tile([P, HALF * PACK], BF16, name="rounded%d%d" % u, align_bytes=64) for u in units[:-1]}
         rounded[last] = keep.tile([P, HALF * PACK], BF16, name="rounded_last", tag="reused", align_bytes=64)
         x_codes = {u: keep.tile([P, HALF], U32, name="x_codes%d%d" % u, align_bytes=64) for u in units}
@@ -87,7 +92,7 @@ def tile_list_dl_prod_res_kernel(tc, xT, wgt, w4_words, w4_scales, wd, res, offs
         wd_rounded = [keep.tile([P, HALF * PACK], BF16, name="wd_rounded%d" % h, align_bytes=64) for h in range(2)]
         blocks = [(h, r) for h in range(2) for r in range(2)]
         first = {b: keep.tile([P, 2, HALF], F32, name="first%d%d" % b) for b in blocks}
-        pair = {b: keep.tile([P, 2, HALF], F32, name="pair%d%d" % b) for b in blocks}
+        pair = {b: keep.tile([P, 2, HALF], F32, name="pair%d%d" % b)[:] for b in blocks[2:]}
         triple = {b: keep.tile([P, 2, HALF], F32, name="triple%d%d" % b) for b in blocks}
         result = {b: keep.tile([P, 2, HALF], F32, name="result%d%d" % b) for b in blocks[2:]}
         sums = {}
@@ -95,13 +100,13 @@ def tile_list_dl_prod_res_kernel(tc, xT, wgt, w4_words, w4_scales, wd, res, offs
         def half(h):
             return slice(h * HALF, (h + 1) * HALF)
 
-        def gather(dst, t, c, places):
-            m0, m1 = c * J + places.start, c * J + places.stop
+        def gather(dst, t, m0, m1):
             window = planes[t][:].indirect(offsets[:, m0 // GROUP : m1 // GROUP])
-            nc.vector.tensor_tensor(dst, window, weights[:, m0:m1], MULT)
+            nc.vector.tensor_tensor(dst, window, (weights0 if m0 == 0 else weights)[:, m0:m1], MULT)
 
         def gather_unit(t, u):
-            gather((low, high)[t // 2][u][:, t % 2, :], t, u[1], half(u[0]))
+            m0 = u[1] * J + u[0] * HALF
+            gather((low, high)[t // 2][u][:, t % 2, :], t, m0, m0 + HALF)
 
         def interleave(dst, src):
             nc.scalar.copy(
@@ -127,8 +132,8 @@ def tile_list_dl_prod_res_kernel(tc, xT, wgt, w4_words, w4_scales, wd, res, offs
                 a = 2 * r + i
                 nc.tensor.matmul_mx(
                     out=acc[i],
-                    lhsT=wd_codes[:, P * a : P * (a + 1)].bitcast(FP8X4),
-                    lhsT_scale=wd_scale[:, P * a : P * (a + 1)],
+                    lhsT=wd_codes[r][:, P * i : P * (i + 1)].bitcast(FP8X4),
+                    lhsT_scale=wd_scale[r][:, P * i : P * (i + 1)],
                     rhs=x_codes[u][:].bitcast(FP8X4),
                     rhs_scale=x_scale[u][:],
                     start=True,
@@ -147,7 +152,9 @@ def tile_list_dl_prod_res_kernel(tc, xT, wgt, w4_words, w4_scales, wd, res, offs
                     )
 
         def prepare(u):
-            gather_unit(2, u)
+            if u in whole:
+                gather_unit(2, u)
+                gather_unit(1, u)
             gather_unit(3, u)
             if u in whole:
                 interleave(rounded[u][:], whole[u])
@@ -163,10 +170,10 @@ def tile_list_dl_prod_res_kernel(tc, xT, wgt, w4_words, w4_scales, wd, res, offs
             nc.scalar.copy(out=first[b][:], in_=sums[(b[0], 0), b[1]][:])
 
         def times_second(b):
-            nc.vector.tensor_tensor(pair[b][:], sums[(b[0], 1), b[1]][:], first[b][:], MULT)
+            nc.vector.tensor_tensor(pair[b], sums[(b[0], 1), b[1]][:], first[b][:], MULT)
 
         def times_third(b):
-            nc.vector.tensor_tensor(triple[b][:], sums[(b[0], 2), b[1]][:], pair[b][:], MULT)
+            nc.vector.tensor_tensor(triple[b][:], sums[(b[0], 2), b[1]][:], pair[b], MULT)
 
         def times_third_last(b, i):
             nc.vector.tensor_tensor(triple[b][:, i, :], sums[last, b[1]][i], pair[b][:, i, :], MULT)
@@ -177,43 +184,48 @@ def tile_list_dl_prod_res_kernel(tc, xT, wgt, w4_words, w4_scales, wd, res, offs
             engine.tensor_tensor(result[b][:, tiles, :], triple[b][:, tiles, :], residual[:, rows, half(h)], ADD)
             queue.dma_start(out=out_rows[:, rows, half(h)], in_=result[b][:, tiles, :])
 
+        def quantize_wd(h):
+            nc.vector.quantize_mx(out=wd_codes[h][:].bitcast(FP8X4), scales=wd_scale[h][:], in_=wd_rounded[h][:])
+
         for h in range(2):
             interleave(wd_rounded[h][:], wd_raw[h][:])
-            nc.vector.quantize_mx(
-                out=wd_codes[:, half(h)].bitcast(FP8X4), scales=wd_scale[:, half(h)], in_=wd_rounded[h][:]
-            )
+        quantize_wd(0)
 
-        for c in range(PICKS):
-            for h in range(2):
-                gather_unit(0, (h, c))
-        for u in whole:
-            gather_unit(1, u)
-        gather(low0[:, 1, :], 1, 0, slice(0, J))
-        for u in units[4:]:
-            gather_unit(1, u)
-        for u in units:
-            if u not in whole:
-                interleave_pair(u, 0)
+        cuts = (0, HALF, 3 * HALF, 5 * HALF)
+        for t in range(2):
+            for i in range(3):
+                gather(lows[:, t, cuts[i] : cuts[i + 1]], t, cuts[i], cuts[i + 1])
+            if t == 0:
+                gather_unit(0, last)
+        for u in ((0, 0), (1, 0), (0, 1), (1, 1), (0, 2)):
+            interleave_pair(u, 0)
+        gather_unit(2, (0, 0))
+        gather(odd[:, 1:3, :].rearrange("p s j -> p (s j)"), 2, cuts[1], cuts[2])
+        gather(even[:, 1:3, :].rearrange("p s j -> p (s j)"), 2, cuts[2], cuts[3])
 
-        for u in units[:PICKS]:
-            prepare(u)
-        for i in range(PICKS):
-            if i == PICKS - 1:
+        prepare(units[0])
+        prepare(units[1])
+        wd_codes.append(keep.tile([P, HALF], U32, name="wd_codes1", tag="head", align_bytes=64))
+        quantize_wd(1)
+        for i in range(4):
+            multiply(units[i])
+            if i == 3:
                 copy_first(blocks[0])
                 copy_first(blocks[1])
-            multiply(units[i])
-            prepare(units[i + PICKS])
-        for u in units[PICKS:]:
-            multiply(u)
+            prepare(units[i + 2])
+        multiply(units[4])
+        multiply(units[5])
         copy_first(blocks[2])
         copy_first(blocks[3])
 
+        pair0 = keep.tile([P, 2, 2, HALF], F32, name="pair0", tag="late")
+        for b in blocks[:2]:
+            pair[b] = pair0[:, b[1]]
+        early = keep.tile([P, 2, 2, HALF], F32, name="early", tag="reused", align_bytes=64)
         for b in blocks[:2]:
             times_second(b)
         for b in blocks[:2]:
             times_third(b)
-        early = keep.tile([P, 2, 2, HALF], F32, name="early", tag="reused", align_bytes=64)
-        for b in blocks[:2]:
             result[b] = early[:, b[1]]
             finish(nc.gpsimd, nc.sync, b, slice(0, 2))
 

@@ -1,6 +1,7 @@
 from contextlib import ExitStack
 
 import concourse.mybir as mybir
+from concourse.masks import make_identity
 
 K, N, T, J, PICKS = 512, 512, 2048, 512, 3
 FLOPS = 2 * 2 * K * N * J * PICKS
@@ -25,7 +26,7 @@ N_TILES = N // P
 RUN = 4
 BANKS = 8
 QUADRANT = 32
-WGT_CUTS = (0, 256, 768, 1536)
+WGT_CUTS = (0, 128, 256, 512)
 
 
 def tile_list_dl_prod_res_kernel(tc, xT, wgt, w4_words, w4_scales, wd, res, offs, out):
@@ -36,61 +37,82 @@ def tile_list_dl_prod_res_kernel(tc, xT, wgt, w4_words, w4_scales, wd, res, offs
 
         offsets = keep.tile([P, PICKS * J // GROUP], U16, name="offsets")
         planes = [keep.tile([P, T], F32, name="plane%d" % t) for t in range(PACK)]
-        weights0 = keep.tile([P, HALF], F32, name="weights0", tag="head", align_bytes=64)
-        weights = keep.tile([P, PICKS * J], F32, name="weights", tag="late")
+        weights = keep.tile([P, PICKS * J], F32, name="weights")
         w4_codes = keep.tile([P, 2 * N], U8, name="w4_codes", align_bytes=64)
         w4_scale = keep.tile([P, N], U8, name="w4_scale", align_bytes=64)
         wd_raw = [keep.tile([P, PACK, HALF], F32, name="wd_raw%d" % h) for h in range(2)]
-        wd_codes = [keep.tile([P, HALF], U32, name="wd_codes0", align_bytes=64)]
+        wd_codes = [keep.tile([P, HALF], U32, name="wd_codes%d" % h, align_bytes=64) for h in range(2)]
         wd_scale = [keep.tile([P, HALF], U8, name="wd_scale%d" % h, align_bytes=64) for h in range(2)]
         residual = keep.tile([P, N_TILES, J], F32, name="residual")
 
         x_rows = xT.rearrange("(p t) w -> t p w", t=PACK)
         wd_rows = wd.rearrange("(p t) n -> p t n", t=PACK)
         out_rows = out.rearrange("(a p) j -> p a j", p=P)
-        wgt_pieces = [slice(WGT_CUTS[i], WGT_CUTS[i + 1]) for i in range(3)]
+        wgt_pieces = [slice(0, P), slice(P, 3 * P), slice(11 * P, 12 * P)]
 
         nc.vector.memset(w4_scale[:].bitcast(U32), 0)
-        nc.sync.dma_start(out=planes[0][:], in_=x_rows[0])
-        nc.sync.dma_start(offsets[:], offs)
-        nc.scalar.dma_start(out=weights0[:], in_=wgt[:, wgt_pieces[0]])
-        for piece in wgt_pieces[1:]:
-            nc.sync.dma_start(out=weights[:, piece], in_=wgt[:, piece])
-        nc.sync.dma_start(out=planes[1][:], in_=x_rows[1])
-        nc.sync.dma_start(out=wd_raw[0][:], in_=wd_rows[:, :, 0:HALF])
-        nc.sync.dma_start(out=planes[2][:], in_=x_rows[2])
-        for q in range(P // QUADRANT):
+        thin = keep.tile([P, P], F32, name="thin")
+        spread = [
+            keep.tile([P, 2, 2, P], F32, name="spread%d" % e, tag="spread%d" % e, align_bytes=64) for e in range(2)
+        ]
+        identity = keep.tile([P, P], F32, name="identity")
+        make_identity(nc, identity[:])
+
+        def load_scales(q):
             nc.sync.dma_start(
                 out=w4_scale[QUADRANT * q : QUADRANT * q + 4, :].bitcast(I32),
                 in_=w4_scales[0, 4 * q : 4 * q + 4, :].bitcast(I32),
             )
+
+        nc.sync.dma_start(out=thin[:], in_=wgt.rearrange("(u a) (c w) -> u (a c) w", a=8, w=P)[:, 10:88:11, :])
+        nc.sync.dma_start(out=planes[0][:], in_=x_rows[0])
+        nc.sync.dma_start(offsets[:], offs)
+        nc.scalar.dma_start(out=weights[:, wgt_pieces[0]], in_=wgt[:, wgt_pieces[0]])
+        for piece in wgt_pieces[1:]:
+            nc.sync.dma_start(out=weights[:, piece], in_=wgt[:, piece])
+        nc.sync.dma_start(out=wd_raw[0][:], in_=wd_rows[:, :, 0:HALF])
+        nc.sync.dma_start(out=planes[1][:], in_=x_rows[1])
+        nc.sync.dma_start(out=planes[2][:], in_=x_rows[2])
         nc.sync.dma_start(out=wd_raw[1][:], in_=wd_rows[:, :, HALF:N])
         nc.sync.dma_start(out=planes[3][:], in_=x_rows[3])
+        for q in range(P // QUADRANT):
+            load_scales(q)
         nc.sync.dma_start(out=w4_codes[:].bitcast(I32), in_=w4_words[0].bitcast(I32))
         nc.sync.dma_start(out=residual[:], in_=res.rearrange("(a p) j -> p a j", p=P))
 
-        units = [(h, c) for h in range(2) for c in range(PICKS)]
+        units = [(h, c) for h in (1, 0) for c in range(PICKS)]
         last = units[-1]
-        lows = keep.tile([P, 2, 5 * HALF], F32, name="lows")
-        even = keep.tile([P, PACK, HALF], F32, name="even")
-        odd = keep.tile([P, PACK, HALF], F32, name="odd")
-        low = {(h, c): lows[:, :, (2 * c + h) * HALF : (2 * c + h + 1) * HALF] for (h, c) in units[:-1]}
-        low[last] = odd[:, 0:2, :]
-        high = {
-            (0, 0): even[:, 0:4:3, :],
-            (0, 1): odd[:, 2:4, :],
-            (0, 2): even[:, 2:4, :],
-            (1, 0): odd[:, 1:4:2, :],
-            (1, 1): even[:, 1:4:2, :],
-            (1, 2): odd[:, 2:4, :],
-        }
-        whole = {last: odd[:]}
+        turned = psum.tile([P, P], F32, name="acc")
+        nc.tensor.transpose(turned[:], thin[:], identity[:])
+        batches = (slice(1, 3), slice(0, 4, 3))
+        for e in range(2):
+            nc.scalar.copy(
+                out=spread[e][:].rearrange("p a b (u r) -> p a b u r", r=8),
+                in_=turned[:].rearrange("p (u a b) -> p a b u", a=2, b=4)[:, :, batches[e], :]
+                .unsqueeze(4)
+                .to_broadcast([P, 2, 2, 16, 8]),
+            )
+        quads = weights[:, 3 * P : 11 * P].rearrange("p (a b w) -> p a b w", a=2, w=P)
+        for e in range(2):
+            back = psum.tile([P, 2, 2, P], F32, name="acc")
+            for a in range(2):
+                for b in range(2):
+                    nc.tensor.transpose(back[:, a, b, :], spread[e][:, 1 - a, 1 - b, :], identity[:])
+            nc.scalar.copy(out=quads[:, :, batches[e], :], in_=back[:])
+
+        picked = [
+            keep.tile([P, 4 if c else 7, HALF], F32, name="picked%d" % c, tag="picked%d" % c, align_bytes=64)
+            for c in range(PICKS)
+        ]
+        highs = [picked[0][:, 4:7:2, :]] + [keep.tile([P, 2, HALF], F32, name="high%d" % c)[:] for c in (1, 2)]
+        low = {(h, c): picked[c][:, h : h + 3 : 2, :] for (h, c) in units}
+        high = {(h, c): highs[c] for (h, c) in units}
+        whole = units[PICKS : PICKS + 1]
         rounded = {u: keep.tile([P, HALF * PACK], BF16, name="rounded%d%d" % u, align_bytes=64) for u in units[:-1]}
         rounded[last] = keep.tile([P, HALF * PACK], BF16, name="rounded_last", tag="reused", align_bytes=64)
         x_codes = {u: keep.tile([P, HALF], U32, name="x_codes%d%d" % u, align_bytes=64) for u in units}
         x_scale = {u: keep.tile([P, HALF], U8, name="x_scale%d%d" % u, align_bytes=64) for u in units}
-        wd_rounded = [keep.tile([P, HALF * PACK], BF16, name="wd_rounded%d" % h, align_bytes=64) for h in range(2)]
-        blocks = [(h, r) for h in range(2) for r in range(2)]
+        blocks = [(h, r) for h in (1, 0) for r in range(2)]
         first = {b: keep.tile([P, 2, HALF], F32, name="first%d%d" % b) for b in blocks}
         pair = {b: keep.tile([P, 2, HALF], F32, name="pair%d%d" % b)[:] for b in blocks[2:]}
         triple = {b: keep.tile([P, 2, HALF], F32, name="triple%d%d" % b) for b in blocks}
@@ -102,7 +124,7 @@ def tile_list_dl_prod_res_kernel(tc, xT, wgt, w4_words, w4_scales, wd, res, offs
 
         def gather(dst, t, m0, m1):
             window = planes[t][:].indirect(offsets[:, m0 // GROUP : m1 // GROUP])
-            nc.vector.tensor_tensor(dst, window, (weights0 if m0 == 0 else weights)[:, m0:m1], MULT)
+            nc.vector.tensor_tensor(dst, window, weights[:, m0:m1], MULT)
 
         def gather_unit(t, u):
             m0 = u[1] * J + u[0] * HALF
@@ -151,13 +173,22 @@ def tile_list_dl_prod_res_kernel(tc, xT, wgt, w4_words, w4_scales, wd, res, offs
                         stop=(j0 + W4_COLS == HALF),
                     )
 
+        def gather_pick(t, c):
+            gather(picked[c][:, 2 * t : 2 * t + 2, :].rearrange("p s j -> p (s j)"), t, c * J, (c + 1) * J)
+
+        def interleave_whole(u):
+            slots = picked[u[1]][:, 0:7:2, :].rearrange("p (e s) (g i) -> p g e s i", s=2, i=RUN)
+            nc.scalar.copy(
+                out=rounded[u][:].rearrange("p (g i e s) -> p g e s i", i=RUN, e=2, s=2),
+                in_=slots,
+            )
+
         def prepare(u):
-            if u in whole:
+            if u in units[PICKS:]:
                 gather_unit(2, u)
-                gather_unit(1, u)
             gather_unit(3, u)
             if u in whole:
-                interleave(rounded[u][:], whole[u])
+                interleave_whole(u)
             else:
                 interleave_pair(u, 1)
 
@@ -184,47 +215,44 @@ def tile_list_dl_prod_res_kernel(tc, xT, wgt, w4_words, w4_scales, wd, res, offs
             engine.tensor_tensor(result[b][:, tiles, :], triple[b][:, tiles, :], residual[:, rows, half(h)], ADD)
             queue.dma_start(out=out_rows[:, rows, half(h)], in_=result[b][:, tiles, :])
 
-        def quantize_wd(h):
-            nc.vector.quantize_mx(out=wd_codes[h][:].bitcast(FP8X4), scales=wd_scale[h][:], in_=wd_rounded[h][:])
 
-        for h in range(2):
-            interleave(wd_rounded[h][:], wd_raw[h][:])
-        quantize_wd(0)
+        def round_wd(h, room):
+            wd_rounded = keep.tile([P, HALF * PACK], BF16, name="wd_rounded%d" % h, tag=room, align_bytes=64)
+            interleave(wd_rounded[:], wd_raw[h][:])
+            nc.vector.quantize_mx(out=wd_codes[h][:].bitcast(FP8X4), scales=wd_scale[h][:], in_=wd_rounded[:])
 
-        cuts = (0, HALF, 3 * HALF, 5 * HALF)
-        for t in range(2):
-            for i in range(3):
-                gather(lows[:, t, cuts[i] : cuts[i + 1]], t, cuts[i], cuts[i + 1])
-            if t == 0:
-                gather_unit(0, last)
-        for u in ((0, 0), (1, 0), (0, 1), (1, 1), (0, 2)):
+        round_wd(0, "spread1")
+        for m0, m1 in ((0, P), (P, 3 * P), (11 * P, 12 * P), (3 * P, J), (J, 2 * J), (2 * J, 11 * P)):
+            c = m0 // J
+            gather(picked[c][:, 0:2, :].rearrange("p s j -> p (s j)")[:, m0 - c * J : m1 - c * J], 0, m0, m1)
+        for c in (1, 2, 0):
+            gather_pick(1, c)
+        for u in ((1, 1), (0, 1), (1, 2)):
             interleave_pair(u, 0)
-        gather_unit(2, (0, 0))
-        gather(odd[:, 1:3, :].rearrange("p s j -> p (s j)"), 2, cuts[1], cuts[2])
-        gather(even[:, 1:3, :].rearrange("p s j -> p (s j)"), 2, cuts[2], cuts[3])
+        for u in units[:PICKS]:
+            gather_unit(2, u)
+        round_wd(1, "picked1")
+        for u in ((0, 2), (1, 0)):
+            interleave_pair(u, 0)
 
-        prepare(units[0])
-        prepare(units[1])
-        wd_codes.append(keep.tile([P, HALF], U32, name="wd_codes1", tag="head", align_bytes=64))
-        quantize_wd(1)
-        for i in range(4):
+        for u in units[:PICKS]:
+            prepare(u)
+        for i in range(PICKS):
             multiply(units[i])
-            if i == 3:
+            prepare(units[i + PICKS])
+            if i == 0:
                 copy_first(blocks[0])
                 copy_first(blocks[1])
-            prepare(units[i + 2])
-        multiply(units[4])
-        multiply(units[5])
+        for u in units[PICKS:]:
+            multiply(u)
         copy_first(blocks[2])
         copy_first(blocks[3])
 
-        pair0 = keep.tile([P, 2, 2, HALF], F32, name="pair0", tag="late")
-        for b in blocks[:2]:
-            pair[b] = pair0[:, b[1]]
+        pair[blocks[0]] = high[units[4]]
+        pair[blocks[1]] = high[units[5]]
         early = keep.tile([P, 2, 2, HALF], F32, name="early", tag="reused", align_bytes=64)
         for b in blocks[:2]:
             times_second(b)
-        for b in blocks[:2]:
             times_third(b)
             result[b] = early[:, b[1]]
             finish(nc.gpsimd, nc.sync, b, slice(0, 2))

@@ -26,7 +26,9 @@ N_TILES = N // P
 RUN = 4
 BANKS = 8
 QUADRANT = 32
-WGT_CUTS = (0, 128, 256, 512)
+CHUNKS = PICKS * J // P
+SHARE = 8
+SPREAD_FROM, SPREAD_TO = 3 * P, 11 * P
 
 
 def tile_list_dl_prod_res_kernel(tc, xT, wgt, w4_words, w4_scales, wd, res, offs, out):
@@ -48,7 +50,9 @@ def tile_list_dl_prod_res_kernel(tc, xT, wgt, w4_words, w4_scales, wd, res, offs
         x_rows = xT.rearrange("(p t) w -> t p w", t=PACK)
         wd_rows = wd.rearrange("(p t) n -> p t n", t=PACK)
         out_rows = out.rearrange("(a p) j -> p a j", p=P)
-        wgt_pieces = [slice(0, P), slice(P, 3 * P), slice(11 * P, 12 * P)]
+        wgt_pieces = [slice(0, P), slice(P, SPREAD_FROM), slice(SPREAD_TO, PICKS * J)]
+        thin_rows = wgt.rearrange("(u a) (c w) -> u (a c) w", a=SHARE, w=P)
+        thin_rows = thin_rows[:, CHUNKS - 2 : SHARE * (CHUNKS - 1) : CHUNKS - 1, :]
 
         nc.vector.memset(w4_scale[:].bitcast(U32), 0)
         thin = keep.tile([P, P], F32, name="thin")
@@ -58,13 +62,7 @@ def tile_list_dl_prod_res_kernel(tc, xT, wgt, w4_words, w4_scales, wd, res, offs
         identity = keep.tile([P, P], F32, name="identity")
         make_identity(nc, identity[:])
 
-        def load_scales(q):
-            nc.sync.dma_start(
-                out=w4_scale[QUADRANT * q : QUADRANT * q + 4, :].bitcast(I32),
-                in_=w4_scales[0, 4 * q : 4 * q + 4, :].bitcast(I32),
-            )
-
-        nc.sync.dma_start(out=thin[:], in_=wgt.rearrange("(u a) (c w) -> u (a c) w", a=8, w=P)[:, 10:88:11, :])
+        nc.sync.dma_start(out=thin[:], in_=thin_rows)
         nc.sync.dma_start(out=planes[0][:], in_=x_rows[0])
         nc.sync.dma_start(offsets[:], offs)
         nc.scalar.dma_start(out=weights[:, wgt_pieces[0]], in_=wgt[:, wgt_pieces[0]])
@@ -76,23 +74,27 @@ def tile_list_dl_prod_res_kernel(tc, xT, wgt, w4_words, w4_scales, wd, res, offs
         nc.sync.dma_start(out=wd_raw[1][:], in_=wd_rows[:, :, HALF:N])
         nc.sync.dma_start(out=planes[3][:], in_=x_rows[3])
         for q in range(P // QUADRANT):
-            load_scales(q)
+            nc.sync.dma_start(
+                out=w4_scale[QUADRANT * q : QUADRANT * q + 4, :].bitcast(I32),
+                in_=w4_scales[0, 4 * q : 4 * q + 4, :].bitcast(I32),
+            )
         nc.sync.dma_start(out=w4_codes[:].bitcast(I32), in_=w4_words[0].bitcast(I32))
         nc.sync.dma_start(out=residual[:], in_=res.rearrange("(a p) j -> p a j", p=P))
 
         units = [(h, c) for h in (1, 0) for c in range(PICKS)]
         last = units[-1]
+
+        batches = (slice(1, 3), slice(0, 4, 3))
         turned = psum.tile([P, P], F32, name="acc")
         nc.tensor.transpose(turned[:], thin[:], identity[:])
-        batches = (slice(1, 3), slice(0, 4, 3))
+        by_row = turned[:].rearrange("p (u a b) -> p a b u", a=2, b=4)
         for e in range(2):
-            nc.scalar.copy(
-                out=spread[e][:].rearrange("p a b (u r) -> p a b u r", r=8),
-                in_=turned[:].rearrange("p (u a b) -> p a b u", a=2, b=4)[:, :, batches[e], :]
-                .unsqueeze(4)
-                .to_broadcast([P, 2, 2, 16, 8]),
-            )
-        quads = weights[:, 3 * P : 11 * P].rearrange("p (a b w) -> p a b w", a=2, w=P)
+            for a in (1, 0):
+                nc.scalar.copy(
+                    out=spread[e][:, a].rearrange("p b (u r) -> p b u r", r=SHARE),
+                    in_=by_row[:, a, batches[e], :].unsqueeze(3).to_broadcast([P, 2, P // SHARE, SHARE]),
+                )
+        quads = weights[:, SPREAD_FROM:SPREAD_TO].rearrange("p (a b w) -> p a b w", a=2, w=P)
         for e in range(2):
             back = psum.tile([P, 2, 2, P], F32, name="acc")
             for a in range(2):
@@ -107,11 +109,20 @@ def tile_list_dl_prod_res_kernel(tc, xT, wgt, w4_words, w4_scales, wd, res, offs
         highs = [picked[0][:, 4:7:2, :]] + [keep.tile([P, 2, HALF], F32, name="high%d" % c)[:] for c in (1, 2)]
         low = {(h, c): picked[c][:, h : h + 3 : 2, :] for (h, c) in units}
         high = {(h, c): highs[c] for (h, c) in units}
-        whole = units[PICKS : PICKS + 1]
+        whole = units[PICKS]
         rounded = {u: keep.tile([P, HALF * PACK], BF16, name="rounded%d%d" % u, align_bytes=64) for u in units[:-1]}
         rounded[last] = keep.tile([P, HALF * PACK], BF16, name="rounded_last", tag="reused", align_bytes=64)
-        x_codes = {u: keep.tile([P, HALF], U32, name="x_codes%d%d" % u, align_bytes=64) for u in units}
-        x_scale = {u: keep.tile([P, HALF], U8, name="x_scale%d%d" % u, align_bytes=64) for u in units}
+        widths = (HALF, J)
+        x_codes = {
+            (h, g): keep.tile([P, widths[g]], U32, name="x_codes%d%d" % (h, g), align_bytes=64)
+            for h in range(2)
+            for g in range(2)
+        }
+        x_scale = {
+            (h, g): keep.tile([P, widths[g]], U8, name="x_scale%d%d" % (h, g), align_bytes=64)
+            for h in range(2)
+            for g in range(2)
+        }
         blocks = [(h, r) for h in (1, 0) for r in range(2)]
         first = {b: keep.tile([P, 2, HALF], F32, name="first%d%d" % b) for b in blocks}
         pair = {b: keep.tile([P, 2, HALF], F32, name="pair%d%d" % b)[:] for b in blocks[2:]}
@@ -142,36 +153,47 @@ def tile_list_dl_prod_res_kernel(tc, xT, wgt, w4_words, w4_scales, wd, res, offs
                 in_=(low, high)[e][u].rearrange("p t j -> p j t"),
             )
 
-        def project(u, r):
-            if u == last:
-                acc = [psum.tile([P, HALF], F32, name="acc")[:] for i in range(2)]
-                sums[u, r] = acc
-            else:
-                bank = psum.tile([P, 2, HALF], F32, name="acc")
-                sums[u, r] = bank
-                acc = [bank[:, i, :] for i in range(2)]
-            for i in range(2):
-                a = 2 * r + i
-                nc.tensor.matmul_mx(
-                    out=acc[i],
-                    lhsT=wd_codes[r][:, P * i : P * (i + 1)].bitcast(FP8X4),
-                    lhsT_scale=wd_scale[r][:, P * i : P * (i + 1)],
-                    rhs=x_codes[u][:].bitcast(FP8X4),
-                    rhs_scale=x_scale[u][:],
-                    start=True,
-                    stop=False,
-                )
-                for j0 in range(0, HALF, W4_COLS):
-                    cols = slice(j0, j0 + W4_COLS)
-                    nc.tensor.matmul_mx(
-                        out=acc[i][:, cols],
-                        lhsT=w4_codes[:, 2 * P * a : 2 * P * (a + 1)].bitcast(FP4X4),
-                        lhsT_scale=w4_scale[:, P * a : P * (a + 1)],
-                        rhs=x_codes[u][:, cols].bitcast(FP8X4),
-                        rhs_scale=x_scale[u][:, cols],
-                        start=False,
-                        stop=(j0 + W4_COLS == HALF),
-                    )
+        def pass_wd(acc, a, key, cols, opens):
+            w_cols = slice(P * (a % 2), P * (a % 2 + 1))
+            nc.tensor.matmul_mx(
+                out=acc,
+                lhsT=wd_codes[a // 2][:, w_cols].bitcast(FP8X4),
+                lhsT_scale=wd_scale[a // 2][:, w_cols],
+                rhs=x_codes[key][:, cols].bitcast(FP8X4),
+                rhs_scale=x_scale[key][:, cols],
+                start=opens,
+                stop=False,
+            )
+
+        def pass_w4(acc, a, key, cols, closes):
+            nc.tensor.matmul_mx(
+                out=acc,
+                lhsT=w4_codes[:, 2 * P * a : 2 * P * (a + 1)].bitcast(FP4X4),
+                lhsT_scale=w4_scale[:, P * a : P * (a + 1)],
+                rhs=x_codes[key][:, cols].bitcast(FP8X4),
+                rhs_scale=x_scale[key][:, cols],
+                start=False,
+                stop=closes,
+            )
+
+        def project_first(h):
+            for r in range(2):
+                sums[h, 0, r] = psum.tile([P, 2, HALF], F32, name="acc")
+                for i in range(2):
+                    pass_wd(sums[h, 0, r][:, i, :], 2 * r + i, (h, 0), half(0), True)
+                    for j0 in range(0, HALF, W4_COLS):
+                        cols = slice(j0, j0 + W4_COLS)
+                        pass_w4(sums[h, 0, r][:, i, cols], 2 * r + i, (h, 0), cols, j0 + W4_COLS == HALF)
+
+        def project_second(h, tiles):
+            for a in tiles:
+                sums[h, 1, a] = psum.tile([P, J], F32, name="acc")
+                pass_wd(sums[h, 1, a][:, half(0)], a, (h, 1), half(0), True)
+
+        def project_third(h, tiles):
+            for a in tiles:
+                pass_wd(sums[h, 1, a][:, half(1)], a, (h, 1), half(1), False)
+                pass_w4(sums[h, 1, a][:], a, (h, 1), slice(0, J), True)
 
         def gather_pick(t, c):
             gather(picked[c][:, 2 * t : 2 * t + 2, :].rearrange("p s j -> p (s j)"), t, c * J, (c + 1) * J)
@@ -187,27 +209,32 @@ def tile_list_dl_prod_res_kernel(tc, xT, wgt, w4_words, w4_scales, wd, res, offs
             if u in units[PICKS:]:
                 gather_unit(2, u)
             gather_unit(3, u)
-            if u in whole:
+            if u == whole:
                 interleave_whole(u)
             else:
                 interleave_pair(u, 1)
 
-        def multiply(u):
-            nc.vector.quantize_mx(out=x_codes[u][:].bitcast(FP8X4), scales=x_scale[u][:], in_=rounded[u][:])
-            project(u, 0)
-            project(u, 1)
+        def quantize(u):
+            h, c = u
+            key, cols = (h, min(c, 1)), half(c // 2)
+            nc.vector.quantize_mx(
+                out=x_codes[key][:, cols].bitcast(FP8X4), scales=x_scale[key][:, cols], in_=rounded[u][:]
+            )
 
         def copy_first(b):
-            nc.scalar.copy(out=first[b][:], in_=sums[(b[0], 0), b[1]][:])
+            nc.scalar.copy(out=first[b][:], in_=sums[b[0], 0, b[1]][:])
 
         def times_second(b):
-            nc.vector.tensor_tensor(pair[b], sums[(b[0], 1), b[1]][:], first[b][:], MULT)
+            for i in range(2):
+                nc.vector.tensor_tensor(
+                    pair[b][:, i, :], sums[b[0], 1, 2 * b[1] + i][:, half(0)], first[b][:, i, :], MULT
+                )
 
         def times_third(b):
-            nc.vector.tensor_tensor(triple[b][:], sums[(b[0], 2), b[1]][:], pair[b], MULT)
-
-        def times_third_last(b, i):
-            nc.vector.tensor_tensor(triple[b][:, i, :], sums[last, b[1]][i], pair[b][:, i, :], MULT)
+            for i in range(2):
+                nc.vector.tensor_tensor(
+                    triple[b][:, i, :], sums[b[0], 1, 2 * b[1] + i][:, half(1)], pair[b][:, i, :], MULT
+                )
 
         def finish(engine, queue, b, tiles):
             h, r = b
@@ -215,16 +242,18 @@ def tile_list_dl_prod_res_kernel(tc, xT, wgt, w4_words, w4_scales, wd, res, offs
             engine.tensor_tensor(result[b][:, tiles, :], triple[b][:, tiles, :], residual[:, rows, half(h)], ADD)
             queue.dma_start(out=out_rows[:, rows, half(h)], in_=result[b][:, tiles, :])
 
-
         def round_wd(h, room):
             wd_rounded = keep.tile([P, HALF * PACK], BF16, name="wd_rounded%d" % h, tag=room, align_bytes=64)
             interleave(wd_rounded[:], wd_raw[h][:])
             nc.vector.quantize_mx(out=wd_codes[h][:].bitcast(FP8X4), scales=wd_scale[h][:], in_=wd_rounded[:])
 
         round_wd(0, "spread1")
-        for m0, m1 in ((0, P), (P, 3 * P), (11 * P, 12 * P), (3 * P, J), (J, 2 * J), (2 * J, 11 * P)):
-            c = m0 // J
+
+        spread_pieces = [slice(max(c * J, SPREAD_FROM), min((c + 1) * J, SPREAD_TO)) for c in range(PICKS)]
+        for piece in wgt_pieces + spread_pieces:
+            m0, m1, c = piece.start, piece.stop, piece.start // J
             gather(picked[c][:, 0:2, :].rearrange("p s j -> p (s j)")[:, m0 - c * J : m1 - c * J], 0, m0, m1)
+
         for c in (1, 2, 0):
             gather_pick(1, c)
         for u in ((1, 1), (0, 1), (1, 2)):
@@ -237,14 +266,24 @@ def tile_list_dl_prod_res_kernel(tc, xT, wgt, w4_words, w4_scales, wd, res, offs
 
         for u in units[:PICKS]:
             prepare(u)
-        for i in range(PICKS):
-            multiply(units[i])
-            prepare(units[i + PICKS])
-            if i == 0:
-                copy_first(blocks[0])
-                copy_first(blocks[1])
-        for u in units[PICKS:]:
-            multiply(u)
+
+        quantize(units[0])
+        project_first(1)
+        prepare(units[3])
+        copy_first(blocks[0])
+        copy_first(blocks[1])
+        quantize(units[1])
+        project_second(1, range(N_TILES))
+        prepare(units[4])
+        quantize(units[2])
+        project_third(1, range(N_TILES))
+        prepare(units[5])
+        quantize(units[3])
+        project_first(0)
+        quantize(units[4])
+        project_second(0, range(2))
+        quantize(units[5])
+        project_third(0, range(2))
         copy_first(blocks[2])
         copy_first(blocks[3])
 
@@ -257,12 +296,13 @@ def tile_list_dl_prod_res_kernel(tc, xT, wgt, w4_words, w4_scales, wd, res, offs
             result[b] = early[:, b[1]]
             finish(nc.gpsimd, nc.sync, b, slice(0, 2))
 
+        for a in (2, 3):
+            project_second(0, [a])
+            project_third(0, [a])
         for b in blocks[2:]:
             times_second(b)
-        for b in blocks[2:]:
-            for i in range(2):
-                times_third_last(b, i)
-        finish(nc.gpsimd, nc.sync, blocks[2], slice(0, 1))
+            times_third(b)
         finish(nc.vector, nc.sync, blocks[2], slice(1, 2))
-        finish(nc.vector, nc.scalar, blocks[3], slice(0, 1))
-        finish(nc.vector, nc.sync, blocks[3], slice(1, 2))
+        finish(nc.gpsimd, nc.scalar, blocks[2], slice(0, 1))
+        finish(nc.vector, nc.sync, blocks[3], slice(0, 1))
+        finish(nc.vector, nc.scalar, blocks[3], slice(1, 2))

@@ -26,9 +26,9 @@ N_TILES = N // P
 RUN = 4
 BANKS = 8
 QUADRANT = 32
-CHUNKS = PICKS * J // P
+ENTRIES = PICKS * J
+CHUNKS = ENTRIES // P
 SHARE = 8
-SPREAD_FROM, SPREAD_TO = 3 * P, 11 * P
 
 
 def tile_list_dl_prod_res_kernel(tc, xT, wgt, w4_words, w4_scales, wd, res, offs, out):
@@ -37,12 +37,17 @@ def tile_list_dl_prod_res_kernel(tc, xT, wgt, w4_words, w4_scales, wd, res, offs
         keep = ctx.enter_context(tc.tile_pool(name="keep", bufs=1))
         psum = ctx.enter_context(tc.psum_pool(name="psum", bufs=BANKS))
 
-        offsets = keep.tile([P, PICKS * J // GROUP], U16, name="offsets")
+        offsets = keep.tile([P, ENTRIES // GROUP], U16, name="offsets")
         planes = [keep.tile([P, T], F32, name="plane%d" % t) for t in range(PACK)]
-        weights = keep.tile([P, PICKS * J], F32, name="weights")
+        weights = keep.tile([P, ENTRIES], F32, name="weights", tag="weights")
         w4_codes = keep.tile([P, 2 * N], U8, name="w4_codes", align_bytes=64)
         w4_scale = keep.tile([P, N], U8, name="w4_scale", align_bytes=64)
-        wd_raw = [keep.tile([P, PACK, HALF], F32, name="wd_raw%d" % h) for h in range(2)]
+        room = keep.tile([P, 36 * HALF], F32, name="room")
+        slots = room[:].rearrange("p (s j) -> p s j", j=HALF)
+        wd_raw = [
+            slots[:, 12:34:7, :],
+            keep.tile([P, PACK, HALF], F32, name="wd_raw1", tag="wd_raw1", align_bytes=64)[:],
+        ]
         wd_codes = [keep.tile([P, HALF], U32, name="wd_codes%d" % h, align_bytes=64) for h in range(2)]
         wd_scale = [keep.tile([P, HALF], U8, name="wd_scale%d" % h, align_bytes=64) for h in range(2)]
         residual = keep.tile([P, N_TILES, J], F32, name="residual")
@@ -50,28 +55,23 @@ def tile_list_dl_prod_res_kernel(tc, xT, wgt, w4_words, w4_scales, wd, res, offs
         x_rows = xT.rearrange("(p t) w -> t p w", t=PACK)
         wd_rows = wd.rearrange("(p t) n -> p t n", t=PACK)
         out_rows = out.rearrange("(a p) j -> p a j", p=P)
-        wgt_pieces = [slice(0, P), slice(P, SPREAD_FROM), slice(SPREAD_TO, PICKS * J)]
-        thin_rows = wgt.rearrange("(u a) (c w) -> u (a c) w", a=SHARE, w=P)
-        thin_rows = thin_rows[:, CHUNKS - 2 : SHARE * (CHUNKS - 1) : CHUNKS - 1, :]
+
+        thin_rows = wgt.rearrange("(u a) (c w) -> u (a c) w", a=SHARE, w=P)[:, CHUNKS - SHARE :: CHUNKS + 1, :]
 
         nc.vector.memset(w4_scale[:].bitcast(U32), 0)
         thin = keep.tile([P, P], F32, name="thin")
-        spread = [
-            keep.tile([P, 2, 2, P], F32, name="spread%d" % e, tag="spread%d" % e, align_bytes=64) for e in range(2)
-        ]
         identity = keep.tile([P, P], F32, name="identity")
         make_identity(nc, identity[:])
 
         nc.sync.dma_start(out=thin[:], in_=thin_rows)
+        nc.scalar.dma_start(out=weights[:, 0:P], in_=wgt[:, 0:P])
         nc.sync.dma_start(out=planes[0][:], in_=x_rows[0])
         nc.sync.dma_start(offsets[:], offs)
-        nc.scalar.dma_start(out=weights[:, wgt_pieces[0]], in_=wgt[:, wgt_pieces[0]])
-        for piece in wgt_pieces[1:]:
-            nc.sync.dma_start(out=weights[:, piece], in_=wgt[:, piece])
-        nc.sync.dma_start(out=wd_raw[0][:], in_=wd_rows[:, :, 0:HALF])
+        nc.sync.dma_start(out=weights[:, P:J], in_=wgt[:, P:J])
         nc.sync.dma_start(out=planes[1][:], in_=x_rows[1])
+        nc.sync.dma_start(out=wd_raw[0], in_=wd_rows[:, :, 0:HALF])
+        nc.sync.dma_start(out=wd_raw[1], in_=wd_rows[:, :, HALF:N])
         nc.sync.dma_start(out=planes[2][:], in_=x_rows[2])
-        nc.sync.dma_start(out=wd_raw[1][:], in_=wd_rows[:, :, HALF:N])
         nc.sync.dma_start(out=planes[3][:], in_=x_rows[3])
         for q in range(P // QUADRANT):
             nc.sync.dma_start(
@@ -82,36 +82,32 @@ def tile_list_dl_prod_res_kernel(tc, xT, wgt, w4_words, w4_scales, wd, res, offs
         nc.sync.dma_start(out=residual[:], in_=res.rearrange("(a p) j -> p a j", p=P))
 
         units = [(h, c) for h in (1, 0) for c in range(PICKS)]
-        last = units[-1]
 
-        batches = (slice(1, 3), slice(0, 4, 3))
         turned = psum.tile([P, P], F32, name="acc")
         nc.tensor.transpose(turned[:], thin[:], identity[:])
-        by_row = turned[:].rearrange("p (u a b) -> p a b u", a=2, b=4)
-        for e in range(2):
-            for a in (1, 0):
-                nc.scalar.copy(
-                    out=spread[e][:, a].rearrange("p b (u r) -> p b u r", r=SHARE),
-                    in_=by_row[:, a, batches[e], :].unsqueeze(3).to_broadcast([P, 2, P // SHARE, SHARE]),
-                )
-        quads = weights[:, SPREAD_FROM:SPREAD_TO].rearrange("p (a b w) -> p a b w", a=2, w=P)
-        for e in range(2):
-            back = psum.tile([P, 2, 2, P], F32, name="acc")
-            for a in range(2):
-                for b in range(2):
-                    nc.tensor.transpose(back[:, a, b, :], spread[e][:, 1 - a, 1 - b, :], identity[:])
-            nc.scalar.copy(out=quads[:, :, batches[e], :], in_=back[:])
+        by_chunk = turned[:].rearrange("p (u i) -> p i u", i=SHARE)
+        spread = [
+            keep.tile([P, 2, P], F32, name="spread%d" % e, tag="spread%d" % e, align_bytes=64)[:] for e in range(2)
+        ] + [slots[:, s, :].rearrange("p (i w) -> p i w", w=P) for s in range(2)]
+        for e in (2, 3, 0, 1):
+            nc.vector.tensor_copy(
+                out=spread[e].rearrange("p i (u r) -> p i u r", r=SHARE),
+                in_=by_chunk[:, 2 * e : 2 * e + 2, :].unsqueeze(3).to_broadcast([P, 2, P // SHARE, SHARE]),
+            )
+        for c in (2, 1):
+            back = psum.tile([P, 4, P], F32, name="acc")
+            for i in range(4):
+                nc.tensor.transpose(back[:, i, :], spread[2 * c - 2 + i // 2][:, i % 2, :], identity[:])
+            nc.scalar.copy(out=weights[:, c * J : (c + 1) * J], in_=back[:].rearrange("p i w -> p (i w)"))
 
-        picked = [
-            keep.tile([P, 4 if c else 7, HALF], F32, name="picked%d" % c, tag="picked%d" % c, align_bytes=64)
-            for c in range(PICKS)
-        ]
-        highs = [picked[0][:, 4:7:2, :]] + [keep.tile([P, 2, HALF], F32, name="high%d" % c)[:] for c in (1, 2)]
-        low = {(h, c): picked[c][:, h : h + 3 : 2, :] for (h, c) in units}
-        high = {(h, c): highs[c] for (h, c) in units}
-        whole = units[PICKS]
-        rounded = {u: keep.tile([P, HALF * PACK], BF16, name="rounded%d%d" % u, align_bytes=64) for u in units[:-1]}
-        rounded[last] = keep.tile([P, HALF * PACK], BF16, name="rounded_last", tag="reused", align_bytes=64)
+        def entry0(u):
+            return u[1] * J + u[0] * HALF
+
+        high = {u: (slots[:, 12:19:6, :], slots[:, 19:26:6, :], slots[:, 26:28, :])[u[1]] for u in units}
+        low = {}
+        for u in units:
+            s = entry0(u) // HALF
+            low[u] = slots[:, s : s + 7 : 6, :]
         widths = (HALF, J)
         x_codes = {
             (h, g): keep.tile([P, widths[g]], U32, name="x_codes%d%d" % (h, g), align_bytes=64)
@@ -125,9 +121,9 @@ def tile_list_dl_prod_res_kernel(tc, xT, wgt, w4_words, w4_scales, wd, res, offs
         }
         blocks = [(h, r) for h in (1, 0) for r in range(2)]
         first = {b: keep.tile([P, 2, HALF], F32, name="first%d%d" % b) for b in blocks}
-        pair = {b: keep.tile([P, 2, HALF], F32, name="pair%d%d" % b)[:] for b in blocks[2:]}
+        pair = {b: keep.tile([P, 2, HALF], F32, name="pair%d%d" % b)[:] for b in blocks[1:]}
         triple = {b: keep.tile([P, 2, HALF], F32, name="triple%d%d" % b) for b in blocks}
-        result = {b: keep.tile([P, 2, HALF], F32, name="result%d%d" % b) for b in blocks[2:]}
+        result = {blocks[3]: keep.tile([P, 2, HALF], F32, name="result")}
         sums = {}
 
         def half(h):
@@ -137,19 +133,36 @@ def tile_list_dl_prod_res_kernel(tc, xT, wgt, w4_words, w4_scales, wd, res, offs
             window = planes[t][:].indirect(offsets[:, m0 // GROUP : m1 // GROUP])
             nc.vector.tensor_tensor(dst, window, weights[:, m0:m1], MULT)
 
-        def gather_unit(t, u):
-            m0 = u[1] * J + u[0] * HALF
-            gather((low, high)[t // 2][u][:, t % 2, :], t, m0, m0 + HALF)
+        def gather_low(t, m0, m1):
+            gather(room[:, t * ENTRIES + m0 : t * ENTRIES + m1], t, m0, m1)
 
-        def interleave(dst, src):
+        def gather_unit(t, u):
+            gather(high[u][:, t % 2, :], t, entry0(u), entry0(u) + HALF)
+
+        wd_both = keep.tile([P, N * PACK], BF16, name="wd_both", tag="spread1", align_bytes=64)
+
+        def round_wd(h):
+            wd_rounded = wd_both[:, h * HALF * PACK : (h + 1) * HALF * PACK]
             nc.scalar.copy(
-                out=dst.rearrange("p (g i t) -> p g t i", i=RUN, t=PACK),
-                in_=src.rearrange("p t (g i) -> p g t i", i=RUN),
+                out=wd_rounded.rearrange("p (g i t) -> p g t i", i=RUN, t=PACK),
+                in_=wd_raw[h].rearrange("p t (g i) -> p g t i", i=RUN),
             )
+            nc.vector.quantize_mx(out=wd_codes[h][:].bitcast(FP8X4), scales=wd_scale[h][:], in_=wd_rounded)
+
+        gather_low(0, 0, P)
+        gather_low(0, P, J)
+        gather_low(0, J, ENTRIES)
+        gather_low(1, 0, ENTRIES // 2)
+        gather_low(1, ENTRIES // 2, ENTRIES)
+        round_wd(0)
+        round_wd(1)
+
+        rounded_all = keep.tile([P, len(units) * HALF * PACK], BF16, name="rounded", tag="wd_raw1", align_bytes=64)
+        rounded = {u: rounded_all[:, i * HALF * PACK : (i + 1) * HALF * PACK] for i, u in enumerate(units)}
 
         def interleave_pair(u, e):
             nc.scalar.copy(
-                out=rounded[u][:].rearrange("p (j t) -> p j t", t=PACK)[:, :, 2 * e : 2 * e + 2],
+                out=rounded[u].rearrange("p (j t) -> p j t", t=PACK)[:, :, 2 * e : 2 * e + 2],
                 in_=(low, high)[e][u].rearrange("p t j -> p j t"),
             )
 
@@ -195,30 +208,11 @@ def tile_list_dl_prod_res_kernel(tc, xT, wgt, w4_words, w4_scales, wd, res, offs
                 pass_wd(sums[h, 1, a][:, half(1)], a, (h, 1), half(1), False)
                 pass_w4(sums[h, 1, a][:], a, (h, 1), slice(0, J), True)
 
-        def gather_pick(t, c):
-            gather(picked[c][:, 2 * t : 2 * t + 2, :].rearrange("p s j -> p (s j)"), t, c * J, (c + 1) * J)
-
-        def interleave_whole(u):
-            slots = picked[u[1]][:, 0:7:2, :].rearrange("p (e s) (g i) -> p g e s i", s=2, i=RUN)
-            nc.scalar.copy(
-                out=rounded[u][:].rearrange("p (g i e s) -> p g e s i", i=RUN, e=2, s=2),
-                in_=slots,
-            )
-
-        def prepare(u):
-            if u in units[PICKS:]:
-                gather_unit(2, u)
-            gather_unit(3, u)
-            if u == whole:
-                interleave_whole(u)
-            else:
-                interleave_pair(u, 1)
-
         def quantize(u):
             h, c = u
             key, cols = (h, min(c, 1)), half(c // 2)
             nc.vector.quantize_mx(
-                out=x_codes[key][:, cols].bitcast(FP8X4), scales=x_scale[key][:, cols], in_=rounded[u][:]
+                out=x_codes[key][:, cols].bitcast(FP8X4), scales=x_scale[key][:, cols], in_=rounded[u]
             )
 
         def copy_first(b):
@@ -242,67 +236,66 @@ def tile_list_dl_prod_res_kernel(tc, xT, wgt, w4_words, w4_scales, wd, res, offs
             engine.tensor_tensor(result[b][:, tiles, :], triple[b][:, tiles, :], residual[:, rows, half(h)], ADD)
             queue.dma_start(out=out_rows[:, rows, half(h)], in_=result[b][:, tiles, :])
 
-        def round_wd(h, room):
-            wd_rounded = keep.tile([P, HALF * PACK], BF16, name="wd_rounded%d" % h, tag=room, align_bytes=64)
-            interleave(wd_rounded[:], wd_raw[h][:])
-            nc.vector.quantize_mx(out=wd_codes[h][:].bitcast(FP8X4), scales=wd_scale[h][:], in_=wd_rounded[:])
-
-        round_wd(0, "spread1")
-
-        spread_pieces = [slice(max(c * J, SPREAD_FROM), min((c + 1) * J, SPREAD_TO)) for c in range(PICKS)]
-        for piece in wgt_pieces + spread_pieces:
-            m0, m1, c = piece.start, piece.stop, piece.start // J
-            gather(picked[c][:, 0:2, :].rearrange("p s j -> p (s j)")[:, m0 - c * J : m1 - c * J], 0, m0, m1)
-
-        for c in (1, 2, 0):
-            gather_pick(1, c)
-        for u in ((1, 1), (0, 1), (1, 2)):
-            interleave_pair(u, 0)
+        for i in (0, 1, 2, 5):
+            interleave_pair(units[i], 0)
         for u in units[:PICKS]:
             gather_unit(2, u)
-        round_wd(1, "picked1")
-        for u in ((0, 2), (1, 0)):
-            interleave_pair(u, 0)
-
         for u in units[:PICKS]:
-            prepare(u)
+            gather_unit(3, u)
+            interleave_pair(u, 1)
 
         quantize(units[0])
         project_first(1)
-        prepare(units[3])
-        copy_first(blocks[0])
-        copy_first(blocks[1])
+        gather_unit(2, units[3])
+        gather_unit(3, units[3])
+        nc.scalar.copy(
+            out=rounded[units[3]].rearrange("p (g i t) -> p g t i", i=RUN, t=PACK),
+            in_=slots[:, 0:19:6, :].rearrange("p t (g i) -> p g t i", i=RUN),
+        )
         quantize(units[1])
         project_second(1, range(N_TILES))
-        prepare(units[4])
+        gather_unit(2, units[4])
+        gather_unit(3, units[4])
         quantize(units[2])
         project_third(1, range(N_TILES))
-        prepare(units[5])
+        gather_unit(2, units[5])
+        gather_unit(3, units[5])
+        copy_first(blocks[0])
+        four = slots[:, 2:36, :].rearrange("p (e s) j -> p e s j", e=2)[:, :, 0:7:6, :]
+        nc.scalar.copy(
+            out=rounded[units[4]].rearrange("p (g i e s) -> p g e s i", i=RUN, e=2, s=2),
+            in_=four.rearrange("p e s (g i) -> p g e s i", i=RUN),
+        )
+        interleave_pair(units[5], 1)
         quantize(units[3])
         project_first(0)
         quantize(units[4])
-        project_second(0, range(2))
+        project_second(0, [0])
         quantize(units[5])
-        project_third(0, range(2))
+        copy_first(blocks[1])
         copy_first(blocks[2])
         copy_first(blocks[3])
 
-        pair[blocks[0]] = high[units[4]]
-        pair[blocks[1]] = high[units[5]]
-        early = keep.tile([P, 2, 2, HALF], F32, name="early", tag="reused", align_bytes=64)
-        for b in blocks[:2]:
+        early = keep.tile([P, 3, 2, HALF], F32, name="early", tag="wd_raw1", align_bytes=64)
+        for i in range(3):
+            result[blocks[i]] = early[:, i]
+        pair[blocks[0]] = keep.tile([P, 2, HALF], F32, name="pair_first", tag="weights")[:]
+        triple[blocks[0]] = slots[:, 24:27:2, :]
+        times_second(blocks[0])
+        times_third(blocks[0])
+        project_second(0, [1])
+        project_third(0, range(2))
+        project_second(0, range(2, N_TILES))
+        project_third(0, range(2, N_TILES))
+        finish(nc.gpsimd, nc.sync, blocks[0], slice(0, 1))
+        finish(nc.gpsimd, nc.sync, blocks[0], slice(1, 2))
+        for b in blocks[1:3]:
             times_second(b)
             times_third(b)
-            result[b] = early[:, b[1]]
-            finish(nc.gpsimd, nc.sync, b, slice(0, 2))
-
-        for a in (2, 3):
-            project_second(0, [a])
-            project_third(0, [a])
-        for b in blocks[2:]:
-            times_second(b)
-            times_third(b)
-        finish(nc.vector, nc.sync, blocks[2], slice(1, 2))
-        finish(nc.gpsimd, nc.scalar, blocks[2], slice(0, 1))
+        finish(nc.gpsimd, nc.sync, blocks[1], slice(0, 2))
+        finish(nc.gpsimd, nc.sync, blocks[2], slice(0, 1))
+        times_second(blocks[3])
+        times_third(blocks[3])
+        finish(nc.vector, nc.scalar, blocks[2], slice(1, 2))
         finish(nc.vector, nc.sync, blocks[3], slice(0, 1))
         finish(nc.vector, nc.scalar, blocks[3], slice(1, 2))

@@ -59,22 +59,21 @@ def tile_list_dl_prod_res_kernel(tc, xT, wgt, w4_words, w4_scales, wd, res, offs
         thin_rows = wgt.rearrange("(u a) (c w) -> u (a c) w", a=SHARE, w=P)[:, CHUNKS - SHARE :: CHUNKS + 1, :]
 
         nc.vector.memset(w4_scale[:].bitcast(U32), 0)
-        thin = keep.tile([P, P], F32, name="thin")
+        thin = keep.tile([P, P], F32, name="thin", tag="thin", align_bytes=64)
         identity = keep.tile([P, P], F32, name="identity")
         make_identity(nc, identity[:])
 
         nc.sync.dma_start(out=thin[:], in_=thin_rows)
-        nc.scalar.dma_start(out=weights[:, 0:P], in_=wgt[:, 0:P])
         nc.sync.dma_start(out=planes[0][:], in_=x_rows[0])
         nc.sync.dma_start(offsets[:], offs)
-        nc.sync.dma_start(out=weights[:, P:J], in_=wgt[:, P:J])
+        nc.sync.dma_start(out=weights[:, 0:J], in_=wgt[:, 0:J])
         nc.sync.dma_start(out=planes[1][:], in_=x_rows[1])
         nc.sync.dma_start(out=wd_raw[0], in_=wd_rows[:, :, 0:HALF])
         nc.sync.dma_start(out=wd_raw[1], in_=wd_rows[:, :, HALF:N])
         nc.sync.dma_start(out=planes[2][:], in_=x_rows[2])
         nc.sync.dma_start(out=planes[3][:], in_=x_rows[3])
         for q in range(P // QUADRANT):
-            nc.sync.dma_start(
+            (nc.sync if q else nc.scalar).dma_start(
                 out=w4_scale[QUADRANT * q : QUADRANT * q + 4, :].bitcast(I32),
                 in_=w4_scales[0, 4 * q : 4 * q + 4, :].bitcast(I32),
             )
@@ -86,19 +85,20 @@ def tile_list_dl_prod_res_kernel(tc, xT, wgt, w4_words, w4_scales, wd, res, offs
         turned = psum.tile([P, P], F32, name="acc")
         nc.tensor.transpose(turned[:], thin[:], identity[:])
         by_chunk = turned[:].rearrange("p (u i) -> p i u", i=SHARE)
-        spread = [
-            keep.tile([P, 2, P], F32, name="spread%d" % e, tag="spread%d" % e, align_bytes=64)[:] for e in range(2)
-        ] + [slots[:, s, :].rearrange("p (i w) -> p i w", w=P) for s in range(2)]
-        for e in (2, 3, 0, 1):
-            nc.vector.tensor_copy(
+        spread = [slots[:, 0, :].rearrange("p (i w) -> p i w", w=P)] + [
+            keep.tile([P, 2, P], F32, name="spread%d" % e, tag="spread%d" % e, align_bytes=64)[:] for e in (1, 2, 3)
+        ]
+        for e in (3, 2, 0, 1):
+            (nc.scalar.copy, nc.vector.tensor_copy)[e // 2](
                 out=spread[e].rearrange("p i (u r) -> p i u r", r=SHARE),
                 in_=by_chunk[:, 2 * e : 2 * e + 2, :].unsqueeze(3).to_broadcast([P, 2, P // SHARE, SHARE]),
             )
-        for c in (2, 1):
-            back = psum.tile([P, 4, P], F32, name="acc")
-            for i in range(4):
-                nc.tensor.transpose(back[:, i, :], spread[2 * c - 2 + i // 2][:, i % 2, :], identity[:])
-            nc.scalar.copy(out=weights[:, c * J : (c + 1) * J], in_=back[:].rearrange("p i w -> p (i w)"))
+        for copy, tiles in ((nc.vector.tensor_copy, (3,)), (nc.scalar.copy, (2,)), (nc.scalar.copy, (0, 1))):
+            back = psum.tile([P, 2 * len(tiles), P], F32, name="acc")
+            for i in range(2 * len(tiles)):
+                nc.tensor.transpose(back[:, i, :], spread[tiles[i // 2]][:, i % 2, :], identity[:])
+            m0 = J + tiles[0] * HALF
+            copy(out=weights[:, m0 : m0 + len(tiles) * HALF], in_=back[:].rearrange("p i w -> p (i w)"))
 
         def entry0(u):
             return u[1] * J + u[0] * HALF
@@ -149,9 +149,9 @@ def tile_list_dl_prod_res_kernel(tc, xT, wgt, w4_words, w4_scales, wd, res, offs
             )
             nc.vector.quantize_mx(out=wd_codes[h][:].bitcast(FP8X4), scales=wd_scale[h][:], in_=wd_rounded)
 
-        gather_low(0, 0, P)
-        gather_low(0, P, J)
-        gather_low(0, J, ENTRIES)
+        gather_low(0, ENTRIES - HALF, ENTRIES)
+        gather_low(0, 0, J)
+        gather_low(0, J, ENTRIES - HALF)
         gather_low(1, 0, ENTRIES // 2)
         gather_low(1, ENTRIES // 2, ENTRIES)
         round_wd(0)
@@ -160,10 +160,10 @@ def tile_list_dl_prod_res_kernel(tc, xT, wgt, w4_words, w4_scales, wd, res, offs
         rounded_all = keep.tile([P, len(units) * HALF * PACK], BF16, name="rounded", tag="wd_raw1", align_bytes=64)
         rounded = {u: rounded_all[:, i * HALF * PACK : (i + 1) * HALF * PACK] for i, u in enumerate(units)}
 
-        def interleave_pair(u, e):
+        def interleave_pair(u, e, cols=slice(0, HALF)):
             nc.scalar.copy(
-                out=rounded[u].rearrange("p (j t) -> p j t", t=PACK)[:, :, 2 * e : 2 * e + 2],
-                in_=(low, high)[e][u].rearrange("p t j -> p j t"),
+                out=rounded[u].rearrange("p (j t) -> p j t", t=PACK)[:, cols, 2 * e : 2 * e + 2],
+                in_=(low, high)[e][u][:, :, cols].rearrange("p t j -> p j t"),
             )
 
         def pass_wd(acc, a, key, cols, opens):
@@ -259,14 +259,16 @@ def tile_list_dl_prod_res_kernel(tc, xT, wgt, w4_words, w4_scales, wd, res, offs
         quantize(units[2])
         project_third(1, range(N_TILES))
         gather_unit(2, units[5])
-        gather_unit(3, units[5])
+        for cols in (slice(0, P), slice(P, HALF)):
+            gather(high[units[5]][:, 1, cols], 3, entry0(units[5]) + cols.start, entry0(units[5]) + cols.stop)
         copy_first(blocks[0])
         four = slots[:, 2:36, :].rearrange("p (e s) j -> p e s j", e=2)[:, :, 0:7:6, :]
         nc.scalar.copy(
             out=rounded[units[4]].rearrange("p (g i e s) -> p g e s i", i=RUN, e=2, s=2),
             in_=four.rearrange("p e s (g i) -> p g e s i", i=RUN),
         )
-        interleave_pair(units[5], 1)
+        for cols in (slice(0, P), slice(P, HALF)):
+            interleave_pair(units[5], 1, cols)
         quantize(units[3])
         project_first(0)
         quantize(units[4])

@@ -73,7 +73,7 @@ def tile_list_dl_prod_res_kernel(tc, xT, wgt, w4_words, w4_scales, wd, res, offs
         nc.sync.dma_start(out=planes[2][:], in_=x_rows[2])
         nc.sync.dma_start(out=planes[3][:], in_=x_rows[3])
         for q in range(P // QUADRANT):
-            (nc.sync if q else nc.scalar).dma_start(
+            nc.scalar.dma_start(
                 out=w4_scale[QUADRANT * q : QUADRANT * q + 4, :].bitcast(I32),
                 in_=w4_scales[0, 4 * q : 4 * q + 4, :].bitcast(I32),
             )
@@ -152,8 +152,8 @@ def tile_list_dl_prod_res_kernel(tc, xT, wgt, w4_words, w4_scales, wd, res, offs
         gather_low(0, ENTRIES - HALF, ENTRIES)
         gather_low(0, 0, J)
         gather_low(0, J, ENTRIES - HALF)
-        gather_low(1, 0, ENTRIES // 2)
         gather_low(1, ENTRIES // 2, ENTRIES)
+        gather_low(1, 0, ENTRIES // 2)
         round_wd(0)
         round_wd(1)
 
@@ -236,7 +236,7 @@ def tile_list_dl_prod_res_kernel(tc, xT, wgt, w4_words, w4_scales, wd, res, offs
             engine.tensor_tensor(result[b][:, tiles, :], triple[b][:, tiles, :], residual[:, rows, half(h)], ADD)
             queue.dma_start(out=out_rows[:, rows, half(h)], in_=result[b][:, tiles, :])
 
-        for i in (0, 1, 2, 5):
+        for i in (1, 2, 5, 0):
             interleave_pair(units[i], 0)
         for u in units[:PICKS]:
             gather_unit(2, u)

@@ -27,8 +27,10 @@ RUN = 4
 BANKS = 8
 QUADRANT = 32
 ENTRIES = PICKS * J
+UNITS = ENTRIES // HALF
 CHUNKS = ENTRIES // P
 SHARE = 8
+HIGH_SLOTS = (12, 14, 17)
 
 
 def tile_list_dl_prod_res_kernel(tc, xT, wgt, w4_words, w4_scales, wd, res, offs, out):
@@ -42,10 +44,10 @@ def tile_list_dl_prod_res_kernel(tc, xT, wgt, w4_words, w4_scales, wd, res, offs
         weights = keep.tile([P, ENTRIES], F32, name="weights", tag="weights")
         w4_codes = keep.tile([P, 2 * N], U8, name="w4_codes", align_bytes=64)
         w4_scale = keep.tile([P, N], U8, name="w4_scale", align_bytes=64)
-        room = keep.tile([P, 36 * HALF], F32, name="room")
+        room = keep.tile([P, PACK * ENTRIES], F32, name="room")
         slots = room[:].rearrange("p (s j) -> p s j", j=HALF)
         wd_raw = [
-            slots[:, 12:34:7, :],
+            room[:, 2 * ENTRIES : 2 * ENTRIES + 10 * HALF].rearrange("p (t x) -> p t x", t=PACK)[:, :, 0:HALF],
             keep.tile([P, PACK, HALF], F32, name="wd_raw1", tag="wd_raw1", align_bytes=64)[:],
         ]
         wd_codes = [keep.tile([P, HALF], U32, name="wd_codes%d" % h, align_bytes=64) for h in range(2)]
@@ -59,7 +61,7 @@ def tile_list_dl_prod_res_kernel(tc, xT, wgt, w4_words, w4_scales, wd, res, offs
         thin_rows = wgt.rearrange("(u a) (c w) -> u (a c) w", a=SHARE, w=P)[:, CHUNKS - SHARE :: CHUNKS + 1, :]
 
         nc.vector.memset(w4_scale[:].bitcast(U32), 0)
-        thin = keep.tile([P, P], F32, name="thin", tag="thin", align_bytes=64)
+        thin = keep.tile([P, P], F32, name="thin", align_bytes=64)
         identity = keep.tile([P, P], F32, name="identity")
         make_identity(nc, identity[:])
 
@@ -103,11 +105,8 @@ def tile_list_dl_prod_res_kernel(tc, xT, wgt, w4_words, w4_scales, wd, res, offs
         def entry0(u):
             return u[1] * J + u[0] * HALF
 
-        high = {u: (slots[:, 12:19:6, :], slots[:, 19:26:6, :], slots[:, 26:28, :])[u[1]] for u in units}
-        low = {}
-        for u in units:
-            s = entry0(u) // HALF
-            low[u] = slots[:, s : s + 7 : 6, :]
+        high = {u: slots[:, HIGH_SLOTS[u[1]] : HIGH_SLOTS[u[1]] + UNITS + 1 : UNITS, :] for u in units}
+        low = {u: slots[:, entry0(u) // HALF : entry0(u) // HALF + UNITS + 1 : UNITS, :] for u in units}
         widths = (HALF, J)
         x_codes = {
             (h, g): keep.tile([P, widths[g]], U32, name="x_codes%d%d" % (h, g), align_bytes=64)
@@ -122,8 +121,8 @@ def tile_list_dl_prod_res_kernel(tc, xT, wgt, w4_words, w4_scales, wd, res, offs
         blocks = [(h, r) for h in (1, 0) for r in range(2)]
         first = {b: keep.tile([P, 2, HALF], F32, name="first%d%d" % b) for b in blocks}
         pair = {b: keep.tile([P, 2, HALF], F32, name="pair%d%d" % b)[:] for b in blocks[1:]}
-        triple = {b: keep.tile([P, 2, HALF], F32, name="triple%d%d" % b) for b in blocks}
-        result = {blocks[3]: keep.tile([P, 2, HALF], F32, name="result")}
+        triple = {b: keep.tile([P, 2, HALF], F32, name="triple%d%d" % b)[:] for b in blocks[1:]}
+        result = {blocks[3]: keep.tile([P, 2, HALF], F32, name="result")[:]}
         sums = {}
 
         def half(h):
@@ -136,17 +135,20 @@ def tile_list_dl_prod_res_kernel(tc, xT, wgt, w4_words, w4_scales, wd, res, offs
         def gather_low(t, m0, m1):
             gather(room[:, t * ENTRIES + m0 : t * ENTRIES + m1], t, m0, m1)
 
-        def gather_unit(t, u):
-            gather(high[u][:, t % 2, :], t, entry0(u), entry0(u) + HALF)
+        def gather_unit(t, u, cols=slice(0, HALF)):
+            gather(high[u][:, t % 2, cols], t, entry0(u) + cols.start, entry0(u) + cols.stop)
+
+        def interleave(dst, src):
+            nc.scalar.copy(
+                out=dst.rearrange("p (g i t) -> p g t i", i=RUN, t=PACK),
+                in_=src.rearrange("p t (g i) -> p g t i", i=RUN),
+            )
 
         wd_both = keep.tile([P, N * PACK], BF16, name="wd_both", tag="spread1", align_bytes=64)
 
         def round_wd(h):
             wd_rounded = wd_both[:, h * HALF * PACK : (h + 1) * HALF * PACK]
-            nc.scalar.copy(
-                out=wd_rounded.rearrange("p (g i t) -> p g t i", i=RUN, t=PACK),
-                in_=wd_raw[h].rearrange("p t (g i) -> p g t i", i=RUN),
-            )
+            interleave(wd_rounded, wd_raw[h])
             nc.vector.quantize_mx(out=wd_codes[h][:].bitcast(FP8X4), scales=wd_scale[h][:], in_=wd_rounded)
 
         gather_low(0, ENTRIES - HALF, ENTRIES)
@@ -157,7 +159,7 @@ def tile_list_dl_prod_res_kernel(tc, xT, wgt, w4_words, w4_scales, wd, res, offs
         round_wd(0)
         round_wd(1)
 
-        rounded_all = keep.tile([P, len(units) * HALF * PACK], BF16, name="rounded", tag="wd_raw1", align_bytes=64)
+        rounded_all = keep.tile([P, UNITS * HALF * PACK], BF16, name="rounded", tag="wd_raw1", align_bytes=64)
         rounded = {u: rounded_all[:, i * HALF * PACK : (i + 1) * HALF * PACK] for i, u in enumerate(units)}
 
         def interleave_pair(u, e, cols=slice(0, HALF)):
@@ -165,6 +167,9 @@ def tile_list_dl_prod_res_kernel(tc, xT, wgt, w4_words, w4_scales, wd, res, offs
                 out=rounded[u].rearrange("p (j t) -> p j t", t=PACK)[:, cols, 2 * e : 2 * e + 2],
                 in_=(low, high)[e][u][:, :, cols].rearrange("p t j -> p j t"),
             )
+
+        def interleave_whole(u):
+            interleave(rounded[u], slots[:, entry0(u) // HALF :: UNITS, :])
 
         def pass_wd(acc, a, key, cols, opens):
             w_cols = slice(P * (a % 2), P * (a % 2 + 1))
@@ -236,22 +241,22 @@ def tile_list_dl_prod_res_kernel(tc, xT, wgt, w4_words, w4_scales, wd, res, offs
             engine.tensor_tensor(result[b][:, tiles, :], triple[b][:, tiles, :], residual[:, rows, half(h)], ADD)
             queue.dma_start(out=out_rows[:, rows, half(h)], in_=result[b][:, tiles, :])
 
-        for i in (1, 2, 5, 0):
-            interleave_pair(units[i], 0)
+        for u in ((1, 1), (0, 2), (1, 0), (0, 1)):
+            interleave_pair(u, 0)
         for u in units[:PICKS]:
             gather_unit(2, u)
-        for u in units[:PICKS]:
+        for u in units[:2]:
             gather_unit(3, u)
             interleave_pair(u, 1)
+        gather_unit(3, units[2])
+        interleave_whole(units[2])
 
+        pieces = (slice(0, HALF // 2), slice(HALF // 2, HALF))
         quantize(units[0])
         project_first(1)
         gather_unit(2, units[3])
         gather_unit(3, units[3])
-        nc.scalar.copy(
-            out=rounded[units[3]].rearrange("p (g i t) -> p g t i", i=RUN, t=PACK),
-            in_=slots[:, 0:19:6, :].rearrange("p t (g i) -> p g t i", i=RUN),
-        )
+        interleave_whole(units[3])
         quantize(units[1])
         project_second(1, range(N_TILES))
         gather_unit(2, units[4])
@@ -259,36 +264,32 @@ def tile_list_dl_prod_res_kernel(tc, xT, wgt, w4_words, w4_scales, wd, res, offs
         quantize(units[2])
         project_third(1, range(N_TILES))
         gather_unit(2, units[5])
-        for cols in (slice(0, P), slice(P, HALF)):
-            gather(high[units[5]][:, 1, cols], 3, entry0(units[5]) + cols.start, entry0(units[5]) + cols.stop)
+        for cols in pieces:
+            gather_unit(3, units[5], cols)
         copy_first(blocks[0])
-        four = slots[:, 2:36, :].rearrange("p (e s) j -> p e s j", e=2)[:, :, 0:7:6, :]
-        nc.scalar.copy(
-            out=rounded[units[4]].rearrange("p (g i e s) -> p g e s i", i=RUN, e=2, s=2),
-            in_=four.rearrange("p e s (g i) -> p g e s i", i=RUN),
-        )
-        for cols in (slice(0, P), slice(P, HALF)):
+        interleave_pair(units[4], 1)
+        for cols in pieces:
             interleave_pair(units[5], 1, cols)
         quantize(units[3])
         project_first(0)
         quantize(units[4])
         project_second(0, [0])
         quantize(units[5])
-        copy_first(blocks[1])
-        copy_first(blocks[2])
-        copy_first(blocks[3])
+        for b in blocks[1:]:
+            copy_first(b)
 
         early = keep.tile([P, 3, 2, HALF], F32, name="early", tag="wd_raw1", align_bytes=64)
         for i in range(3):
             result[blocks[i]] = early[:, i]
         pair[blocks[0]] = keep.tile([P, 2, HALF], F32, name="pair_first", tag="weights")[:]
-        triple[blocks[0]] = slots[:, 24:27:2, :]
+        triple[blocks[0]] = slots[:, PACK * UNITS - 2 :, :]
         times_second(blocks[0])
         times_third(blocks[0])
         project_second(0, [1])
         project_third(0, range(2))
         project_second(0, range(2, N_TILES))
         project_third(0, range(2, N_TILES))
+
         finish(nc.gpsimd, nc.sync, blocks[0], slice(0, 1))
         finish(nc.gpsimd, nc.sync, blocks[0], slice(1, 2))
         for b in blocks[1:3]:

@@ -30,6 +30,8 @@ ENTRIES = PICKS * J
 UNITS = ENTRIES // HALF
 CHUNKS = ENTRIES // P
 SHARE = 8
+SPREAD = SHARE * P
+NARROW = (ENTRIES - SPREAD) // SHARE
 HIGH_SLOTS = (12, 14, 17)
 
 
@@ -41,7 +43,7 @@ def tile_list_dl_prod_res_kernel(tc, xT, wgt, w4_words, w4_scales, wd, res, offs
 
         offsets = keep.tile([P, ENTRIES // GROUP], U16, name="offsets")
         planes = [keep.tile([P, T], F32, name="plane%d" % t) for t in range(PACK)]
-        weights = keep.tile([P, ENTRIES], F32, name="weights", tag="weights")
+        weights = keep.tile([P, ENTRIES], F32, name="weights", tag="weights", align_bytes=64)
         w4_codes = keep.tile([P, 2 * N], U8, name="w4_codes", align_bytes=64)
         w4_scale = keep.tile([P, N], U8, name="w4_scale", align_bytes=64)
         room = keep.tile([P, PACK * ENTRIES], F32, name="room")
@@ -58,17 +60,22 @@ def tile_list_dl_prod_res_kernel(tc, xT, wgt, w4_words, w4_scales, wd, res, offs
         wd_rows = wd.rearrange("(p t) n -> p t n", t=PACK)
         out_rows = out.rearrange("(a p) j -> p a j", p=P)
 
-        thin_rows = wgt.rearrange("(u a) (c w) -> u (a c) w", a=SHARE, w=P)[:, CHUNKS - SHARE :: CHUNKS + 1, :]
+        thin_rows = wgt.rearrange("(u a) (c w) -> u (a c) w", a=SHARE, w=P)[:, :: CHUNKS + 1, :]
+
+        narrow_rows = wgt.rearrange("(u a) (c w) -> u (a c) w", a=SHARE, w=NARROW)[
+            :, SPREAD // NARROW :: ENTRIES // NARROW + 1, :
+        ]
 
         nc.vector.memset(w4_scale[:].bitcast(U32), 0)
         thin = keep.tile([P, P], F32, name="thin", align_bytes=64)
+        narrow = keep.tile([P, NARROW], F32, name="narrow", align_bytes=64)
         identity = keep.tile([P, P], F32, name="identity")
         make_identity(nc, identity[:])
 
+        nc.sync.dma_start(out=narrow[:], in_=narrow_rows)
         nc.sync.dma_start(out=thin[:], in_=thin_rows)
         nc.sync.dma_start(out=planes[0][:], in_=x_rows[0])
         nc.sync.dma_start(offsets[:], offs)
-        nc.sync.dma_start(out=weights[:, 0:J], in_=wgt[:, 0:J])
         nc.sync.dma_start(out=planes[1][:], in_=x_rows[1])
         nc.sync.dma_start(out=wd_raw[0], in_=wd_rows[:, :, 0:HALF])
         nc.sync.dma_start(out=wd_raw[1], in_=wd_rows[:, :, HALF:N])
@@ -84,23 +91,35 @@ def tile_list_dl_prod_res_kernel(tc, xT, wgt, w4_words, w4_scales, wd, res, offs
 
         units = [(h, c) for h in (1, 0) for c in range(PICKS)]
 
+        blocked = keep.tile([P, NARROW], F32, name="blocked", align_bytes=64)
+        for s0 in range(0, NARROW, QUADRANT):
+            nc.vector.transpose(blocked[:, s0 : s0 + QUADRANT], narrow[:, s0 : s0 + QUADRANT])
+        repeated = keep.tile([P, ENTRIES - SPREAD], F32, name="repeated", align_bytes=64)
+        nc.vector.tensor_copy(
+            out=repeated[:].rearrange("p (i s u r) -> p i s u r", i=SHARE, u=QUADRANT // SHARE, r=SHARE),
+            in_=blocked[:]
+            .rearrange("p (s u i) -> p i s u", i=SHARE, u=QUADRANT // SHARE)
+            .unsqueeze(4)
+            .to_broadcast([P, SHARE, NARROW // QUADRANT, QUADRANT // SHARE, SHARE]),
+        )
+        nc.vector.transpose(weights[:, SPREAD:ENTRIES], repeated[:])
+
         turned = psum.tile([P, P], F32, name="acc")
         nc.tensor.transpose(turned[:], thin[:], identity[:])
         by_chunk = turned[:].rearrange("p (u i) -> p i u", i=SHARE)
-        spread = [slots[:, 0, :].rearrange("p (i w) -> p i w", w=P)] + [
-            keep.tile([P, 2, P], F32, name="spread%d" % e, tag="spread%d" % e, align_bytes=64)[:] for e in (1, 2, 3)
-        ]
-        for e in (3, 2, 0, 1):
-            (nc.scalar.copy, nc.vector.tensor_copy)[e // 2](
-                out=spread[e].rearrange("p i (u r) -> p i u r", r=SHARE),
-                in_=by_chunk[:, 2 * e : 2 * e + 2, :].unsqueeze(3).to_broadcast([P, 2, P // SHARE, SHARE]),
+        spread = {}
+        for c0 in (0, PACK):
+            tag = "spread%d" % c0
+            spread[c0] = keep.tile([P, PACK, P], F32, name=tag, tag=tag, align_bytes=64)
+            nc.scalar.copy(
+                out=spread[c0][:].rearrange("p i (u r) -> p i u r", r=SHARE),
+                in_=by_chunk[:, c0 : c0 + PACK, :].unsqueeze(3).to_broadcast([P, PACK, P // SHARE, SHARE]),
             )
-        for copy, tiles in ((nc.vector.tensor_copy, (3,)), (nc.scalar.copy, (2,)), (nc.scalar.copy, (0, 1))):
-            back = psum.tile([P, 2 * len(tiles), P], F32, name="acc")
-            for i in range(2 * len(tiles)):
-                nc.tensor.transpose(back[:, i, :], spread[tiles[i // 2]][:, i % 2, :], identity[:])
-            m0 = J + tiles[0] * HALF
-            copy(out=weights[:, m0 : m0 + len(tiles) * HALF], in_=back[:].rearrange("p i w -> p (i w)"))
+        for c0 in (0, PACK):
+            back = psum.tile([P, PACK, P], F32, name="acc")
+            for i in range(PACK):
+                nc.tensor.transpose(back[:, i, :], spread[c0][:, i, :], identity[:])
+            nc.scalar.copy(out=weights[:, c0 * P : (c0 + PACK) * P], in_=back[:].rearrange("p i w -> p (i w)"))
 
         def entry0(u):
             return u[1] * J + u[0] * HALF
@@ -144,16 +163,16 @@ def tile_list_dl_prod_res_kernel(tc, xT, wgt, w4_words, w4_scales, wd, res, offs
                 in_=src.rearrange("p t (g i) -> p g t i", i=RUN),
             )
 
-        wd_both = keep.tile([P, N * PACK], BF16, name="wd_both", tag="spread1", align_bytes=64)
+        wd_both = keep.tile([P, N * PACK], BF16, name="wd_both", tag="spread4", align_bytes=64)
 
         def round_wd(h):
             wd_rounded = wd_both[:, h * HALF * PACK : (h + 1) * HALF * PACK]
             interleave(wd_rounded, wd_raw[h])
             nc.vector.quantize_mx(out=wd_codes[h][:].bitcast(FP8X4), scales=wd_scale[h][:], in_=wd_rounded)
 
-        gather_low(0, ENTRIES - HALF, ENTRIES)
+        gather_low(0, SPREAD, ENTRIES)
         gather_low(0, 0, J)
-        gather_low(0, J, ENTRIES - HALF)
+        gather_low(0, J, SPREAD)
         gather_low(1, ENTRIES // 2, ENTRIES)
         gather_low(1, 0, ENTRIES // 2)
         round_wd(0)
@@ -281,7 +300,7 @@ def tile_list_dl_prod_res_kernel(tc, xT, wgt, w4_words, w4_scales, wd, res, offs
         early = keep.tile([P, 3, 2, HALF], F32, name="early", tag="wd_raw1", align_bytes=64)
         for i in range(3):
             result[blocks[i]] = early[:, i]
-        pair[blocks[0]] = keep.tile([P, 2, HALF], F32, name="pair_first", tag="weights")[:]
+        pair[blocks[0]] = keep.tile([P, 2, HALF], F32, name="pair_first", tag="weights", align_bytes=64)[:]
         triple[blocks[0]] = slots[:, PACK * UNITS - 2 :, :]
         times_second(blocks[0])
         times_third(blocks[0])

@@ -1,7 +1,6 @@
 from contextlib import ExitStack
 
 import concourse.mybir as mybir
-from concourse.masks import make_identity
 
 K, N, T, J, PICKS = 512, 512, 2048, 512, 3
 FLOPS = 2 * 2 * K * N * J * PICKS
@@ -21,7 +20,6 @@ P = 128
 PACK = 4
 GROUP = 16
 HALF = 256
-W4_COLS = 128
 N_TILES = N // P
 RUN = 4
 BANKS = 8
@@ -31,8 +29,6 @@ UNITS = ENTRIES // HALF
 CHUNKS = ENTRIES // P
 SHARE = 8
 SPREAD = SHARE * P
-NARROW = (ENTRIES - SPREAD) // SHARE
-HIGH_SLOTS = (12, 14, 17)
 
 
 def tile_list_dl_prod_res_kernel(tc, xT, wgt, w4_words, w4_scales, wd, res, offs, out):
@@ -49,9 +45,10 @@ def tile_list_dl_prod_res_kernel(tc, xT, wgt, w4_words, w4_scales, wd, res, offs
         room = keep.tile([P, PACK * ENTRIES], F32, name="room")
         slots = room[:].rearrange("p (s j) -> p s j", j=HALF)
         wd_raw = [
-            room[:, 2 * ENTRIES : 2 * ENTRIES + 10 * HALF].rearrange("p (t x) -> p t x", t=PACK)[:, :, 0:HALF],
-            keep.tile([P, PACK, HALF], F32, name="wd_raw1", tag="wd_raw1", align_bytes=64)[:],
+            keep.tile([P, PACK, HALF], F32, name="wd_raw0", tag="staged", align_bytes=64),
+            keep.tile([P, PACK, HALF], F32, name="wd_raw1", align_bytes=64),
         ]
+        wd_rounded = [keep.tile([P, HALF * PACK], BF16, name="wd_rounded%d" % h, align_bytes=64) for h in range(2)]
         wd_codes = [keep.tile([P, HALF], U32, name="wd_codes%d" % h, align_bytes=64) for h in range(2)]
         wd_scale = [keep.tile([P, HALF], U8, name="wd_scale%d" % h, align_bytes=64) for h in range(2)]
         residual = keep.tile([P, N_TILES, J], F32, name="residual")
@@ -59,87 +56,58 @@ def tile_list_dl_prod_res_kernel(tc, xT, wgt, w4_words, w4_scales, wd, res, offs
         x_rows = xT.rearrange("(p t) w -> t p w", t=PACK)
         wd_rows = wd.rearrange("(p t) n -> p t n", t=PACK)
         out_rows = out.rearrange("(a p) j -> p a j", p=P)
-
         thin_rows = wgt.rearrange("(u a) (c w) -> u (a c) w", a=SHARE, w=P)[:, :: CHUNKS + 1, :]
-
-        narrow_rows = wgt.rearrange("(u a) (c w) -> u (a c) w", a=SHARE, w=NARROW)[
-            :, SPREAD // NARROW :: ENTRIES // NARROW + 1, :
-        ]
 
         nc.vector.memset(w4_scale[:].bitcast(U32), 0)
         thin = keep.tile([P, P], F32, name="thin", align_bytes=64)
-        narrow = keep.tile([P, NARROW], F32, name="narrow", align_bytes=64)
-        identity = keep.tile([P, P], F32, name="identity")
-        make_identity(nc, identity[:])
 
-        nc.sync.dma_start(out=narrow[:], in_=narrow_rows)
         nc.sync.dma_start(out=thin[:], in_=thin_rows)
         nc.sync.dma_start(out=planes[0][:], in_=x_rows[0])
         nc.sync.dma_start(offsets[:], offs)
-        nc.sync.dma_start(out=planes[1][:], in_=x_rows[1])
-        nc.sync.dma_start(out=wd_raw[0], in_=wd_rows[:, :, 0:HALF])
-        nc.sync.dma_start(out=wd_raw[1], in_=wd_rows[:, :, HALF:N])
-        nc.sync.dma_start(out=planes[2][:], in_=x_rows[2])
-        nc.sync.dma_start(out=planes[3][:], in_=x_rows[3])
+        nc.sync.dma_start(out=weights[:, SPREAD:ENTRIES], in_=wgt[:, SPREAD:ENTRIES])
         for q in range(P // QUADRANT):
-            nc.scalar.dma_start(
+            nc.sync.dma_start(
                 out=w4_scale[QUADRANT * q : QUADRANT * q + 4, :].bitcast(I32),
                 in_=w4_scales[0, 4 * q : 4 * q + 4, :].bitcast(I32),
             )
+        nc.sync.dma_start(out=planes[1][:], in_=x_rows[1])
+        nc.sync.dma_start(out=wd_raw[0][:], in_=wd_rows[:, :, 0:HALF])
+        nc.sync.dma_start(out=planes[2][:], in_=x_rows[2])
+        nc.sync.dma_start(out=planes[3][:], in_=x_rows[3])
         nc.sync.dma_start(out=w4_codes[:].bitcast(I32), in_=w4_words[0].bitcast(I32))
+        nc.sync.dma_start(out=wd_raw[1][:], in_=wd_rows[:, :, HALF:N])
         nc.sync.dma_start(out=residual[:], in_=res.rearrange("(a p) j -> p a j", p=P))
 
-        units = [(h, c) for h in (1, 0) for c in range(PICKS)]
-
-        blocked = keep.tile([P, NARROW], F32, name="blocked", align_bytes=64)
-        for s0 in range(0, NARROW, QUADRANT):
-            nc.vector.transpose(blocked[:, s0 : s0 + QUADRANT], narrow[:, s0 : s0 + QUADRANT])
-        repeated = keep.tile([P, ENTRIES - SPREAD], F32, name="repeated", align_bytes=64)
-        nc.vector.tensor_copy(
-            out=repeated[:].rearrange("p (i s u r) -> p i s u r", i=SHARE, u=QUADRANT // SHARE, r=SHARE),
-            in_=blocked[:]
-            .rearrange("p (s u i) -> p i s u", i=SHARE, u=QUADRANT // SHARE)
-            .unsqueeze(4)
-            .to_broadcast([P, SHARE, NARROW // QUADRANT, QUADRANT // SHARE, SHARE]),
-        )
-        nc.vector.transpose(weights[:, SPREAD:ENTRIES], repeated[:])
-
-        turned = psum.tile([P, P], F32, name="acc")
-        nc.tensor.transpose(turned[:], thin[:], identity[:])
-        by_chunk = turned[:].rearrange("p (u i) -> p i u", i=SHARE)
-        spread = {}
-        for c0 in (0, PACK):
-            tag = "spread%d" % c0
-            spread[c0] = keep.tile([P, PACK, P], F32, name=tag, tag=tag, align_bytes=64)
-            nc.scalar.copy(
-                out=spread[c0][:].rearrange("p i (u r) -> p i u r", r=SHARE),
-                in_=by_chunk[:, c0 : c0 + PACK, :].unsqueeze(3).to_broadcast([P, PACK, P // SHARE, SHARE]),
+        blocked = keep.tile([P, P], F32, name="blocked", align_bytes=64)
+        nc.vector.transpose(blocked[:], thin[:])
+        by_chunk = blocked[:].rearrange("p (s u i) -> p i s u", i=SHARE, u=QUADRANT // SHARE)
+        repeated = [keep.tile([P, J], F32, name="repeated%d" % e, align_bytes=64) for e in range(2)]
+        for e, copy in enumerate((nc.vector.tensor_copy, nc.scalar.copy)):
+            copy(
+                out=repeated[e][:].rearrange("p (i s u r) -> p i s u r", i=PACK, u=QUADRANT // SHARE, r=SHARE),
+                in_=by_chunk[:, PACK * e : PACK * (e + 1)]
+                .unsqueeze(4)
+                .to_broadcast([P, PACK, P // QUADRANT, QUADRANT // SHARE, SHARE]),
             )
-        for c0 in (0, PACK):
-            back = psum.tile([P, PACK, P], F32, name="acc")
-            for i in range(PACK):
-                nc.tensor.transpose(back[:, i, :], spread[c0][:, i, :], identity[:])
-            nc.scalar.copy(out=weights[:, c0 * P : (c0 + PACK) * P], in_=back[:].rearrange("p i w -> p (i w)"))
+        for e in range(2):
+            nc.vector.transpose(weights[:, e * J : (e + 1) * J], repeated[e][:])
+
+        units = [(0, 0), (0, 1), (0, 2), (1, 2), (1, 0), (1, 1)]
 
         def entry0(u):
             return u[1] * J + u[0] * HALF
 
-        high = {u: slots[:, HIGH_SLOTS[u[1]] : HIGH_SLOTS[u[1]] + UNITS + 1 : UNITS, :] for u in units}
-        low = {u: slots[:, entry0(u) // HALF : entry0(u) // HALF + UNITS + 1 : UNITS, :] for u in units}
-        widths = (HALF, J)
-        x_codes = {
-            (h, g): keep.tile([P, widths[g]], U32, name="x_codes%d%d" % (h, g), align_bytes=64)
-            for h in range(2)
-            for g in range(2)
-        }
-        x_scale = {
-            (h, g): keep.tile([P, widths[g]], U8, name="x_scale%d%d" % (h, g), align_bytes=64)
-            for h in range(2)
-            for g in range(2)
-        }
-        blocks = [(h, r) for h in (1, 0) for r in range(2)]
-        first = {b: keep.tile([P, 2, HALF], F32, name="first%d%d" % b) for b in blocks}
-        pair = {b: keep.tile([P, 2, HALF], F32, name="pair%d%d" % b)[:] for b in blocks[1:]}
+        def own(u):
+            return entry0(u) // HALF
+
+        side = [keep.tile([P, 3, HALF], F32, name="side%d" % i) for i in range(2)]
+        rings = [slots[:, 17 :: UNITS, :], side[0][:, 0:2, :], side[1][:, 1:3, :]]
+        high = {u: rings[i % PICKS] for i, u in enumerate(units)}
+        x_codes = {u: keep.tile([P, HALF], U32, name="x_codes%d%d" % u, align_bytes=64) for u in units}
+        x_scale = {u: keep.tile([P, HALF], U8, name="x_scale%d%d" % u, align_bytes=64) for u in units}
+        blocks = [(h, r) for h in range(2) for r in range(2)]
+        first = {b: keep.tile([P, 2 * HALF], F32, name="first%d%d" % b) for b in blocks}
+        pair = {b: keep.tile([P, 2 * HALF], F32, name="pair%d%d" % b)[:] for b in blocks[1:]}
         triple = {b: keep.tile([P, 2, HALF], F32, name="triple%d%d" % b)[:] for b in blocks[1:]}
         result = {blocks[3]: keep.tile([P, 2, HALF], F32, name="result")[:]}
         sums = {}
@@ -163,96 +131,93 @@ def tile_list_dl_prod_res_kernel(tc, xT, wgt, w4_words, w4_scales, wd, res, offs
                 in_=src.rearrange("p t (g i) -> p g t i", i=RUN),
             )
 
-        wd_both = keep.tile([P, N * PACK], BF16, name="wd_both", tag="spread4", align_bytes=64)
-
         def round_wd(h):
-            wd_rounded = wd_both[:, h * HALF * PACK : (h + 1) * HALF * PACK]
-            interleave(wd_rounded, wd_raw[h])
-            nc.vector.quantize_mx(out=wd_codes[h][:].bitcast(FP8X4), scales=wd_scale[h][:], in_=wd_rounded)
+            interleave(wd_rounded[h][:], wd_raw[h][:])
 
+        def quantize_wd(h):
+            nc.vector.quantize_mx(out=wd_codes[h][:].bitcast(FP8X4), scales=wd_scale[h][:], in_=wd_rounded[h][:])
+
+        gather_low(0, 0, SPREAD)
         gather_low(0, SPREAD, ENTRIES)
-        gather_low(0, 0, J)
-        gather_low(0, J, SPREAD)
-        gather_low(1, ENTRIES // 2, ENTRIES)
-        gather_low(1, 0, ENTRIES // 2)
+        gather_low(1, 0, J)
+        gather_low(1, J, ENTRIES)
         round_wd(0)
-        round_wd(1)
+        quantize_wd(0)
 
-        rounded_all = keep.tile([P, UNITS * HALF * PACK], BF16, name="rounded", tag="wd_raw1", align_bytes=64)
-        rounded = {u: rounded_all[:, i * HALF * PACK : (i + 1) * HALF * PACK] for i, u in enumerate(units)}
+        rounded_all = keep.tile([P, ENTRIES * PACK], BF16, name="rounded", tag="staged", align_bytes=64)
+        by_entry = rounded_all[:].rearrange("p (m t) -> p m t", t=PACK)
+        rounded = {u: rounded_all[:, entry0(u) * PACK : (entry0(u) + HALF) * PACK] for u in units}
 
-        def interleave_pair(u, e, cols=slice(0, HALF)):
+        def interleave_low(u):
             nc.scalar.copy(
-                out=rounded[u].rearrange("p (j t) -> p j t", t=PACK)[:, cols, 2 * e : 2 * e + 2],
-                in_=(low, high)[e][u][:, :, cols].rearrange("p t j -> p j t"),
+                out=by_entry[:, entry0(u) : entry0(u) + HALF, 0:2],
+                in_=slots[:, own(u) : own(u) + UNITS + 1 : UNITS, :].rearrange("p t j -> p j t"),
+            )
+
+        def interleave_high(u, cols=slice(0, HALF)):
+            nc.scalar.copy(
+                out=by_entry[:, entry0(u) + cols.start : entry0(u) + cols.stop, 2:4],
+                in_=high[u][:, :, cols].rearrange("p t j -> p j t"),
             )
 
         def interleave_whole(u):
-            interleave(rounded[u], slots[:, entry0(u) // HALF :: UNITS, :])
+            interleave(rounded[u], slots[:, own(u) :: UNITS, :])
 
-        def pass_wd(acc, a, key, cols, opens):
+        def pass_wd(u, a, opens, closes):
             w_cols = slice(P * (a % 2), P * (a % 2 + 1))
             nc.tensor.matmul_mx(
-                out=acc,
+                out=sums[u, a // 2][:, half(a % 2)],
                 lhsT=wd_codes[a // 2][:, w_cols].bitcast(FP8X4),
                 lhsT_scale=wd_scale[a // 2][:, w_cols],
-                rhs=x_codes[key][:, cols].bitcast(FP8X4),
-                rhs_scale=x_scale[key][:, cols],
+                rhs=x_codes[u][:].bitcast(FP8X4),
+                rhs_scale=x_scale[u][:],
                 start=opens,
-                stop=False,
-            )
-
-        def pass_w4(acc, a, key, cols, closes):
-            nc.tensor.matmul_mx(
-                out=acc,
-                lhsT=w4_codes[:, 2 * P * a : 2 * P * (a + 1)].bitcast(FP4X4),
-                lhsT_scale=w4_scale[:, P * a : P * (a + 1)],
-                rhs=x_codes[key][:, cols].bitcast(FP8X4),
-                rhs_scale=x_scale[key][:, cols],
-                start=False,
                 stop=closes,
             )
 
-        def project_first(h):
-            for r in range(2):
-                sums[h, 0, r] = psum.tile([P, 2, HALF], F32, name="acc")
-                for i in range(2):
-                    pass_wd(sums[h, 0, r][:, i, :], 2 * r + i, (h, 0), half(0), True)
-                    for j0 in range(0, HALF, W4_COLS):
-                        cols = slice(j0, j0 + W4_COLS)
-                        pass_w4(sums[h, 0, r][:, i, cols], 2 * r + i, (h, 0), cols, j0 + W4_COLS == HALF)
-
-        def project_second(h, tiles):
-            for a in tiles:
-                sums[h, 1, a] = psum.tile([P, J], F32, name="acc")
-                pass_wd(sums[h, 1, a][:, half(0)], a, (h, 1), half(0), True)
-
-        def project_third(h, tiles):
-            for a in tiles:
-                pass_wd(sums[h, 1, a][:, half(1)], a, (h, 1), half(1), False)
-                pass_w4(sums[h, 1, a][:], a, (h, 1), slice(0, J), True)
-
-        def quantize(u):
-            h, c = u
-            key, cols = (h, min(c, 1)), half(c // 2)
-            nc.vector.quantize_mx(
-                out=x_codes[key][:, cols].bitcast(FP8X4), scales=x_scale[key][:, cols], in_=rounded[u]
+        def pass_w4(u, a, opens, closes):
+            nc.tensor.matmul_mx(
+                out=sums[u, a // 2][:, half(a % 2)],
+                lhsT=w4_codes[:, 2 * P * a : 2 * P * (a + 1)].bitcast(FP4X4),
+                lhsT_scale=w4_scale[:, P * a : P * (a + 1)],
+                rhs=x_codes[u][:].bitcast(FP8X4),
+                rhs_scale=x_scale[u][:],
+                start=opens,
+                stop=closes,
             )
 
+        def open_bank(u, r):
+            sums[u, r] = psum.tile([P, 2 * HALF], F32, name="acc")
+            pass_w4(u, 2 * r, True, False)
+            pass_w4(u, 2 * r + 1, False, False)
+
+        def close_bank(u, r):
+            pass_wd(u, 2 * r, False, False)
+            pass_wd(u, 2 * r + 1, False, True)
+
+        def project(u):
+            for r in range(2):
+                open_bank(u, r)
+                close_bank(u, r)
+
+        def quantize(u):
+            nc.vector.quantize_mx(out=x_codes[u][:].bitcast(FP8X4), scales=x_scale[u][:], in_=rounded[u])
+
+        def factor(b, i):
+            return sums[units[PICKS * b[0] + i], b[1]]
+
         def copy_first(b):
-            nc.scalar.copy(out=first[b][:], in_=sums[b[0], 0, b[1]][:])
+            nc.scalar.copy(out=first[b][:], in_=factor(b, 0)[:])
 
-        def times_second(b):
-            for i in range(2):
-                nc.vector.tensor_tensor(
-                    pair[b][:, i, :], sums[b[0], 1, 2 * b[1] + i][:, half(0)], first[b][:, i, :], MULT
-                )
+        def times_second(b, tiles=slice(0, 2)):
+            cols = slice(tiles.start * HALF, tiles.stop * HALF)
+            nc.vector.tensor_tensor(pair[b][:, cols], factor(b, 1)[:, cols], first[b][:, cols], MULT)
 
-        def times_third(b):
-            for i in range(2):
-                nc.vector.tensor_tensor(
-                    triple[b][:, i, :], sums[b[0], 1, 2 * b[1] + i][:, half(1)], pair[b][:, i, :], MULT
-                )
+        def times_third(b, tiles=slice(0, 2)):
+            cols = slice(tiles.start * HALF, tiles.stop * HALF)
+            nc.vector.tensor_tensor(
+                triple[b][:, tiles, :].rearrange("p a j -> p (a j)"), factor(b, 2)[:, cols], pair[b][:, cols], MULT
+            )
 
         def finish(engine, queue, b, tiles):
             h, r = b
@@ -260,63 +225,67 @@ def tile_list_dl_prod_res_kernel(tc, xT, wgt, w4_words, w4_scales, wd, res, offs
             engine.tensor_tensor(result[b][:, tiles, :], triple[b][:, tiles, :], residual[:, rows, half(h)], ADD)
             queue.dma_start(out=out_rows[:, rows, half(h)], in_=result[b][:, tiles, :])
 
-        for u in ((1, 1), (0, 2), (1, 0), (0, 1)):
-            interleave_pair(u, 0)
-        for u in units[:PICKS]:
-            gather_unit(2, u)
+        for i in (0, 4, 1, 5, 2):
+            interleave_low(units[i])
+        for t in (2, 3):
+            for u in units[:PICKS]:
+                gather_unit(t, u)
         for u in units[:2]:
-            gather_unit(3, u)
-            interleave_pair(u, 1)
-        gather_unit(3, units[2])
-        interleave_whole(units[2])
+            interleave_high(u)
 
         pieces = (slice(0, HALF // 2), slice(HALF // 2, HALF))
-        quantize(units[0])
-        project_first(1)
-        gather_unit(2, units[3])
-        gather_unit(3, units[3])
+        for u, later in zip(units[:2], units[3:5]):
+            quantize(u)
+            open_bank(u, 0)
+            close_bank(u, 0)
+            open_bank(u, 1)
+            gather_unit(2, later)
+            gather_unit(3, later)
+        round_wd(1)
+        interleave_high(units[2])
         interleave_whole(units[3])
-        quantize(units[1])
-        project_second(1, range(N_TILES))
-        gather_unit(2, units[4])
-        gather_unit(3, units[4])
+        quantize_wd(1)
+        close_bank(units[0], 1)
+        close_bank(units[1], 1)
         quantize(units[2])
-        project_third(1, range(N_TILES))
+        project(units[2])
         gather_unit(2, units[5])
         for cols in pieces:
             gather_unit(3, units[5], cols)
         copy_first(blocks[0])
-        interleave_pair(units[4], 1)
+        interleave_high(units[4])
         for cols in pieces:
-            interleave_pair(units[5], 1, cols)
+            interleave_high(units[5], cols)
         quantize(units[3])
-        project_first(0)
+        project(units[3])
         quantize(units[4])
-        project_second(0, [0])
         quantize(units[5])
         for b in blocks[1:]:
             copy_first(b)
 
-        early = keep.tile([P, 3, 2, HALF], F32, name="early", tag="wd_raw1", align_bytes=64)
+        early = keep.tile([P, 3, 2, HALF], F32, name="early", tag="staged", align_bytes=64)
         for i in range(3):
             result[blocks[i]] = early[:, i]
-        pair[blocks[0]] = keep.tile([P, 2, HALF], F32, name="pair_first", tag="weights", align_bytes=64)[:]
-        triple[blocks[0]] = slots[:, PACK * UNITS - 2 :, :]
-        times_second(blocks[0])
-        times_third(blocks[0])
-        project_second(0, [1])
-        project_third(0, range(2))
-        project_second(0, range(2, N_TILES))
-        project_third(0, range(2, N_TILES))
-
+        pair[blocks[0]] = side[1][:, 0:2, :].rearrange("p a j -> p (a j)")
+        triple[blocks[0]] = side[0][:, 1:3, :]
+        times_second(blocks[0], slice(0, 1))
+        times_third(blocks[0], slice(0, 1))
+        times_second(blocks[0], slice(1, 2))
+        times_second(blocks[1], slice(0, 1))
+        times_third(blocks[0], slice(1, 2))
+        times_second(blocks[1], slice(1, 2))
+        project(units[4])
+        project(units[5])
         finish(nc.gpsimd, nc.sync, blocks[0], slice(0, 1))
         finish(nc.gpsimd, nc.sync, blocks[0], slice(1, 2))
-        for b in blocks[1:3]:
-            times_second(b)
-            times_third(b)
+        times_third(blocks[1], slice(0, 1))
+        times_third(blocks[1], slice(1, 2))
         finish(nc.gpsimd, nc.sync, blocks[1], slice(0, 2))
-        finish(nc.gpsimd, nc.sync, blocks[2], slice(0, 1))
+        times_second(blocks[2])
         times_second(blocks[3])
+        times_third(blocks[2], slice(0, 1))
+        finish(nc.gpsimd, nc.sync, blocks[2], slice(0, 1))
+        times_third(blocks[2], slice(1, 2))
         times_third(blocks[3])
         finish(nc.vector, nc.scalar, blocks[2], slice(1, 2))
         finish(nc.vector, nc.sync, blocks[3], slice(0, 1))

@@ -137,8 +137,8 @@ def tile_list_dl_prod_res_kernel(tc, xT, wgt, w4_words, w4_scales, wd, res, offs
         def quantize_wd(h):
             nc.vector.quantize_mx(out=wd_codes[h][:].bitcast(FP8X4), scales=wd_scale[h][:], in_=wd_rounded[h][:])
 
-        gather_low(0, 0, SPREAD)
-        gather_low(0, SPREAD, ENTRIES)
+        gather_low(0, 0, J)
+        gather_low(0, J, ENTRIES)
         gather_low(1, 0, J)
         gather_low(1, J, ENTRIES)
         round_wd(0)
@@ -219,11 +219,12 @@ def tile_list_dl_prod_res_kernel(tc, xT, wgt, w4_words, w4_scales, wd, res, offs
                 triple[b][:, tiles, :].rearrange("p a j -> p (a j)"), factor(b, 2)[:, cols], pair[b][:, cols], MULT
             )
 
-        def finish(engine, queue, b, tiles):
+        def finish(engine, queue, b, tiles, cols=slice(0, HALF)):
             h, r = b
             rows = slice(2 * r + tiles.start, 2 * r + tiles.stop)
-            engine.tensor_tensor(result[b][:, tiles, :], triple[b][:, tiles, :], residual[:, rows, half(h)], ADD)
-            queue.dma_start(out=out_rows[:, rows, half(h)], in_=result[b][:, tiles, :])
+            places = slice(h * HALF + cols.start, h * HALF + cols.stop)
+            engine.tensor_tensor(result[b][:, tiles, cols], triple[b][:, tiles, cols], residual[:, rows, places], ADD)
+            queue.dma_start(out=out_rows[:, rows, places], in_=result[b][:, tiles, cols])
 
         for i in (0, 4, 1, 5, 2):
             interleave_low(units[i])
@@ -289,4 +290,5 @@ def tile_list_dl_prod_res_kernel(tc, xT, wgt, w4_words, w4_scales, wd, res, offs
         times_third(blocks[3])
         finish(nc.vector, nc.scalar, blocks[2], slice(1, 2))
         finish(nc.vector, nc.sync, blocks[3], slice(0, 1))
-        finish(nc.vector, nc.scalar, blocks[3], slice(1, 2))
+        finish(nc.vector, nc.scalar, blocks[3], slice(1, 2), pieces[0])
+        finish(nc.vector, nc.sync, blocks[3], slice(1, 2), pieces[1])

@@ -28,7 +28,7 @@ ENTRIES = PICKS * J
 UNITS = ENTRIES // HALF
 CHUNKS = ENTRIES // P
 SHARE = 8
-SPREAD = SHARE * P
+NARROW = J // SHARE
 
 
 def tile_list_dl_prod_res_kernel(tc, xT, wgt, w4_words, w4_scales, wd, res, offs, out):
@@ -56,15 +56,18 @@ def tile_list_dl_prod_res_kernel(tc, xT, wgt, w4_words, w4_scales, wd, res, offs
         x_rows = xT.rearrange("(p t) w -> t p w", t=PACK)
         wd_rows = wd.rearrange("(p t) n -> p t n", t=PACK)
         out_rows = out.rearrange("(a p) j -> p a j", p=P)
-        thin_rows = wgt.rearrange("(u a) (c w) -> u (a c) w", a=SHARE, w=P)[:, :: CHUNKS + 1, :]
+        thin_rows = wgt.rearrange("r (c w) -> (r c) w", c=2)[:: GROUP + 1, 0:J].rearrange("x (y w) -> x y w", y=SHARE)
 
         nc.vector.memset(w4_scale[:].bitcast(U32), 0)
-        thin = keep.tile([P, P], F32, name="thin", align_bytes=64)
+        thin = keep.tile([P, NARROW], F32, name="thin", align_bytes=64)
 
         nc.sync.dma_start(out=thin[:], in_=thin_rows)
         nc.sync.dma_start(out=planes[0][:], in_=x_rows[0])
         nc.sync.dma_start(offsets[:], offs)
-        nc.sync.dma_start(out=weights[:, SPREAD:ENTRIES], in_=wgt[:, SPREAD:ENTRIES])
+        nc.sync.dma_start(
+            out=weights[:].rearrange("p (e w) -> p e w", e=2)[:, :, J:],
+            in_=wgt.rearrange("p (e w) -> p e w", e=2)[:, :, J:],
+        )
         for q in range(P // QUADRANT):
             nc.sync.dma_start(
                 out=w4_scale[QUADRANT * q : QUADRANT * q + 4, :].bitcast(I32),
@@ -78,19 +81,18 @@ def tile_list_dl_prod_res_kernel(tc, xT, wgt, w4_words, w4_scales, wd, res, offs
         nc.sync.dma_start(out=wd_raw[1][:], in_=wd_rows[:, :, HALF:N])
         nc.sync.dma_start(out=residual[:], in_=res.rearrange("(a p) j -> p a j", p=P))
 
-        blocked = keep.tile([P, P], F32, name="blocked", align_bytes=64)
-        nc.vector.transpose(blocked[:], thin[:])
-        by_chunk = blocked[:].rearrange("p (s u i) -> p i s u", i=SHARE, u=QUADRANT // SHARE)
+        blocked = keep.tile([P, NARROW], F32, name="blocked", align_bytes=64)
+        for s0 in range(0, NARROW, QUADRANT):
+            nc.vector.transpose(blocked[:, s0 : s0 + QUADRANT], thin[:, s0 : s0 + QUADRANT])
+        by_run = blocked[:].rearrange("p (s u e y) -> p e y s u", u=2, e=2, y=SHARE)
         repeated = [keep.tile([P, J], F32, name="repeated%d" % e, align_bytes=64) for e in range(2)]
         for e, copy in enumerate((nc.vector.tensor_copy, nc.scalar.copy)):
             copy(
-                out=repeated[e][:].rearrange("p (i s u r) -> p i s u r", i=PACK, u=QUADRANT // SHARE, r=SHARE),
-                in_=by_chunk[:, PACK * e : PACK * (e + 1)]
-                .unsqueeze(4)
-                .to_broadcast([P, PACK, P // QUADRANT, QUADRANT // SHARE, SHARE]),
+                out=repeated[e][:].rearrange("p (y s u r) -> p y s u r", y=SHARE, u=2, r=GROUP),
+                in_=by_run[:, e].unsqueeze(4).to_broadcast([P, SHARE, NARROW // QUADRANT, 2, GROUP]),
             )
         for e in range(2):
-            nc.vector.transpose(weights[:, e * J : (e + 1) * J], repeated[e][:])
+            nc.vector.transpose(weights[:, e * ENTRIES // 2 : e * ENTRIES // 2 + J], repeated[e][:])
 
         units = [(0, 0), (0, 1), (0, 2), (1, 2), (1, 0), (1, 1)]
 
@@ -100,14 +102,14 @@ def tile_list_dl_prod_res_kernel(tc, xT, wgt, w4_words, w4_scales, wd, res, offs
         def own(u):
             return entry0(u) // HALF
 
-        side = [keep.tile([P, 3, HALF], F32, name="side%d" % i) for i in range(2)]
-        rings = [slots[:, 17 :: UNITS, :], side[0][:, 0:2, :], side[1][:, 1:3, :]]
+        side = keep.tile([P, 4, HALF], F32, name="side")
+        rings = [slots[:, 17 :: UNITS, :], side[:, 0:2, :], side[:, 2:4, :]]
         high = {u: rings[i % PICKS] for i, u in enumerate(units)}
         x_codes = {u: keep.tile([P, HALF], U32, name="x_codes%d%d" % u, align_bytes=64) for u in units}
         x_scale = {u: keep.tile([P, HALF], U8, name="x_scale%d%d" % u, align_bytes=64) for u in units}
         blocks = [(h, r) for h in range(2) for r in range(2)]
         first = {b: keep.tile([P, 2 * HALF], F32, name="first%d%d" % b) for b in blocks}
-        pair = {b: keep.tile([P, 2 * HALF], F32, name="pair%d%d" % b)[:] for b in blocks[1:]}
+        pair = {b: keep.tile([P, 2 * HALF], F32, name="pair%d%d" % b)[:] for b in blocks}
         triple = {b: keep.tile([P, 2, HALF], F32, name="triple%d%d" % b)[:] for b in blocks[1:]}
         result = {blocks[3]: keep.tile([P, 2, HALF], F32, name="result")[:]}
         sums = {}
@@ -267,27 +269,28 @@ def tile_list_dl_prod_res_kernel(tc, xT, wgt, w4_words, w4_scales, wd, res, offs
         early = keep.tile([P, 3, 2, HALF], F32, name="early", tag="staged", align_bytes=64)
         for i in range(3):
             result[blocks[i]] = early[:, i]
-        pair[blocks[0]] = side[1][:, 0:2, :].rearrange("p a j -> p (a j)")
-        triple[blocks[0]] = side[0][:, 1:3, :]
-        times_second(blocks[0], slice(0, 1))
-        times_third(blocks[0], slice(0, 1))
-        times_second(blocks[0], slice(1, 2))
-        times_second(blocks[1], slice(0, 1))
-        times_third(blocks[0], slice(1, 2))
-        times_second(blocks[1], slice(1, 2))
+        triple[blocks[0]] = side[:, 1:3, :]
+        tile = (slice(0, 1), slice(1, 2))
+        times_second(blocks[0], tile[0])
+        times_second(blocks[0], tile[1])
+        times_third(blocks[0], tile[0])
+        times_second(blocks[1], tile[0])
+        times_second(blocks[1], tile[1])
+        times_third(blocks[0], tile[1])
         project(units[4])
         project(units[5])
-        finish(nc.gpsimd, nc.sync, blocks[0], slice(0, 1))
-        finish(nc.gpsimd, nc.sync, blocks[0], slice(1, 2))
-        times_third(blocks[1], slice(0, 1))
-        times_third(blocks[1], slice(1, 2))
+        finish(nc.gpsimd, nc.sync, blocks[0], tile[0])
+        finish(nc.gpsimd, nc.sync, blocks[0], tile[1])
+        times_third(blocks[1], tile[0])
+        times_third(blocks[1], tile[1])
         finish(nc.gpsimd, nc.sync, blocks[1], slice(0, 2))
         times_second(blocks[2])
         times_second(blocks[3])
-        times_third(blocks[2], slice(0, 1))
-        finish(nc.gpsimd, nc.sync, blocks[2], slice(0, 1))
-        times_third(blocks[2], slice(1, 2))
-        times_third(blocks[3])
+        times_third(blocks[2], tile[0])
+        finish(nc.gpsimd, nc.sync, blocks[2], tile[0])
+        times_third(blocks[2], tile[1])
+        times_third(blocks[3], tile[0])
+        times_third(blocks[3], tile[1])
         finish(nc.vector, nc.scalar, blocks[2], slice(1, 2))
         finish(nc.vector, nc.sync, blocks[3], slice(0, 1))
         finish(nc.vector, nc.scalar, blocks[3], slice(1, 2), pieces[0])

@@ -94,7 +94,7 @@ def tile_list_dl_prod_res_kernel(tc, xT, wgt, w4_words, w4_scales, wd, res, offs
         for e in range(2):
             nc.vector.transpose(weights[:, e * ENTRIES // 2 : e * ENTRIES // 2 + J], repeated[e][:])
 
-        units = [(0, 0), (0, 1), (0, 2), (1, 2), (1, 0), (1, 1)]
+        units = [(0, 0), (0, 1), (0, 2), (1, 0), (1, 2), (1, 1)]
 
         def entry0(u):
             return u[1] * J + u[0] * HALF
@@ -102,9 +102,14 @@ def tile_list_dl_prod_res_kernel(tc, xT, wgt, w4_words, w4_scales, wd, res, offs
         def own(u):
             return entry0(u) // HALF
 
-        side = keep.tile([P, 4, HALF], F32, name="side")
-        rings = [slots[:, 17 :: UNITS, :], side[:, 0:2, :], side[:, 2:4, :]]
-        high = {u: rings[i % PICKS] for i, u in enumerate(units)}
+        high = {
+            (0, 1): slots[:, 14:21:6, :],
+            (1, 0): slots[:, 13:20:6, :],
+            (0, 2): slots[:, 1:4:2, :],
+            (1, 2): slots[:, 2:15:12, :],
+            (1, 1): slots[:, 0:2, :],
+        }
+        third_plane = {(0, 0): 18, (0, 1): 20, (1, 0): 19, (0, 2): 3, (1, 2): 14, (1, 1): 1}
         x_codes = {u: keep.tile([P, HALF], U32, name="x_codes%d%d" % u, align_bytes=64) for u in units}
         x_scale = {u: keep.tile([P, HALF], U8, name="x_scale%d%d" % u, align_bytes=64) for u in units}
         blocks = [(h, r) for h in range(2) for r in range(2)]
@@ -124,8 +129,8 @@ def tile_list_dl_prod_res_kernel(tc, xT, wgt, w4_words, w4_scales, wd, res, offs
         def gather_low(t, m0, m1):
             gather(room[:, t * ENTRIES + m0 : t * ENTRIES + m1], t, m0, m1)
 
-        def gather_unit(t, u, cols=slice(0, HALF)):
-            gather(high[u][:, t % 2, cols], t, entry0(u) + cols.start, entry0(u) + cols.stop)
+        def gather_last(u):
+            gather(slots[:, third_plane[u], :], 3, entry0(u), entry0(u) + HALF)
 
         def interleave(dst, src):
             nc.scalar.copy(
@@ -141,8 +146,8 @@ def tile_list_dl_prod_res_kernel(tc, xT, wgt, w4_words, w4_scales, wd, res, offs
 
         gather_low(0, 0, J)
         gather_low(0, J, ENTRIES)
-        gather_low(1, 0, J)
-        gather_low(1, J, ENTRIES)
+        gather_low(1, 0, ENTRIES // 2)
+        gather_low(1, ENTRIES // 2, ENTRIES)
         round_wd(0)
         quantize_wd(0)
 
@@ -150,10 +155,10 @@ def tile_list_dl_prod_res_kernel(tc, xT, wgt, w4_words, w4_scales, wd, res, offs
         by_entry = rounded_all[:].rearrange("p (m t) -> p m t", t=PACK)
         rounded = {u: rounded_all[:, entry0(u) * PACK : (entry0(u) + HALF) * PACK] for u in units}
 
-        def interleave_low(u):
+        def interleave_low(m0, m1):
             nc.scalar.copy(
-                out=by_entry[:, entry0(u) : entry0(u) + HALF, 0:2],
-                in_=slots[:, own(u) : own(u) + UNITS + 1 : UNITS, :].rearrange("p t j -> p j t"),
+                out=by_entry[:, m0:m1, 0:2],
+                in_=room[:].rearrange("p (t m) -> p m t", t=PACK)[:, m0:m1, 0:2],
             )
 
         def interleave_high(u, cols=slice(0, HALF)):
@@ -161,9 +166,6 @@ def tile_list_dl_prod_res_kernel(tc, xT, wgt, w4_words, w4_scales, wd, res, offs
                 out=by_entry[:, entry0(u) + cols.start : entry0(u) + cols.stop, 2:4],
                 in_=high[u][:, :, cols].rearrange("p t j -> p j t"),
             )
-
-        def interleave_whole(u):
-            interleave(rounded[u], slots[:, own(u) :: UNITS, :])
 
         def pass_wd(u, a, opens, closes):
             w_cols = slice(P * (a % 2), P * (a % 2 + 1))
@@ -215,61 +217,70 @@ def tile_list_dl_prod_res_kernel(tc, xT, wgt, w4_words, w4_scales, wd, res, offs
             cols = slice(tiles.start * HALF, tiles.stop * HALF)
             nc.vector.tensor_tensor(pair[b][:, cols], factor(b, 1)[:, cols], first[b][:, cols], MULT)
 
+        first_triples = (slots[:, 14:15, :], first[blocks[1]][:, 0:HALF].unsqueeze(1))
+
+        def triple_of(b, tiles):
+            return first_triples[tiles.start] if b == blocks[0] else triple[b][:, tiles, :]
+
         def times_third(b, tiles=slice(0, 2)):
             cols = slice(tiles.start * HALF, tiles.stop * HALF)
             nc.vector.tensor_tensor(
-                triple[b][:, tiles, :].rearrange("p a j -> p (a j)"), factor(b, 2)[:, cols], pair[b][:, cols], MULT
+                triple_of(b, tiles).rearrange("p a j -> p (a j)"), factor(b, 2)[:, cols], pair[b][:, cols], MULT
             )
 
         def finish(engine, queue, b, tiles, cols=slice(0, HALF)):
             h, r = b
             rows = slice(2 * r + tiles.start, 2 * r + tiles.stop)
             places = slice(h * HALF + cols.start, h * HALF + cols.stop)
-            engine.tensor_tensor(result[b][:, tiles, cols], triple[b][:, tiles, cols], residual[:, rows, places], ADD)
+            engine.tensor_tensor(result[b][:, tiles, cols], triple_of(b, tiles)[:, :, cols], residual[:, rows, places], ADD)
             queue.dma_start(out=out_rows[:, rows, places], in_=result[b][:, tiles, cols])
 
-        for i in (0, 4, 1, 5, 2):
-            interleave_low(units[i])
-        for t in (2, 3):
-            for u in units[:PICKS]:
-                gather_unit(t, u)
-        for u in units[:2]:
-            interleave_high(u)
+        interleave_low(HALF, ENTRIES // 2)
+        interleave_low(ENTRIES // 2, ENTRIES)
+        gather_low(2, 0, ENTRIES // 2)
+        for i in (0, 1, 3):
+            gather_last(units[i])
+        interleave(rounded[units[0]], slots[:, 0::UNITS, :])
+        interleave_high(units[1])
 
         pieces = (slice(0, HALF // 2), slice(HALF // 2, HALF))
-        for u, later in zip(units[:2], units[3:5]):
-            quantize(u)
-            open_bank(u, 0)
-            close_bank(u, 0)
-            open_bank(u, 1)
-            gather_unit(2, later)
-            gather_unit(3, later)
+        quantize(units[0])
+        open_bank(units[0], 0)
+        close_bank(units[0], 0)
+        open_bank(units[0], 1)
+        gather(room[:, 0 : ENTRIES // 2], 2, ENTRIES // 2, ENTRIES)
+        gather_last(units[2])
+        quantize(units[1])
+        open_bank(units[1], 0)
+        close_bank(units[1], 0)
+        open_bank(units[1], 1)
         round_wd(1)
+        interleave_high(units[3])
         interleave_high(units[2])
-        interleave_whole(units[3])
         quantize_wd(1)
+        quantize(units[3])
+        gather_last(units[4])
+        quantize(units[2])
+        open_bank(units[2], 0)
+        close_bank(units[2], 0)
         close_bank(units[0], 1)
         close_bank(units[1], 1)
-        quantize(units[2])
-        project(units[2])
-        gather_unit(2, units[5])
-        for cols in pieces:
-            gather_unit(3, units[5], cols)
+        open_bank(units[2], 1)
+        close_bank(units[2], 1)
+        project(units[3])
+        gather_last(units[5])
         copy_first(blocks[0])
         interleave_high(units[4])
-        for cols in pieces:
-            interleave_high(units[5], cols)
-        quantize(units[3])
-        project(units[3])
+        interleave_high(units[5])
         quantize(units[4])
         quantize(units[5])
         for b in blocks[1:]:
             copy_first(b)
 
-        early = keep.tile([P, 3, 2, HALF], F32, name="early", tag="staged", align_bytes=64)
-        for i in range(3):
+        early = keep.tile([P, 2, 2, HALF], F32, name="early", tag="staged", align_bytes=64)
+        for i in range(2):
             result[blocks[i]] = early[:, i]
-        triple[blocks[0]] = side[:, 1:3, :]
+        result[blocks[2]] = pair[blocks[3]].rearrange("p (a j) -> p a j", a=2)
         tile = (slice(0, 1), slice(1, 2))
         times_second(blocks[0], tile[0])
         times_second(blocks[0], tile[1])
@@ -287,10 +298,10 @@ def tile_list_dl_prod_res_kernel(tc, xT, wgt, w4_words, w4_scales, wd, res, offs
         times_second(blocks[2])
         times_second(blocks[3])
         times_third(blocks[2], tile[0])
-        finish(nc.gpsimd, nc.sync, blocks[2], tile[0])
         times_third(blocks[2], tile[1])
         times_third(blocks[3], tile[0])
         times_third(blocks[3], tile[1])
+        finish(nc.vector, nc.sync, blocks[2], tile[0])
         finish(nc.vector, nc.scalar, blocks[2], slice(1, 2))
         finish(nc.vector, nc.sync, blocks[3], slice(0, 1))
         finish(nc.vector, nc.scalar, blocks[3], slice(1, 2), pieces[0])

from contextlib import ExitStack

import concourse.mybir as mybir

K, N, T, J, PICKS = 512, 512, 2048, 512, 3
FLOPS = 2 * 2 * K * N * J * PICKS

F32 = mybir.dt.float32
BF16 = mybir.dt.bfloat16
I32 = mybir.dt.int32
U32 = mybir.dt.uint32
U16 = mybir.dt.uint16
U8 = mybir.dt.uint8
FP8X4 = mybir.dt.float8_e4m3fn_x4
FP4X4 = mybir.dt.float4_e2m1fn_x4
MULT = mybir.AluOpType.mult
ADD = mybir.AluOpType.add

P = 128
PACK = 4
GROUP = 16
HALF = 256
N_TILES = N // P
RUN = 4
BANKS = 8
QUADRANT = 32
ENTRIES = PICKS * J
UNITS = ENTRIES // HALF
CHUNKS = ENTRIES // P
SHARE = 8
NARROW = J // SHARE


def tile_list_dl_prod_res_kernel(tc, xT, wgt, w4_words, w4_scales, wd, res, offs, out):
    nc = tc.nc
    with ExitStack() as ctx:
        keep = ctx.enter_context(tc.tile_pool(name="keep", bufs=1))
        psum = ctx.enter_context(tc.psum_pool(name="psum", bufs=BANKS))

        offsets = keep.tile([P, ENTRIES // GROUP], U16, name="offsets")
        planes = [keep.tile([P, T], F32, name="plane%d" % t) for t in range(PACK)]
        weights = keep.tile([P, ENTRIES], F32, name="weights", tag="weights", align_bytes=64)
        w4_codes = keep.tile([P, 2 * N], U8, name="w4_codes", align_bytes=64)
        w4_scale = keep.tile([P, N], U8, name="w4_scale", align_bytes=64)
        room = keep.tile([P, PACK * ENTRIES], F32, name="room")
        slots = room[:].rearrange("p (s j) -> p s j", j=HALF)
        wd_raw = [
            keep.tile([P, PACK, HALF], F32, name="wd_raw0", tag="staged", align_bytes=64),
            keep.tile([P, PACK, HALF], F32, name="wd_raw1", align_bytes=64),
        ]
        wd_rounded = [keep.tile([P, HALF * PACK], BF16, name="wd_rounded%d" % h, align_bytes=64) for h in range(2)]
        wd_codes = [keep.tile([P, HALF], U32, name="wd_codes%d" % h, align_bytes=64) for h in range(2)]
        wd_scale = [keep.tile([P, HALF], U8, name="wd_scale%d" % h, align_bytes=64) for h in range(2)]
        residual = keep.tile([P, N_TILES, J], F32, name="residual")

        x_rows = xT.rearrange("(p t) w -> t p w", t=PACK)
        wd_rows = wd.rearrange("(p t) n -> p t n", t=PACK)
        out_rows = out.rearrange("(a p) j -> p a j", p=P)
        thin_rows = wgt.rearrange("r (c w) -> (r c) w", c=2)[:: GROUP + 1, 0:J].rearrange("x (y w) -> x y w", y=SHARE)

        nc.vector.memset(w4_scale[:].bitcast(U32), 0)
        thin = keep.tile([P, NARROW], F32, name="thin", align_bytes=64)

        nc.sync.dma_start(out=thin[:], in_=thin_rows)
        nc.sync.dma_start(out=planes[0][:], in_=x_rows[0])
        nc.sync.dma_start(offsets[:], offs)
        nc.sync.dma_start(
            out=weights[:].rearrange("p (e w) -> p e w", e=2)[:, :, J:],
            in_=wgt.rearrange("p (e w) -> p e w", e=2)[:, :, J:],
        )
        for q in range(P // QUADRANT):
            nc.sync.dma_start(
                out=w4_scale[QUADRANT * q : QUADRANT * q + 4, :].bitcast(I32),
                in_=w4_scales[0, 4 * q : 4 * q + 4, :].bitcast(I32),
            )
        nc.sync.dma_start(out=planes[1][:], in_=x_rows[1])
        nc.sync.dma_start(out=wd_raw[0][:], in_=wd_rows[:, :, 0:HALF])
        nc.sync.dma_start(out=planes[2][:], in_=x_rows[2])
        nc.sync.dma_start(out=planes[3][:], in_=x_rows[3])
        nc.sync.dma_start(out=w4_codes[:].bitcast(I32), in_=w4_words[0].bitcast(I32))
        nc.sync.dma_start(out=wd_raw[1][:], in_=wd_rows[:, :, HALF:N])
        nc.sync.dma_start(out=residual[:], in_=res.rearrange("(a p) j -> p a j", p=P))

        blocked = keep.tile([P, NARROW], F32, name="blocked", align_bytes=64)
        for s0 in range(0, NARROW, QUADRANT):
            nc.vector.transpose(blocked[:, s0 : s0 + QUADRANT], thin[:, s0 : s0 + QUADRANT])
        by_run = blocked[:].rearrange("p (s u e y) -> p e y s u", u=2, e=2, y=SHARE)
        repeated = [keep.tile([P, J], F32, name="repeated%d" % e, align_bytes=64) for e in range(2)]
        for e, copy in enumerate((nc.vector.tensor_copy, nc.scalar.copy)):
            copy(
                out=repeated[e][:].rearrange("p (y s u r) -> p y s u r", y=SHARE, u=2, r=GROUP),
                in_=by_run[:, e].unsqueeze(4).to_broadcast([P, SHARE, NARROW // QUADRANT, 2, GROUP]),
            )
        for e in range(2):
            nc.vector.transpose(weights[:, e * ENTRIES // 2 : e * ENTRIES // 2 + J], repeated[e][:])

        units = [(0, 0), (0, 1), (0, 2), (1, 0), (1, 2), (1, 1)]

        def entry0(u):
            return u[1] * J + u[0] * HALF

        def own(u):
            return entry0(u) // HALF

        high = {
            (0, 1): slots[:, 14:21:6, :],
            (1, 0): slots[:, 13:20:6, :],
            (0, 2): slots[:, 1:4:2, :],
            (1, 2): slots[:, 2:15:12, :],
            (1, 1): slots[:, 0:2, :],
        }
        third_plane = {(0, 0): 18, (0, 1): 20, (1, 0): 19, (0, 2): 3, (1, 2): 14, (1, 1): 1}
        x_codes = {u: keep.tile([P, HALF], U32, name="x_codes%d%d" % u, align_bytes=64) for u in units}
        x_scale = {u: keep.tile([P, HALF], U8, name="x_scale%d%d" % u, align_bytes=64) for u in units}
        blocks = [(h, r) for h in range(2) for r in range(2)]
        first = {b: keep.tile([P, 2 * HALF], F32, name="first%d%d" % b) for b in blocks}
        pair = {b: keep.tile([P, 2 * HALF], F32, name="pair%d%d" % b)[:] for b in blocks}
        triple = {b: keep.tile([P, 2, HALF], F32, name="triple%d%d" % b)[:] for b in blocks[1:]}
        result = {blocks[3]: keep.tile([P, 2, HALF], F32, name="result")[:]}
        sums = {}

        def half(h):
            return slice(h * HALF, (h + 1) * HALF)

        def gather(dst, t, m0, m1):
            window = planes[t][:].indirect(offsets[:, m0 // GROUP : m1 // GROUP])
            nc.vector.tensor_tensor(dst, window, weights[:, m0:m1], MULT)

        def gather_low(t, m0, m1):
            gather(room[:, t * ENTRIES + m0 : t * ENTRIES + m1], t, m0, m1)

        def gather_last(u):
            gather(slots[:, third_plane[u], :], 3, entry0(u), entry0(u) + HALF)

        def interleave(dst, src):
            nc.scalar.copy(
                out=dst.rearrange("p (g i t) -> p g t i", i=RUN, t=PACK),
                in_=src.rearrange("p t (g i) -> p g t i", i=RUN),
            )

        def round_wd(h):
            interleave(wd_rounded[h][:], wd_raw[h][:])

        def quantize_wd(h):
            nc.vector.quantize_mx(out=wd_codes[h][:].bitcast(FP8X4), scales=wd_scale[h][:], in_=wd_rounded[h][:])

        gather_low(0, 0, J)
        gather_low(0, J, ENTRIES)
        gather_low(1, 0, ENTRIES // 2)
        gather_low(1, ENTRIES // 2, ENTRIES)
        round_wd(0)
        quantize_wd(0)

        rounded_all = keep.tile([P, ENTRIES * PACK], BF16, name="rounded", tag="staged", align_bytes=64)
        by_entry = rounded_all[:].rearrange("p (m t) -> p m t", t=PACK)
        rounded = {u: rounded_all[:, entry0(u) * PACK : (entry0(u) + HALF) * PACK] for u in units}

        def interleave_low(m0, m1):
            nc.scalar.copy(
                out=by_entry[:, m0:m1, 0:2],
                in_=room[:].rearrange("p (t m) -> p m t", t=PACK)[:, m0:m1, 0:2],
            )

        def interleave_high(u, cols=slice(0, HALF)):
            nc.scalar.copy(
                out=by_entry[:, entry0(u) + cols.start : entry0(u) + cols.stop, 2:4],
                in_=high[u][:, :, cols].rearrange("p t j -> p j t"),
            )

        def pass_wd(u, a, opens, closes):
            w_cols = slice(P * (a % 2), P * (a % 2 + 1))
            nc.tensor.matmul_mx(
                out=sums[u, a // 2][:, half(a % 2)],
                lhsT=wd_codes[a // 2][:, w_cols].bitcast(FP8X4),
                lhsT_scale=wd_scale[a // 2][:, w_cols],
                rhs=x_codes[u][:].bitcast(FP8X4),
                rhs_scale=x_scale[u][:],
                start=opens,
                stop=closes,
            )

        def pass_w4(u, a, opens, closes):
            nc.tensor.matmul_mx(
                out=sums[u, a // 2][:, half(a % 2)],
                lhsT=w4_codes[:, 2 * P * a : 2 * P * (a + 1)].bitcast(FP4X4),
                lhsT_scale=w4_scale[:, P * a : P * (a + 1)],
                rhs=x_codes[u][:].bitcast(FP8X4),
                rhs_scale=x_scale[u][:],
                start=opens,
                stop=closes,
            )

        def open_bank(u, r):
            sums[u, r] = psum.tile([P, 2 * HALF], F32, name="acc")
            pass_w4(u, 2 * r, True, False)
            pass_w4(u, 2 * r + 1, False, False)

        def close_bank(u, r):
            pass_wd(u, 2 * r, False, False)
            pass_wd(u, 2 * r + 1, False, True)

        def project(u):
            for r in range(2):
                open_bank(u, r)
                close_bank(u, r)

        def quantize(u):
            nc.vector.quantize_mx(out=x_codes[u][:].bitcast(FP8X4), scales=x_scale[u][:], in_=rounded[u])

        def factor(b, i):
            return sums[units[PICKS * b[0] + i], b[1]]

        def copy_first(b):
            nc.scalar.copy(out=first[b][:], in_=factor(b, 0)[:])

        def times_second(b, tiles=slice(0, 2)):
            cols = slice(tiles.start * HALF, tiles.stop * HALF)
            nc.vector.tensor_tensor(pair[b][:, cols], factor(b, 1)[:, cols], first[b][:, cols], MULT)

        first_triples = (slots[:, 14:15, :], first[blocks[1]][:, 0:HALF].unsqueeze(1))

        def triple_of(b, tiles):
            return first_triples[tiles.start] if b == blocks[0] else triple[b][:, tiles, :]

        def times_third(b, tiles=slice(0, 2)):
            cols = slice(tiles.start * HALF, tiles.stop * HALF)
            nc.vector.tensor_tensor(
                triple_of(b, tiles).rearrange("p a j -> p (a j)"), factor(b, 2)[:, cols], pair[b][:, cols], MULT
            )

        def finish(engine, queue, b, tiles, cols=slice(0, HALF)):
            h, r = b
            rows = slice(2 * r + tiles.start, 2 * r + tiles.stop)
            places = slice(h * HALF + cols.start, h * HALF + cols.stop)
            engine.tensor_tensor(result[b][:, tiles, cols], triple_of(b, tiles)[:, :, cols], residual[:, rows, places], ADD)
            queue.dma_start(out=out_rows[:, rows, places], in_=result[b][:, tiles, cols])

        interleave_low(HALF, ENTRIES // 2)
        interleave_low(ENTRIES // 2, ENTRIES)
        gather_low(2, 0, ENTRIES // 2)
        for i in (0, 1, 3):
            gather_last(units[i])
        interleave(rounded[units[0]], slots[:, 0::UNITS, :])
        interleave_high(units[1])

        pieces = (slice(0, HALF // 2), slice(HALF // 2, HALF))
        quantize(units[0])
        open_bank(units[0], 0)
        close_bank(units[0], 0)
        open_bank(units[0], 1)
        gather(room[:, 0 : ENTRIES // 2], 2, ENTRIES // 2, ENTRIES)
        gather_last(units[2])
        quantize(units[1])
        open_bank(units[1], 0)
        close_bank(units[1], 0)
        open_bank(units[1], 1)
        round_wd(1)
        interleave_high(units[3])
        interleave_high(units[2])
        quantize_wd(1)
        quantize(units[3])
        gather_last(units[4])
        quantize(units[2])
        open_bank(units[2], 0)
        close_bank(units[2], 0)
        close_bank(units[0], 1)
        close_bank(units[1], 1)
        open_bank(units[2], 1)
        close_bank(units[2], 1)
        project(units[3])
        gather_last(units[5])
        copy_first(blocks[0])
        interleave_high(units[4])
        interleave_high(units[5])
        quantize(units[4])
        quantize(units[5])
        for b in blocks[1:]:
            copy_first(b)

        early = keep.tile([P, 2, 2, HALF], F32, name="early", tag="staged", align_bytes=64)
        for i in range(2):
            result[blocks[i]] = early[:, i]
        result[blocks[2]] = pair[blocks[3]].rearrange("p (a j) -> p a j", a=2)
        tile = (slice(0, 1), slice(1, 2))
        times_second(blocks[0], tile[0])
        times_second(blocks[0], tile[1])
        times_third(blocks[0], tile[0])
        times_second(blocks[1], tile[0])
        times_second(blocks[1], tile[1])
        times_third(blocks[0], tile[1])
        project(units[4])
        project(units[5])
        finish(nc.gpsimd, nc.sync, blocks[0], tile[0])
        finish(nc.gpsimd, nc.sync, blocks[0], tile[1])
        times_third(blocks[1], tile[0])
        times_third(blocks[1], tile[1])
        finish(nc.gpsimd, nc.sync, blocks[1], slice(0, 2))
        times_second(blocks[2])
        times_second(blocks[3])
        times_third(blocks[2], tile[0])
        times_third(blocks[2], tile[1])
        times_third(blocks[3], tile[0])
        times_third(blocks[3], tile[1])
        finish(nc.vector, nc.sync, blocks[2], tile[0])
        finish(nc.vector, nc.scalar, blocks[2], slice(1, 2))
        finish(nc.vector, nc.sync, blocks[3], slice(0, 1))
        finish(nc.vector, nc.scalar, blocks[3], slice(1, 2), pieces[0])
        finish(nc.vector, nc.sync, blocks[3], slice(1, 2), pieces[1])
